import numpy as np
import ml_dtypes


def mxq(x, axis, fmt="e4m3"):
    dtype, down = {"e4m3": (ml_dtypes.float8_e4m3fn, 7), "e5m2": (ml_dtypes.float8_e5m2, 14)}[fmt]
    v = np.moveaxis(np.asarray(x, np.float32).astype(ml_dtypes.bfloat16).astype(np.float64), axis, -1)
    blocks = v.reshape(v.shape[:-1] + (-1, 32))
    amax = np.abs(blocks).max(-1, keepdims=True)
    byte = np.maximum(np.where(amax > 0, np.frexp(amax)[1] - 1 + 127, 0) - down, 1)
    scale = np.exp2(byte - 127.0)
    codes = (blocks / scale).astype(np.float32).astype(dtype).astype(np.float64)
    return np.moveaxis((codes * scale).reshape(v.shape), -1, axis)


WIDE = False


def mx_kscale(k):
    if not WIDE:
        return np.ones(k)
    levels = np.array([24, -24, 12, -12, 0])
    if k % 512:
        return np.exp2(np.random.permutation(np.resize(levels, k // 32))).repeat(32)
    a = np.empty((k // 512, 16))
    for p in range(k // 512):
        a[p, :8] = np.random.permutation(np.resize(levels, 8))
        for g in range(8):
            far = levels[np.abs(levels - a[p, g]) >= 10]
            a[p, g + 8] = far[np.random.randint(len(far))]
    return np.exp2(a.ravel()).repeat(32)


def f64(x):
    return np.asarray(x).astype(np.float64)


def striped8(idx):
    return np.concatenate([v.reshape(-1, 16).T for v in idx]).astype(np.uint16)


def unstriped8(offs):
    return np.stack([offs[16 * g:16 * g + 16].T.reshape(-1) for g in range(8)]).astype(np.int64)


E2M1 = np.array([0.0, 0.5, 1.0, 1.5, 2.0, 3.0, 4.0, 6.0, -0.0, -0.5, -1.0, -1.5, -2.0, -3.0, -4.0, -6.0])


def pack_weight(w, fmt):
    k, n = w.shape
    w = f64(np.asarray(w, np.float32).astype(ml_dtypes.bfloat16)).reshape(k // 32, 32, n)
    amax = np.abs(w).max(1)
    if fmt == "e4m3":
        byte = np.frexp(amax)[1] - 1 + 127 - 7
    else:
        mant, ex = np.frexp(amax / 6.0)
        byte = np.where(mant > 0.5, ex, ex - 1) + 127
    byte = np.clip(np.where(amax > 0, byte, 1), 1, 254)
    scaled = (w * np.exp2(127.0 - byte)[:, None, :]).reshape(k, n).astype(np.float32)
    by_word = np.ascontiguousarray(scaled.reshape(k // 512, 128, 4, n).transpose(0, 1, 3, 2))
    if fmt == "e4m3":
        words = by_word.astype(ml_dtypes.float8_e4m3fn).view(np.uint8)
    else:
        c = by_word.astype(ml_dtypes.float4_e2m1fn).view(np.uint8) & 0xF
        words = (c[..., 0::2] | (c[..., 1::2] << 4)).reshape(k // 512, 128, 2 * n)
    return np.ascontiguousarray(words), np.ascontiguousarray(byte.astype(np.uint8).reshape(k // 512, 16, n))


def unpack_weight(words, scales, fmt):
    g, _, n = scales.shape
    words = np.ascontiguousarray(words).reshape(g, 128, n, -1)
    if fmt == "e4m3":
        vals = words.view(ml_dtypes.float8_e4m3fn).astype(np.float64)
    else:
        nib = np.empty((g, 128, n, 4), np.uint8)
        nib[..., 0::2] = words & 0xF
        nib[..., 1::2] = words >> 4
        vals = E2M1[nib]
    vals = vals * np.repeat(np.exp2(scales.astype(np.float64) - 127.0), 8, axis=1)[..., None]
    return vals.transpose(0, 1, 3, 2).reshape(g * 512, n)


def sigm(f):
    return 1.0 / (1.0 + np.exp(-np.maximum(f, -700.0)))


K, R, N, T, J = 1024, 1024, 512, 2048, 1024


def setup_inputs():
    n = np.random.standard_normal
    s = mx_kscale(K)[:, None]
    u = mx_kscale(R)[:, None]
    p_wu = pack_weight(n((K, R)) / np.sqrt(K) / s * u.T, "e4m3")
    p_wd = pack_weight(n((R, N)) / np.sqrt(R) / u, "e4m3")
    return {
        "xT": (n((K, T)) * s).astype(np.float32),
        "wgt": np.repeat(np.random.uniform(0.5, 2.0, (8, J)), 16, axis=0).astype(np.float32),
        "wg": (n((K, R)) / np.sqrt(K) / s).astype(np.float32),
        "wu_words": p_wu[0],
        "wu_scales": p_wu[1],
        "wd_words": p_wd[0],
        "wd_scales": p_wd[1],
        "b": (0.3 * n(N)).astype(np.float32),
        "wgo": np.repeat(np.random.uniform(0.5, 2.0, (8, J)), 16, axis=0).astype(np.float32),
        "offs": striped8(np.stack([np.random.permutation(T)[:J] for _ in range(8)])),
        "offs2": striped8(np.stack([np.random.permutation(T)[:J] for _ in range(8)])),
    }


def reference(xT, wgt, wg, wu_words, wu_scales, wd_words, wd_scales, b, wgo, offs, offs2):
    idx = unstriped8(offs)
    idx2 = unstriped8(offs2)
    rows = np.arange(K)
    xg = f64(wgt)[rows // 4 % 128] * f64(xT)[rows[:, None], idx[rows % 512 // 64]]
    xT_ = mxq(xg, 0, "e4m3")
    wg_ = mxq(f64(wg), 0, "e4m3")
    wu_ = unpack_weight(wu_words, wu_scales, "e4m3")
    ga = wg_.T @ xT_
    ub = wu_.T @ xT_
    h = sigm(ga) * ub
    h_ = mxq(h, 0, "e4m3")
    wd_ = unpack_weight(wd_words, wd_scales, "e4m3")
    y = wd_.T @ h_
    out = np.zeros((N, T))
    rows = np.arange(N)
    out[rows[:, None], idx2[rows % 128 // 16]] = f64(wgo)[rows % 128] * (y + f64(b)[:, None])
    return out

@@ -1,0 +1,309 @@
+from contextlib import ExitStack
+
+import concourse.mybir as mybir
+
+K, R, N, T, J = 1024, 1024, 512, 2048, 1024
+FLOPS = 2 * J * (2 * K * R + R * N)
+
+F32 = mybir.dt.float32
+BF16 = mybir.dt.bfloat16
+I32 = mybir.dt.int32
+U16 = mybir.dt.uint16
+U8 = mybir.dt.uint8
+FP8X4 = mybir.dt.float8_e4m3fn_x4
+MULT = mybir.AluOpType.mult
+ACT = mybir.ActivationFunctionType
+
+P = 128
+PACK = 4
+PASS = 512
+HALF = 512
+JT = 128
+
+
+def tile_list_sigm_scatb_kernel(
+    tc, xT, wgt, wg, wu_words, wu_scales, wd_words, wd_scales, b, wgo, offs, offs2, out
+):
+    nc = tc.nc
+    with ExitStack() as ctx:
+        keep = ctx.enter_context(tc.tile_pool(name="keep", bufs=1))
+        ring = ctx.enter_context(tc.tile_pool(name="ring", bufs=2))
+        psum = ctx.enter_context(tc.psum_pool(name="psum", bufs=1))
+
+        offs_t = keep.tile([P, J // 16], U16, name="offs_t")
+        offs2_t = keep.tile([P, J // 16], U16, name="offs2_t")
+        wgt_t = keep.tile([P, J], F32, name="wgt_t")
+        wgo_t = keep.tile([P, J], F32, name="wgo_t")
+        bias = keep.tile([P, N // P], F32, name="bias")
+        warm = keep.tile([P, 2], F32, name="warm")
+        planes = {(a, i): keep.tile([P, T], F32, name="x%d%d" % (a, i)) for a in range(2) for i in range(PACK)}
+        pages = [keep.tile([P, T], F32, name="page%d" % n) for n in range(4)]
+        wu_sraw = keep.tile([P, R], U8, name="wu_sraw", align_bytes=64)
+        wu_s = keep.tile([P, R], U8, name="wu_s", align_bytes=64)
+        wd_s = keep.tile([P, N], U8, name="wd_s", align_bytes=64)
+        wd_q = keep.tile([P, 2, N], I32, name="wd_q", align_bytes=64)
+        wu_q = [keep.tile([P, 2, PASS], I32, name="wu_q%d" % c, align_bytes=64) for c in range(2)]
+        wg_q = {(c, a): keep.tile([P, PASS], I32, name="wg_q%d%d" % (c, a), align_bytes=64) for c in range(2) for a in range(2)}
+        wg_s = {(c, a): keep.tile([P, PASS], U8, name="wg_s%d%d" % (c, a), align_bytes=64) for c in range(2) for a in range(2)}
+        x_q = [keep.tile([P, J], I32, name="x_q%d" % a, align_bytes=64) for a in range(2)]
+        x_s = [keep.tile([P, J], U8, name="x_s%d" % a, align_bytes=64) for a in range(2)]
+        h_q = [keep.tile([P, J], I32, name="h_q%d" % c, align_bytes=64) for c in range(2)]
+        h_s = [keep.tile([P, J], U8, name="h_s%d" % c, align_bytes=64) for c in range(2)]
+
+        x_rows = xT.rearrange("(a p i) t -> a i p t", a=2, i=PACK)
+        wg_rows = wg.rearrange("(a p i) r -> a p i r", a=2, i=PACK)
+        wu_rows = wu_words.rearrange("a p r i -> p a (r i)")
+
+        nc.vector.memset(warm[:, 0:1], 0.0)
+        nc.scalar.activation(warm[:, 1:2], warm[:, 0:1], ACT.Sigmoid)
+        nc.vector.memset(wu_sraw[:].bitcast(I32), 0)
+        nc.vector.memset(wd_s[:].bitcast(I32), 0)
+        for q in range(4):
+            nc.scalar.dma_start(out=wu_sraw[32 * q : 32 * q + 8, :].bitcast(I32), in_=wu_scales[:, 4 * q : 4 * q + 4, :].bitcast(I32))
+        for n in range(2):
+            nc.vector.memset(pages[n][:], 0.0)
+            nc.gpsimd.memset(pages[2 + n][:], 0.0)
+
+        wg_raw = {}
+        wu_raw = {}
+
+        def load_x(a, i):
+            nc.sync.dma_start(out=planes[a, i][:], in_=x_rows[a, i])
+
+        def load_wg(c, a):
+            wg_raw[c, a] = ring.tile([P, PACK, PASS], F32, name="wg_raw", tag="wg_raw")
+            nc.sync.dma_start(out=wg_raw[c, a][:], in_=wg_rows[a][:, :, c * PASS : (c + 1) * PASS])
+
+        def load_wu(c):
+            wu_raw[c] = ring.tile([P, 2, PASS], I32, name="wu_raw", tag="wu_raw")
+            nc.sync.dma_start(out=wu_raw[c][:], in_=wu_rows[:, :, c * PASS * PACK : (c + 1) * PASS * PACK].bitcast(I32))
+
+        nc.sync.dma_start(offs_t[:], offs)
+        nc.sync.dma_start(out=wgt_t[:], in_=wgt)
+        load_x(0, 0)
+        load_wg(0, 0)
+        load_x(0, 1)
+        load_wg(0, 1)
+        load_x(0, 2)
+        load_wu(0)
+        load_x(0, 3)
+        for i in range(PACK):
+            load_x(1, i)
+
+        gath = {}
+        wg_b = {}
+        x_b = {}
+        banks = {}
+        h_b = {}
+
+        def gather(a, i, hf):
+            if i == 0:
+                gath[a, hf] = ring.tile([P, PACK, HALF], F32, name="gath", tag="gath", bufs=3)
+            nc.vector.tensor_tensor(
+                gath[a, hf][:, i, :],
+                planes[a, i][:].indirect(offs_t[:, hf * 32 : (hf + 1) * 32]),
+                wgt_t[:, hf * HALF : (hf + 1) * HALF],
+                MULT,
+            )
+
+        def weave_x(a, hf, j0, j1):
+            if j0 == 0:
+                x_b[a, hf] = ring.tile([P, HALF, PACK], BF16, name="x_b", tag="x_b", align_bytes=64)
+            nc.scalar.copy(
+                x_b[a, hf][:, j0:j1, :].rearrange("p (c j) i -> p c i j", j=4),
+                gath[a, hf][:, :, j0:j1].rearrange("p i (c j) -> p c i j", j=4),
+            )
+
+        def quant_x(a, hf, j0, j1):
+            cols = slice(hf * HALF + j0, hf * HALF + j1)
+            nc.vector.quantize_mx(
+                out=x_q[a][:, cols].bitcast(FP8X4),
+                scales=x_s[a][:, cols],
+                in_=x_b[a, hf][:, j0:j1, :].rearrange("p j i -> p (j i)"),
+            )
+
+        def weave_wg(c, a, eng):
+            wg_b[c, a] = ring.tile([P, PACK, P, PACK], BF16, name="wg_b", tag="wg_b", align_bytes=64)
+            dst = wg_b[c, a][:].rearrange("p t m i -> p m t i")
+            src = wg_raw[c, a][:].rearrange("p i (m t) -> p m t i", t=PACK)
+            if eng == "scalar":
+                nc.scalar.copy(dst, src)
+            else:
+                nc.vector.tensor_copy(dst, src)
+
+        def quant_wg(c, a):
+            nc.vector.quantize_mx(
+                out=wg_q[c, a][:].bitcast(FP8X4),
+                scales=wg_s[c, a][:],
+                in_=wg_b[c, a][:].rearrange("p t m i -> p (t m i)"),
+            )
+
+        def deal_wu(c):
+            nc.vector.tensor_copy(
+                wu_q[c][:].rearrange("p a (t g m) -> p a g t m", t=PACK, m=4),
+                wu_raw[c][:].rearrange("p a (g m t) -> p a g t m", t=PACK, m=4),
+            )
+
+        def deal_wu_scales():
+            nc.vector.tensor_copy(
+                wu_s[:].rearrange("p (c t m) -> p c t m", c=2, t=PACK),
+                wu_sraw[:].rearrange("p (c m t) -> p c t m", c=2, t=PACK),
+            )
+
+        def up_pass(c, jt, a, pair):
+            if a == 0:
+                banks[c, jt] = [psum.tile([P, PACK, JT], F32, name="up", tag="bank%d" % (2 * pair + s)) for s in range(2)]
+            cols = slice(jt * JT, (jt + 1) * JT)
+            for s in range(2):
+                for t in range(PACK):
+                    m = slice(t * P, (t + 1) * P)
+                    if s == 0:
+                        w, ws = wg_q[c, a][:, m], wg_s[c, a][:, m]
+                    else:
+                        w, ws = wu_q[c][:, a, m], wu_s[4 * a : P, c * PASS + t * P : c * PASS + (t + 1) * P]
+                    nc.tensor.matmul_mx(
+                        banks[c, jt][s][:, t, :],
+                        lhsT=w.bitcast(FP8X4),
+                        lhsT_scale=ws,
+                        rhs=x_q[a][:, cols].bitcast(FP8X4),
+                        rhs_scale=x_s[a][:, cols],
+                        start=(a == 0 and t == 0),
+                        stop=(a == 1 and t == PACK - 1),
+                    )
+
+        def gate(c, jt):
+            sig = ring.tile([P, JT, PACK], F32, name="sig", tag="sig", bufs=3)
+            nc.scalar.activation(sig[:], banks[c, jt][0][:].rearrange("p t j -> p j t"), ACT.Sigmoid)
+            h_b[c, jt] = ring.tile([P, JT, PACK], BF16, name="h_b", tag="h_b", bufs=4, align_bytes=64)
+            nc.vector.tensor_tensor(h_b[c, jt][:], banks[c, jt][1][:].rearrange("p t j -> p j t"), sig[:], MULT)
+
+        def quant_h(c, jt):
+            cols = slice(jt * JT, (jt + 1) * JT)
+            nc.vector.quantize_mx(
+                out=h_q[c][:, cols].bitcast(FP8X4),
+                scales=h_s[c][:, cols],
+                in_=h_b[c, jt][:].rearrange("p j t -> p (j t)"),
+            )
+
+        def unit(c, jt, pair):
+            up_pass(c, jt, 0, pair)
+            up_pass(c, jt, 1, pair)
+            gate(c, jt)
+
+        y_bank = {}
+
+        def down(j0, j1, ns, bank):
+            y = psum.tile([P, len(ns), j1 - j0], F32, name="y", tag="bank%d" % bank)
+            for s, n in enumerate(ns):
+                y_bank[j0, n] = y[:, s, :]
+                for c in range(2):
+                    nc.tensor.matmul_mx(
+                        y[:, s, :],
+                        lhsT=wd_q[:, c, n * P : (n + 1) * P].bitcast(FP8X4),
+                        lhsT_scale=wd_s[4 * c : P, n * P : (n + 1) * P],
+                        rhs=h_q[c][:, j0:j1].bitcast(FP8X4),
+                        rhs_scale=h_s[c][:, j0:j1],
+                        start=(c == 0),
+                        stop=(c == 1),
+                    )
+
+        def place(j0, j1, n):
+            y_sb = ring.tile([P, j1 - j0], F32, name="y_sb", tag="y_sb", bufs=4)
+            nc.scalar.activation(y_sb[:], y_bank[j0, n], ACT.Identity, bias=bias[:, n : n + 1])
+            nc.vector.tensor_tensor(
+                pages[n][:].indirect(offs2_t[:, j0 // 16 : j1 // 16]), y_sb[:], wgo_t[:, j0:j1], MULT
+            )
+
+        for hf in range(2):
+            gather(0, 0, hf)
+        weave_wg(0, 0, "scalar")
+        for hf in range(2):
+            gather(0, 1, hf)
+        quant_wg(0, 0)
+        weave_wg(0, 1, "scalar")
+        for hf in range(2):
+            gather(0, 2, hf)
+        quant_wg(0, 1)
+        deal_wu(0)
+        deal_wu_scales()
+        load_wg(1, 0)
+        load_wg(1, 1)
+        load_wu(1)
+        for q in range(4):
+            nc.sync.dma_start(out=wd_s[32 * q : 32 * q + 8, :].bitcast(I32), in_=wd_scales[:, 4 * q : 4 * q + 4, :].bitcast(I32))
+        nc.sync.dma_start(out=wd_q[:], in_=wd_words.rearrange("a p n i -> p a (n i)").bitcast(I32))
+        with nc.allow_non_contiguous_dma(reason="one bias value a partition"):
+            nc.sync.dma_start(out=bias[:], in_=b.rearrange("(c p) -> p c", p=P))
+        nc.sync.dma_start(offs2_t[:], offs2)
+        nc.sync.dma_start(out=wgo_t[:], in_=wgo)
+        for hf in range(2):
+            gather(0, 3, hf)
+        for hf in range(2):
+            weave_x(0, hf, 0, HALF)
+        for hf in range(2):
+            gather(1, 0, hf)
+        quant_x(0, 0, 0, HALF)
+        for hf in range(2):
+            gather(1, 1, hf)
+        quant_x(0, 1, 0, HALF)
+        for jt in range(4):
+            up_pass(0, jt, 0, jt)
+        for hf in range(2):
+            gather(1, 2, hf)
+        for hf in range(2):
+            gather(1, 3, hf)
+        for jt in range(4):
+            weave_x(1, 0, jt * JT, (jt + 1) * JT)
+            quant_x(1, 0, jt * JT, (jt + 1) * JT)
+            up_pass(0, jt, 1, jt)
+        gate(0, 0)
+        weave_wg(1, 0, "scalar")
+        gate(0, 1)
+        quant_h(0, 0)
+        weave_wg(1, 1, "vector")
+        gate(0, 2)
+        quant_h(0, 1)
+        quant_wg(1, 0)
+        gate(0, 3)
+        quant_h(0, 2)
+        quant_wg(1, 1)
+        deal_wu(1)
+        quant_h(0, 3)
+        weave_x(1, 1, 0, HALF)
+        unit(1, 0, 0)
+        quant_x(1, 1, 0, HALF)
+        quant_h(1, 0)
+        unit(1, 1, 1)
+        down(0, 128, range(4), 6)
+        quant_h(1, 1)
+        unit(1, 2, 2)
+        down(128, 256, range(4), 7)
+        for n in range(4):
+            place(0, 128, n)
+        quant_h(1, 2)
+        unit(1, 3, 0)
+        quant_h(1, 3)
+        unit(0, 4, 1)
+        down(256, 512, range(0, 2), 6)
+        place(128, 256, 0)
+        place(128, 256, 1)
+        quant_h(0, 4)
+        unit(1, 4, 2)
+        place(128, 256, 2)
+        place(128, 256, 3)
+        down(256, 512, range(2, 4), 7)
+        quant_h(1, 4)
+        pair = 0
+        for jt in range(5, 8):
+            unit(0, jt, pair % 3)
+            quant_h(0, jt)
+            unit(1, jt, (pair + 1) % 3)
+            place(256, 512, jt - 5)
+            quant_h(1, jt)
+            pair = pair + 2
+        for n in range(4):
+            down(512, 1024, [n], (6 + n) % 8)
+            if n == 0:
+                place(256, 512, 3)
+            place(512, 1024, n)
+            nc.sync.dma_start(out=out[n * P : (n + 1) * P, :], in_=pages[n][:])

@@ -28,7 +28,7 @@ def tile_list_sigm_scatb_kernel(
     with ExitStack() as ctx:
         keep = ctx.enter_context(tc.tile_pool(name="keep", bufs=1))
         ring = ctx.enter_context(tc.tile_pool(name="ring", bufs=2))
-        psum = ctx.enter_context(tc.psum_pool(name="psum", bufs=1))
+        psum = ctx.enter_context(tc.psum_pool(name="psum", bufs=8))
 
         offs_t = keep.tile([P, J // 16], U16, name="offs_t")
         offs2_t = keep.tile([P, J // 16], U16, name="offs2_t")
@@ -36,7 +36,7 @@ def tile_list_sigm_scatb_kernel(
         wgo_t = keep.tile([P, J], F32, name="wgo_t")
         bias = keep.tile([P, N // P], F32, name="bias")
         warm = keep.tile([P, 2], F32, name="warm")
-        planes = {(a, i): keep.tile([P, T], F32, name="x%d%d" % (a, i)) for a in range(2) for i in range(PACK)}
+        planes = {(a, i): keep.tile([P, T], F32, name="x%d%d" % (a, i), tag="x%d%d" % (a, i), align_bytes=64) for a in range(2) for i in range(PACK)}
         pages = [keep.tile([P, T], F32, name="page%d" % n) for n in range(4)]
         wu_sraw = keep.tile([P, R], U8, name="wu_sraw", align_bytes=64)
         wu_s = keep.tile([P, R], U8, name="wu_s", align_bytes=64)
@@ -45,7 +45,7 @@ def tile_list_sigm_scatb_kernel(
         wu_q = [keep.tile([P, 2, PASS], I32, name="wu_q%d" % c, align_bytes=64) for c in range(2)]
         wg_q = {(c, a): keep.tile([P, PASS], I32, name="wg_q%d%d" % (c, a), align_bytes=64) for c in range(2) for a in range(2)}
         wg_s = {(c, a): keep.tile([P, PASS], U8, name="wg_s%d%d" % (c, a), align_bytes=64) for c in range(2) for a in range(2)}
-        x_q = [keep.tile([P, J], I32, name="x_q%d" % a, align_bytes=64) for a in range(2)]
+        x_q = [keep.tile([P, J], I32, name="x_q0", tag="x11", align_bytes=64), keep.tile([P, J], I32, name="x_q1", align_bytes=64)]
         x_s = [keep.tile([P, J], U8, name="x_s%d" % a, align_bytes=64) for a in range(2)]
         h_q = [keep.tile([P, J], I32, name="h_q%d" % c, align_bytes=64) for c in range(2)]
         h_s = [keep.tile([P, J], U8, name="h_s%d" % c, align_bytes=64) for c in range(2)]
@@ -54,15 +54,12 @@ def tile_list_sigm_scatb_kernel(
         wg_rows = wg.rearrange("(a p i) r -> a p i r", a=2, i=PACK)
         wu_rows = wu_words.rearrange("a p r i -> p a (r i)")
 
-        nc.vector.memset(warm[:, 0:1], 0.0)
+        nc.gpsimd.memset(wu_sraw[:].bitcast(I32), 0)
+        nc.gpsimd.memset(warm[:, 0:1], 0.0)
         nc.scalar.activation(warm[:, 1:2], warm[:, 0:1], ACT.Sigmoid)
-        nc.vector.memset(wu_sraw[:].bitcast(I32), 0)
-        nc.vector.memset(wd_s[:].bitcast(I32), 0)
-        for q in range(4):
-            nc.scalar.dma_start(out=wu_sraw[32 * q : 32 * q + 8, :].bitcast(I32), in_=wu_scales[:, 4 * q : 4 * q + 4, :].bitcast(I32))
-        for n in range(2):
-            nc.vector.memset(pages[n][:], 0.0)
-            nc.gpsimd.memset(pages[2 + n][:], 0.0)
+        nc.gpsimd.memset(wd_s[:].bitcast(I32), 0)
+        for n in range(4):
+            nc.gpsimd.memset(pages[n][:], 0.0)
 
         wg_raw = {}
         wu_raw = {}
@@ -71,7 +68,10 @@ def tile_list_sigm_scatb_kernel(
             nc.sync.dma_start(out=planes[a, i][:], in_=x_rows[a, i])
 
         def load_wg(c, a):
-            wg_raw[c, a] = ring.tile([P, PACK, PASS], F32, name="wg_raw", tag="wg_raw")
+            if c == 0:
+                wg_raw[c, a] = keep.tile([P, PACK, PASS], F32, name="wg_raw0%d" % a)
+            else:
+                wg_raw[c, a] = keep.tile([P, PACK, PASS], F32, name="wg_raw1%d" % a, tag="x0%d" % a, align_bytes=64)
             nc.sync.dma_start(out=wg_raw[c, a][:], in_=wg_rows[a][:, :, c * PASS : (c + 1) * PASS])
 
         def load_wu(c):
@@ -79,57 +79,52 @@ def tile_list_sigm_scatb_kernel(
             nc.sync.dma_start(out=wu_raw[c][:], in_=wu_rows[:, :, c * PASS * PACK : (c + 1) * PASS * PACK].bitcast(I32))
 
         nc.sync.dma_start(offs_t[:], offs)
-        nc.sync.dma_start(out=wgt_t[:], in_=wgt)
+        nc.sync.dma_start(out=wgt_t[:, :HALF], in_=wgt[:, :HALF])
         load_x(0, 0)
-        load_wg(0, 0)
+        nc.sync.dma_start(out=wgt_t[:, HALF:], in_=wgt[:, HALF:])
         load_x(0, 1)
-        load_wg(0, 1)
-        load_x(0, 2)
         load_wu(0)
+        load_x(0, 2)
+        load_wg(0, 1)
         load_x(0, 3)
-        for i in range(PACK):
-            load_x(1, i)
+        for q in range(4):
+            nc.sync.dma_start(out=wu_sraw[32 * q : 32 * q + 8, :].bitcast(I32), in_=wu_scales[:, 4 * q : 4 * q + 4, :].bitcast(I32))
+        load_x(1, 0)
+        load_wg(0, 0)
+        load_x(1, 1)
 
-        gath = {}
+        gath = [keep.tile([P, PACK, J], F32, name="gath%d" % a) for a in range(2)]
+        x_b = [keep.tile([P, J, PACK], BF16, name="x_b%d" % a, align_bytes=64) for a in range(2)]
         wg_b = {}
-        x_b = {}
         banks = {}
         h_b = {}
+        y_sb = {}
 
-        def gather(a, i, hf):
-            if i == 0:
-                gath[a, hf] = ring.tile([P, PACK, HALF], F32, name="gath", tag="gath", bufs=3)
+        def gather(a, i, j0, j1):
             nc.vector.tensor_tensor(
-                gath[a, hf][:, i, :],
-                planes[a, i][:].indirect(offs_t[:, hf * 32 : (hf + 1) * 32]),
-                wgt_t[:, hf * HALF : (hf + 1) * HALF],
-                MULT,
+                gath[a][:, i, j0:j1], planes[a, i][:].indirect(offs_t[:, j0 // 16 : j1 // 16]), wgt_t[:, j0:j1], MULT
             )
 
-        def weave_x(a, hf, j0, j1):
-            if j0 == 0:
-                x_b[a, hf] = ring.tile([P, HALF, PACK], BF16, name="x_b", tag="x_b", align_bytes=64)
+        def weave_x(a, j0, j1):
             nc.scalar.copy(
-                x_b[a, hf][:, j0:j1, :].rearrange("p (c j) i -> p c i j", j=4),
-                gath[a, hf][:, :, j0:j1].rearrange("p i (c j) -> p c i j", j=4),
+                x_b[a][:, j0:j1, :].rearrange("p (c j) i -> p c i j", j=4),
+                gath[a][:, :, j0:j1].rearrange("p i (c j) -> p c i j", j=4),
             )
 
-        def quant_x(a, hf, j0, j1):
-            cols = slice(hf * HALF + j0, hf * HALF + j1)
+        def quant_x(a, j0, j1):
             nc.vector.quantize_mx(
-                out=x_q[a][:, cols].bitcast(FP8X4),
-                scales=x_s[a][:, cols],
-                in_=x_b[a, hf][:, j0:j1, :].rearrange("p j i -> p (j i)"),
+                out=x_q[a][:, j0:j1].bitcast(FP8X4),
+                scales=x_s[a][:, j0:j1],
+                in_=x_b[a][:, j0:j1, :].rearrange("p j i -> p (j i)"),
             )
 
-        def weave_wg(c, a, eng):
-            wg_b[c, a] = ring.tile([P, PACK, P, PACK], BF16, name="wg_b", tag="wg_b", align_bytes=64)
-            dst = wg_b[c, a][:].rearrange("p t m i -> p m t i")
-            src = wg_raw[c, a][:].rearrange("p i (m t) -> p m t i", t=PACK)
-            if eng == "scalar":
-                nc.scalar.copy(dst, src)
-            else:
-                nc.vector.tensor_copy(dst, src)
+        def weave_wg(c, a, copy, m0, m1):
+            if m0 == 0:
+                wg_b[c, a] = ring.tile([P, PACK, P, PACK], BF16, name="wg_b", tag="wg_b", align_bytes=64)
+            copy(
+                wg_b[c, a][:, :, m0:m1, :].rearrange("p t m i -> p m t i"),
+                wg_raw[c, a][:, :, m0 * PACK : m1 * PACK].rearrange("p i (m t) -> p m t i", t=PACK),
+            )
 
         def quant_wg(c, a):
             nc.vector.quantize_mx(
@@ -150,9 +145,9 @@ def tile_list_sigm_scatb_kernel(
                 wu_sraw[:].rearrange("p (c m t) -> p c t m", c=2, t=PACK),
             )
 
-        def up_pass(c, jt, a, pair):
+        def up_pass(c, jt, a):
             if a == 0:
-                banks[c, jt] = [psum.tile([P, PACK, JT], F32, name="up", tag="bank%d" % (2 * pair + s)) for s in range(2)]
+                banks[c, jt] = [psum.tile([P, PACK, JT], F32, name="up", tag="bank") for s in range(2)]
             cols = slice(jt * JT, (jt + 1) * JT)
             for s in range(2):
                 for t in range(PACK):
@@ -172,62 +167,65 @@ def tile_list_sigm_scatb_kernel(
                     )
 
         def gate(c, jt):
-            sig = ring.tile([P, JT, PACK], F32, name="sig", tag="sig", bufs=3)
-            nc.scalar.activation(sig[:], banks[c, jt][0][:].rearrange("p t j -> p j t"), ACT.Sigmoid)
-            h_b[c, jt] = ring.tile([P, JT, PACK], BF16, name="h_b", tag="h_b", bufs=4, align_bytes=64)
-            nc.vector.tensor_tensor(h_b[c, jt][:], banks[c, jt][1][:].rearrange("p t j -> p j t"), sig[:], MULT)
-
-        def quant_h(c, jt):
-            cols = slice(jt * JT, (jt + 1) * JT)
-            nc.vector.quantize_mx(
-                out=h_q[c][:, cols].bitcast(FP8X4),
-                scales=h_s[c][:, cols],
-                in_=h_b[c, jt][:].rearrange("p j t -> p (j t)"),
+            if jt == 0:
+                h_b[c] = keep.tile([P, J, PACK], BF16, name="h_b%d" % c, tag="x1%d" % (2 * c), align_bytes=64)
+            sig = ring.tile([P, JT // 2, PACK, 2], F32, name="sig", tag="sig", bufs=3)
+            nc.scalar.activation(sig[:], banks[c, jt][0][:].rearrange("p t (j e) -> p j t e", e=2), ACT.Sigmoid)
+            nc.vector.tensor_tensor(
+                h_b[c][:, jt * JT : (jt + 1) * JT, :].rearrange("p (j e) t -> p j t e", e=2),
+                banks[c, jt][1][:].rearrange("p t (j e) -> p j t e", e=2),
+                sig[:],
+                MULT,
             )
 
-        def unit(c, jt, pair):
-            up_pass(c, jt, 0, pair)
-            up_pass(c, jt, 1, pair)
+        def quant_h(c, j0, j1):
+            nc.vector.quantize_mx(
+                out=h_q[c][:, j0:j1].bitcast(FP8X4),
+                scales=h_s[c][:, j0:j1],
+                in_=h_b[c][:, j0:j1, :].rearrange("p j t -> p (j t)"),
+            )
+
+        def unit(c, jt):
+            up_pass(c, jt, 0)
+            up_pass(c, jt, 1)
             gate(c, jt)
 
-        y_bank = {}
-
-        def down(j0, j1, ns, bank):
-            y = psum.tile([P, len(ns), j1 - j0], F32, name="y", tag="bank%d" % bank)
-            for s, n in enumerate(ns):
-                y_bank[j0, n] = y[:, s, :]
-                for c in range(2):
-                    nc.tensor.matmul_mx(
-                        y[:, s, :],
-                        lhsT=wd_q[:, c, n * P : (n + 1) * P].bitcast(FP8X4),
-                        lhsT_scale=wd_s[4 * c : P, n * P : (n + 1) * P],
-                        rhs=h_q[c][:, j0:j1].bitcast(FP8X4),
-                        rhs_scale=h_s[c][:, j0:j1],
-                        start=(c == 0),
-                        stop=(c == 1),
-                    )
-
-        def place(j0, j1, n):
-            y_sb = ring.tile([P, j1 - j0], F32, name="y_sb", tag="y_sb", bufs=4)
-            nc.scalar.activation(y_sb[:], y_bank[j0, n], ACT.Identity, bias=bias[:, n : n + 1])
+        def down(n, j0, j1):
+            if j0 == 0:
+                y_sb[n] = keep.tile([P, J], F32, name="y_sb%d" % n, tag="x0%d" % n, align_bytes=64)
+            y = psum.tile([P, j1 - j0], F32, name="y", tag="bank")
+            for c in range(2):
+                nc.tensor.matmul_mx(
+                    y[:],
+                    lhsT=wd_q[:, c, n * P : (n + 1) * P].bitcast(FP8X4),
+                    lhsT_scale=wd_s[4 * c : P, n * P : (n + 1) * P],
+                    rhs=h_q[c][:, j0:j1].bitcast(FP8X4),
+                    rhs_scale=h_s[c][:, j0:j1],
+                    start=(c == 0),
+                    stop=(c == 1),
+                )
+            nc.scalar.activation(y_sb[n][:, j0:j1], y[:], ACT.Identity, bias=bias[:, n : n + 1])
             nc.vector.tensor_tensor(
-                pages[n][:].indirect(offs2_t[:, j0 // 16 : j1 // 16]), y_sb[:], wgo_t[:, j0:j1], MULT
+                pages[n][:].indirect(offs2_t[:, j0 // 16 : j1 // 16]), y_sb[n][:, j0:j1], wgo_t[:, j0:j1], MULT
             )
 
-        for hf in range(2):
-            gather(0, 0, hf)
-        weave_wg(0, 0, "scalar")
-        for hf in range(2):
-            gather(0, 1, hf)
-        quant_wg(0, 0)
-        weave_wg(0, 1, "scalar")
-        for hf in range(2):
-            gather(0, 2, hf)
-        quant_wg(0, 1)
-        deal_wu(0)
-        deal_wu_scales()
+        gather(0, 0, 0, HALF)
+        gather(0, 0, HALF, J)
+        gather(0, 1, 0, J)
         load_wg(1, 0)
+        load_x(1, 2)
+        load_x(1, 3)
         load_wg(1, 1)
+        gather(0, 2, 0, J)
+        deal_wu(0)
+        weave_wg(0, 1, nc.scalar.copy, 0, P)
+        gather(0, 3, 0, HALF)
+        gather(0, 3, HALF, J)
+        deal_wu_scales()
+        weave_x(0, 0, HALF)
+        weave_x(0, HALF, J)
+        quant_wg(0, 1)
+        weave_wg(0, 0, nc.scalar.copy, 0, P)
         load_wu(1)
         for q in range(4):
             nc.sync.dma_start(out=wd_s[32 * q : 32 * q + 8, :].bitcast(I32), in_=wd_scales[:, 4 * q : 4 * q + 4, :].bitcast(I32))
@@ -236,74 +234,61 @@ def tile_list_sigm_scatb_kernel(
             nc.sync.dma_start(out=bias[:], in_=b.rearrange("(c p) -> p c", p=P))
         nc.sync.dma_start(offs2_t[:], offs2)
         nc.sync.dma_start(out=wgo_t[:], in_=wgo)
-        for hf in range(2):
-            gather(0, 3, hf)
-        for hf in range(2):
-            weave_x(0, hf, 0, HALF)
-        for hf in range(2):
-            gather(1, 0, hf)
-        quant_x(0, 0, 0, HALF)
-        for hf in range(2):
-            gather(1, 1, hf)
-        quant_x(0, 1, 0, HALF)
+        gather(1, 0, 0, J)
+        gather(1, 1, 0, J)
+        quant_wg(0, 0)
+        quant_x(0, 0, J)
+        gather(1, 2, 0, J)
+        weave_wg(1, 0, nc.scalar.copy, 0, P)
         for jt in range(4):
-            up_pass(0, jt, 0, jt)
-        for hf in range(2):
-            gather(1, 2, hf)
-        for hf in range(2):
-            gather(1, 3, hf)
-        for jt in range(4):
-            weave_x(1, 0, jt * JT, (jt + 1) * JT)
-            quant_x(1, 0, jt * JT, (jt + 1) * JT)
-            up_pass(0, jt, 1, jt)
-        gate(0, 0)
-        weave_wg(1, 0, "scalar")
-        gate(0, 1)
-        quant_h(0, 0)
-        weave_wg(1, 1, "vector")
-        gate(0, 2)
-        quant_h(0, 1)
+            up_pass(0, jt, 0)
+        gather(1, 3, 0, HALF)
+        gather(1, 3, HALF, J)
+        weave_x(1, 0, 256)
+        quant_x(1, 0, 256)
+        up_pass(0, 0, 1)
+        up_pass(0, 1, 1)
+        weave_x(1, 256, HALF)
         quant_wg(1, 0)
-        gate(0, 3)
-        quant_h(0, 2)
-        quant_wg(1, 1)
+        quant_x(1, 256, HALF)
+        up_pass(0, 2, 1)
+        up_pass(0, 3, 1)
+        weave_wg(1, 1, nc.vector.tensor_copy, 0, P // 2)
+        gate(0, 0)
+        weave_wg(1, 1, nc.scalar.copy, P // 2, P)
+        gate(0, 1)
         deal_wu(1)
-        quant_h(0, 3)
-        weave_x(1, 1, 0, HALF)
-        unit(1, 0, 0)
-        quant_x(1, 1, 0, HALF)
-        quant_h(1, 0)
-        unit(1, 1, 1)
-        down(0, 128, range(4), 6)
-        quant_h(1, 1)
-        unit(1, 2, 2)
-        down(128, 256, range(4), 7)
+        quant_wg(1, 1)
+        gate(0, 2)
+        gate(0, 3)
+        unit(1, 0)
+        quant_h(0, 0, HALF)
+        unit(1, 1)
+        quant_h(1, 0, 256)
+        for jt in range(4, 8):
+            weave_x(1, jt * JT, (jt + 1) * JT)
+        quant_x(1, HALF, J)
+        unit(1, 2)
+        down(0, 0, 256)
+        unit(1, 3)
+        down(1, 0, 256)
+        quant_h(1, 256, HALF)
+        unit(0, 4)
+        down(2, 0, 256)
+        unit(0, 5)
+        down(3, 0, 256)
+        unit(0, 6)
+        down(0, 256, HALF)
+        unit(0, 7)
+        down(1, 256, HALF)
+        quant_h(0, HALF, J)
+        unit(1, 4)
+        unit(1, 5)
+        unit(1, 6)
+        unit(1, 7)
+        down(2, 256, HALF)
+        quant_h(1, HALF, J)
+        down(3, 256, HALF)
         for n in range(4):
-            place(0, 128, n)
-        quant_h(1, 2)
-        unit(1, 3, 0)
-        quant_h(1, 3)
-        unit(0, 4, 1)
-        down(256, 512, range(0, 2), 6)
-        place(128, 256, 0)
-        place(128, 256, 1)
-        quant_h(0, 4)
-        unit(1, 4, 2)
-        place(128, 256, 2)
-        place(128, 256, 3)
-        down(256, 512, range(2, 4), 7)
-        quant_h(1, 4)
-        pair = 0
-        for jt in range(5, 8):
-            unit(0, jt, pair % 3)
-            quant_h(0, jt)
-            unit(1, jt, (pair + 1) % 3)
-            place(256, 512, jt - 5)
-            quant_h(1, jt)
-            pair = pair + 2
-        for n in range(4):
-            down(512, 1024, [n], (6 + n) % 8)
-            if n == 0:
-                place(256, 512, 3)
-            place(512, 1024, n)
+            down(n, HALF, J)
             nc.sync.dma_start(out=out[n * P : (n + 1) * P, :], in_=pages[n][:])

@@ -12,6 +12,7 @@ U16 = mybir.dt.uint16
 U8 = mybir.dt.uint8
 FP8X4 = mybir.dt.float8_e4m3fn_x4
 MULT = mybir.AluOpType.mult
+ADD = mybir.AluOpType.add
 ACT = mybir.ActivationFunctionType
 
 P = 128
@@ -45,7 +46,7 @@ def tile_list_sigm_scatb_kernel(
         wu_q = [keep.tile([P, 2, PASS], I32, name="wu_q%d" % c, align_bytes=64) for c in range(2)]
         wg_q = {(c, a): keep.tile([P, PASS], I32, name="wg_q%d%d" % (c, a), align_bytes=64) for c in range(2) for a in range(2)}
         wg_s = {(c, a): keep.tile([P, PASS], U8, name="wg_s%d%d" % (c, a), align_bytes=64) for c in range(2) for a in range(2)}
-        x_q = [keep.tile([P, J], I32, name="x_q0", tag="x11", align_bytes=64), keep.tile([P, J], I32, name="x_q1", align_bytes=64)]
+        x_q = {1: keep.tile([P, J], I32, name="x_q1", align_bytes=64)}
         x_s = [keep.tile([P, J], U8, name="x_s%d" % a, align_bytes=64) for a in range(2)]
         h_q = [keep.tile([P, J], I32, name="h_q%d" % c, align_bytes=64) for c in range(2)]
         h_s = [keep.tile([P, J], U8, name="h_s%d" % c, align_bytes=64) for c in range(2)]
@@ -85,17 +86,25 @@ def tile_list_sigm_scatb_kernel(
         load_x(0, 1)
         load_wu(0)
         load_x(0, 2)
-        load_wg(0, 1)
         load_x(0, 3)
         for q in range(4):
             nc.sync.dma_start(out=wu_sraw[32 * q : 32 * q + 8, :].bitcast(I32), in_=wu_scales[:, 4 * q : 4 * q + 4, :].bitcast(I32))
         load_x(1, 0)
-        load_wg(0, 0)
+        load_wg(0, 1)
         load_x(1, 1)
+        load_wg(0, 0)
+        load_x(1, 2)
 
         gath = [keep.tile([P, PACK, J], F32, name="gath%d" % a) for a in range(2)]
-        x_b = [keep.tile([P, J, PACK], BF16, name="x_b%d" % a, align_bytes=64) for a in range(2)]
+        x_b = [keep.tile([P, J // (a + 1), PACK], BF16, name="x_b%d" % a, align_bytes=64) for a in range(2)]
+
+        def woven(a, j0, j1):
+            if a == 1 and j0 >= HALF:
+                return x_last[0][:, j0 - HALF : j1 - HALF, :]
+            return x_b[a][:, j0:j1, :]
+
         wg_b = {}
+        x_last = []
         banks = {}
         h_b = {}
         y_sb = {}
@@ -107,7 +116,7 @@ def tile_list_sigm_scatb_kernel(
 
         def weave_x(a, j0, j1):
             nc.scalar.copy(
-                x_b[a][:, j0:j1, :].rearrange("p (c j) i -> p c i j", j=4),
+                woven(a, j0, j1).rearrange("p (c j) i -> p c i j", j=4),
                 gath[a][:, :, j0:j1].rearrange("p i (c j) -> p c i j", j=4),
             )
 
@@ -115,12 +124,12 @@ def tile_list_sigm_scatb_kernel(
             nc.vector.quantize_mx(
                 out=x_q[a][:, j0:j1].bitcast(FP8X4),
                 scales=x_s[a][:, j0:j1],
-                in_=x_b[a][:, j0:j1, :].rearrange("p j i -> p (j i)"),
+                in_=woven(a, j0, j1).rearrange("p j i -> p (j i)"),
             )
 
         def weave_wg(c, a, copy, m0, m1):
             if m0 == 0:
-                wg_b[c, a] = ring.tile([P, PACK, P, PACK], BF16, name="wg_b", tag="wg_b", align_bytes=64)
+                wg_b[c, a] = keep.tile([P, PACK, P, PACK], BF16, name="wg_b%d%d" % (c, a), tag="wg_b%d" % a, align_bytes=64)
             copy(
                 wg_b[c, a][:, :, m0:m1, :].rearrange("p t m i -> p m t i"),
                 wg_raw[c, a][:, :, m0 * PACK : m1 * PACK].rearrange("p i (m t) -> p m t i", t=PACK),
@@ -213,19 +222,15 @@ def tile_list_sigm_scatb_kernel(
         gather(0, 0, HALF, J)
         gather(0, 1, 0, J)
         load_wg(1, 0)
-        load_x(1, 2)
         load_x(1, 3)
         load_wg(1, 1)
-        gather(0, 2, 0, J)
         deal_wu(0)
-        weave_wg(0, 1, nc.scalar.copy, 0, P)
+        gather(0, 2, 0, J)
         gather(0, 3, 0, HALF)
         gather(0, 3, HALF, J)
         deal_wu_scales()
         weave_x(0, 0, HALF)
         weave_x(0, HALF, J)
-        quant_wg(0, 1)
-        weave_wg(0, 0, nc.scalar.copy, 0, P)
         load_wu(1)
         for q in range(4):
             nc.sync.dma_start(out=wd_s[32 * q : 32 * q + 8, :].bitcast(I32), in_=wd_scales[:, 4 * q : 4 * q + 4, :].bitcast(I32))
@@ -235,10 +240,14 @@ def tile_list_sigm_scatb_kernel(
         nc.sync.dma_start(offs2_t[:], offs2)
         nc.sync.dma_start(out=wgo_t[:], in_=wgo)
         gather(1, 0, 0, J)
+        weave_wg(0, 1, nc.scalar.copy, 0, P)
         gather(1, 1, 0, J)
-        quant_wg(0, 0)
+        x_q[0] = keep.tile([P, J], I32, name="x_q0", tag="x11", align_bytes=64)
+        weave_wg(0, 0, nc.scalar.copy, 0, P)
+        quant_wg(0, 1)
         quant_x(0, 0, J)
         gather(1, 2, 0, J)
+        quant_wg(0, 0)
         weave_wg(1, 0, nc.scalar.copy, 0, P)
         for jt in range(4):
             up_pass(0, jt, 0)
@@ -249,7 +258,6 @@ def tile_list_sigm_scatb_kernel(
         up_pass(0, 0, 1)
         up_pass(0, 1, 1)
         weave_x(1, 256, HALF)
-        quant_wg(1, 0)
         quant_x(1, 256, HALF)
         up_pass(0, 2, 1)
         up_pass(0, 3, 1)
@@ -257,33 +265,37 @@ def tile_list_sigm_scatb_kernel(
         gate(0, 0)
         weave_wg(1, 1, nc.scalar.copy, P // 2, P)
         gate(0, 1)
+        quant_wg(1, 0)
         deal_wu(1)
         quant_wg(1, 1)
+        x_last.append(keep.tile([P, HALF, PACK], BF16, name="x_last", tag="wg_b1", align_bytes=64))
+        for j0 in range(HALF, J, JT):
+            nc.gpsimd.tensor_scalar(
+                woven(1, j0, j0 + JT), gath[1][:, :, j0 : j0 + JT].rearrange("p i j -> p j i"), 1.0, 0.0, MULT, ADD
+            )
         gate(0, 2)
         gate(0, 3)
         unit(1, 0)
-        quant_h(0, 0, HALF)
         unit(1, 1)
-        quant_h(1, 0, 256)
-        for jt in range(4, 8):
-            weave_x(1, jt * JT, (jt + 1) * JT)
-        quant_x(1, HALF, J)
+        quant_h(0, 0, HALF)
         unit(1, 2)
-        down(0, 0, 256)
+        quant_h(1, 0, 256)
+        quant_x(1, HALF, J)
         unit(1, 3)
-        down(1, 0, 256)
-        quant_h(1, 256, HALF)
+        down(0, 0, 256)
         unit(0, 4)
-        down(2, 0, 256)
+        quant_h(1, 256, HALF)
+        down(1, 0, 256)
         unit(0, 5)
-        down(3, 0, 256)
+        down(2, 0, 256)
         unit(0, 6)
-        down(0, 256, HALF)
         unit(0, 7)
-        down(1, 256, HALF)
-        quant_h(0, HALF, J)
+        down(3, 0, 256)
         unit(1, 4)
+        quant_h(0, HALF, J)
+        down(0, 256, HALF)
         unit(1, 5)
+        down(1, 256, HALF)
         unit(1, 6)
         unit(1, 7)
         down(2, 256, HALF)

@@ -1,6 +1,7 @@
 from contextlib import ExitStack
 
 import concourse.mybir as mybir
+from concourse.masks import make_identity
 
 K, R, N, T, J = 1024, 1024, 512, 2048, 1024
 FLOPS = 2 * J * (2 * K * R + R * N)
@@ -44,7 +45,7 @@ def tile_list_sigm_scatb_kernel(
         wd_s = keep.tile([P, N], U8, name="wd_s", align_bytes=64)
         wd_q = keep.tile([P, 2, N], I32, name="wd_q", align_bytes=64)
         wu_q = [keep.tile([P, 2, PASS], I32, name="wu_q%d" % c, align_bytes=64) for c in range(2)]
-        wg_q = {(c, a): keep.tile([P, PASS], I32, name="wg_q%d%d" % (c, a), align_bytes=64) for c in range(2) for a in range(2)}
+        wg_q = {(1, 1): keep.tile([P, PASS], I32, name="wg_q11", align_bytes=64)}
         wg_s = {(c, a): keep.tile([P, PASS], U8, name="wg_s%d%d" % (c, a), align_bytes=64) for c in range(2) for a in range(2)}
         x_q = {1: keep.tile([P, J], I32, name="x_q1", align_bytes=64)}
         x_s = [keep.tile([P, J], U8, name="x_s%d" % a, align_bytes=64) for a in range(2)]
@@ -55,6 +56,9 @@ def tile_list_sigm_scatb_kernel(
         wg_rows = wg.rearrange("(a p i) r -> a p i r", a=2, i=PACK)
         wu_rows = wu_words.rearrange("a p r i -> p a (r i)")
 
+        ident = keep.tile([P, P], F32, name="ident")
+        rows = keep.tile([P, JT], F32, name="rows")
+        make_identity(nc, ident[:])
         nc.gpsimd.memset(wu_sraw[:].bitcast(I32), 0)
         nc.gpsimd.memset(warm[:, 0:1], 0.0)
         nc.scalar.activation(warm[:, 1:2], warm[:, 0:1], ACT.Sigmoid)
@@ -80,22 +84,22 @@ def tile_list_sigm_scatb_kernel(
             nc.sync.dma_start(out=wu_raw[c][:], in_=wu_rows[:, :, c * PASS * PACK : (c + 1) * PASS * PACK].bitcast(I32))
 
         nc.sync.dma_start(offs_t[:], offs)
-        nc.sync.dma_start(out=wgt_t[:, :HALF], in_=wgt[:, :HALF])
+        nc.sync.dma_start(out=rows[0:64, :], in_=wgt[0:P:16, :].rearrange("g (u j) -> g u j", j=JT))
+        nc.sync.dma_start(out=rows[64:P, :], in_=wgo[0:P:16, :].rearrange("g (u j) -> g u j", j=JT))
         load_x(0, 0)
-        nc.sync.dma_start(out=wgt_t[:, HALF:], in_=wgt[:, HALF:])
         load_x(0, 1)
         load_wu(0)
         load_x(0, 2)
+        load_wg(0, 1)
         load_x(0, 3)
         for q in range(4):
             nc.sync.dma_start(out=wu_sraw[32 * q : 32 * q + 8, :].bitcast(I32), in_=wu_scales[:, 4 * q : 4 * q + 4, :].bitcast(I32))
         load_x(1, 0)
-        load_wg(0, 1)
         load_x(1, 1)
         load_wg(0, 0)
         load_x(1, 2)
 
-        gath = [keep.tile([P, PACK, J], F32, name="gath%d" % a) for a in range(2)]
+        gath = [keep.tile([P, PACK, J], F32, name="gath%d" % a, tag="gath%d" % a, align_bytes=64) for a in range(2)]
         x_b = [keep.tile([P, J // (a + 1), PACK], BF16, name="x_b%d" % a, align_bytes=64) for a in range(2)]
 
         def woven(a, j0, j1):
@@ -129,7 +133,7 @@ def tile_list_sigm_scatb_kernel(
 
         def weave_wg(c, a, copy, m0, m1):
             if m0 == 0:
-                wg_b[c, a] = keep.tile([P, PACK, P, PACK], BF16, name="wg_b%d%d" % (c, a), tag="wg_b%d" % a, align_bytes=64)
+                wg_b[c, a] = keep.tile([P, PACK, P, PACK], BF16, name="wg_b%d%d" % (c, a), tag="wg_b%d" % (a + 2 * c * (1 - a)), align_bytes=64)
             copy(
                 wg_b[c, a][:, :, m0:m1, :].rearrange("p t m i -> p m t i"),
                 wg_raw[c, a][:, :, m0 * PACK : m1 * PACK].rearrange("p i (m t) -> p m t i", t=PACK),
@@ -176,8 +180,10 @@ def tile_list_sigm_scatb_kernel(
                     )
 
         def gate(c, jt):
-            if jt == 0:
-                h_b[c] = keep.tile([P, J, PACK], BF16, name="h_b%d" % c, tag="x1%d" % (2 * c), align_bytes=64)
+            if (c, jt) == (0, 0):
+                h_both = keep.tile([P, 2 * J, PACK], BF16, name="h_both", tag="gath0", align_bytes=64)
+                h_b[0] = h_both[:, :J, :]
+                h_b[1] = h_both[:, J:, :]
             sig = ring.tile([P, JT // 2, PACK, 2], F32, name="sig", tag="sig", bufs=3)
             nc.scalar.activation(sig[:], banks[c, jt][0][:].rearrange("p t (j e) -> p j t e", e=2), ACT.Sigmoid)
             nc.vector.tensor_tensor(
@@ -218,8 +224,24 @@ def tile_list_sigm_scatb_kernel(
                 pages[n][:].indirect(offs2_t[:, j0 // 16 : j1 // 16]), y_sb[n][:, j0:j1], wgo_t[:, j0:j1], MULT
             )
 
+        turned = psum.tile([P, 2, 8, 8], F32, name="turned", tag="bank")
+        nc.tensor.transpose(turned[:].rearrange("p w g u -> p (w g u)"), rows[:], ident[:])
+
+        def spread(w, dst, hf):
+            wide = ring.tile([P, 4, 8, 16], F32, name="wide", tag="wide")
+            src = turned[:, w, :, 4 * hf : 4 * hf + 4].rearrange("p g u -> p u g")
+            nc.scalar.copy(wide[:], src.unsqueeze(3).to_broadcast([P, 4, 8, 16]))
+            back = psum.tile([P, 4, JT], F32, name="back", tag="bank")
+            for u in range(4):
+                nc.tensor.transpose(back[:, u, :], wide[:, u, :, :].rearrange("p g r -> p (g r)"), ident[:])
+            nc.scalar.copy(dst[:, hf * HALF : (hf + 1) * HALF], back[:].rearrange("p u j -> p (u j)"))
+
+        spread(0, wgt_t, 0)
+        spread(0, wgt_t, 1)
         gather(0, 0, 0, HALF)
         gather(0, 0, HALF, J)
+        spread(1, wgo_t, 0)
+        spread(1, wgo_t, 1)
         gather(0, 1, 0, J)
         load_wg(1, 0)
         load_x(1, 3)
@@ -238,21 +260,24 @@ def tile_list_sigm_scatb_kernel(
         with nc.allow_non_contiguous_dma(reason="one bias value a partition"):
             nc.sync.dma_start(out=bias[:], in_=b.rearrange("(c p) -> p c", p=P))
         nc.sync.dma_start(offs2_t[:], offs2)
-        nc.sync.dma_start(out=wgo_t[:], in_=wgo)
         gather(1, 0, 0, J)
         weave_wg(0, 1, nc.scalar.copy, 0, P)
         gather(1, 1, 0, J)
-        x_q[0] = keep.tile([P, J], I32, name="x_q0", tag="x11", align_bytes=64)
+        after11 = keep.tile([P, J + PASS], I32, name="after11", tag="x11", align_bytes=64)
+        x_q[0] = after11[:, :J]
+        wg_q[0, 1] = after11[:, J:]
         weave_wg(0, 0, nc.scalar.copy, 0, P)
         quant_wg(0, 1)
         quant_x(0, 0, J)
         gather(1, 2, 0, J)
+        wg_q[0, 0] = keep.tile([P, PASS], I32, name="wg_q00", tag="x12", align_bytes=64)
         quant_wg(0, 0)
         weave_wg(1, 0, nc.scalar.copy, 0, P)
         for jt in range(4):
             up_pass(0, jt, 0)
         gather(1, 3, 0, HALF)
         gather(1, 3, HALF, J)
+        wg_q[1, 0] = keep.tile([P, PASS], I32, name="wg_q10", tag="x13", align_bytes=64)
         weave_x(1, 0, 256)
         quant_x(1, 0, 256)
         up_pass(0, 0, 1)

@@ -21,6 +21,7 @@ PACK = 4
 PASS = 512
 HALF = 512
 JT = 128
+POOL_UNITS = ((0, 5), (0, 6), (0, 7), (1, 4), (1, 5), (1, 6))
 
 
 def tile_list_sigm_scatb_kernel(
@@ -184,6 +185,12 @@ def tile_list_sigm_scatb_kernel(
                 h_both = keep.tile([P, 2 * J, PACK], BF16, name="h_both", tag="gath0", align_bytes=64)
                 h_b[0] = h_both[:, :J, :]
                 h_b[1] = h_both[:, J:, :]
+            if (c, jt) in POOL_UNITS:
+                both = ring.tile([P, 2, JT, PACK], F32, name="both", tag="both", bufs=2)
+                nc.scalar.activation(both[:, 0], banks[c, jt][0][:].rearrange("p t j -> p j t"), ACT.Sigmoid)
+                nc.scalar.copy(both[:, 1], banks[c, jt][1][:].rearrange("p t j -> p j t"))
+                nc.gpsimd.tensor_tensor(h_b[c][:, jt * JT : (jt + 1) * JT, :], both[:, 0], both[:, 1], MULT)
+                return
             sig = ring.tile([P, JT // 2, PACK, 2], F32, name="sig", tag="sig", bufs=3)
             nc.scalar.activation(sig[:], banks[c, jt][0][:].rearrange("p t (j e) -> p j t e", e=2), ACT.Sigmoid)
             nc.vector.tensor_tensor(
@@ -207,7 +214,7 @@ def tile_list_sigm_scatb_kernel(
 
         def down(n, j0, j1):
             if j0 == 0:
-                y_sb[n] = keep.tile([P, J], F32, name="y_sb%d" % n, tag="x0%d" % n, align_bytes=64)
+                y_sb[n] = keep.tile([P, J + HALF], F32, name="y_sb%d" % n, tag="x0%d" % n, align_bytes=64)
             y = psum.tile([P, j1 - j0], F32, name="y", tag="bank")
             for c in range(2):
                 nc.tensor.matmul_mx(
@@ -220,6 +227,10 @@ def tile_list_sigm_scatb_kernel(
                     stop=(c == 1),
                 )
             nc.scalar.activation(y_sb[n][:, j0:j1], y[:], ACT.Identity, bias=bias[:, n : n + 1])
+            if j0 < HALF:
+                nc.gpsimd.tensor_tensor(y_sb[n][:, J + j0 : J + j1], y_sb[n][:, j0:j1], wgo_t[:, j0:j1], MULT)
+                nc.vector.tensor_copy(pages[n][:].indirect(offs2_t[:, j0 // 16 : j1 // 16]), y_sb[n][:, J + j0 : J + j1])
+                return
             nc.vector.tensor_tensor(
                 pages[n][:].indirect(offs2_t[:, j0 // 16 : j1 // 16]), y_sb[n][:, j0:j1], wgo_t[:, j0:j1], MULT
             )
@@ -312,20 +323,18 @@ def tile_list_sigm_scatb_kernel(
         quant_h(1, 256, HALF)
         down(1, 0, 256)
         unit(0, 5)
-        down(2, 0, 256)
+        down(2, 0, HALF)
         unit(0, 6)
         unit(0, 7)
-        down(3, 0, 256)
+        down(3, 0, HALF)
         unit(1, 4)
         quant_h(0, HALF, J)
-        down(0, 256, HALF)
         unit(1, 5)
-        down(1, 256, HALF)
-        unit(1, 6)
         unit(1, 7)
-        down(2, 256, HALF)
+        unit(1, 6)
+        down(0, 256, HALF)
         quant_h(1, HALF, J)
-        down(3, 256, HALF)
+        down(1, 256, HALF)
         for n in range(4):
             down(n, HALF, J)
             nc.sync.dma_start(out=out[n * P : (n + 1) * P, :], in_=pages[n][:])

@@ -20,8 +20,17 @@ P = 128
 PACK = 4
 PASS = 512
 HALF = 512
+QUART = 256
 JT = 128
-POOL_UNITS = ((0, 5), (0, 6), (0, 7), (1, 4), (1, 5), (1, 6))
+KB = 1024
+
+AT_X = 0
+AT_GATH = 64 * KB
+AT_WG_RAW = 96 * KB
+AT_WG_B = 112 * KB
+AT_SIG = 128 * KB
+AT_WU_RAW = 136 * KB
+AT_X_B = 144 * KB
 
 
 def tile_list_sigm_scatb_kernel(
@@ -30,8 +39,23 @@ def tile_list_sigm_scatb_kernel(
     nc = tc.nc
     with ExitStack() as ctx:
         keep = ctx.enter_context(tc.tile_pool(name="keep", bufs=1))
+        share = ctx.enter_context(tc.tile_pool(name="share", bufs=1))
         ring = ctx.enter_context(tc.tile_pool(name="ring", bufs=2))
-        psum = ctx.enter_context(tc.psum_pool(name="psum", bufs=8))
+        psum = ctx.enter_context(tc.psum_pool(name="psum", bufs=1))
+
+        def placed(name, shape, dtype, at):
+            return share.tile(shape, dtype, name=name, offset=at, align_bytes=64)
+
+        handed = []
+
+        def bank(name, shape, k=None):
+            if k is None:
+                k = len(handed) % 8
+                handed.append(name)
+            return psum.tile(shape, F32, name=name, tag="bank%d" % k)
+
+        def at_x(a, i):
+            return AT_X + (PACK * a + i) * 8 * KB
 
         offs_t = keep.tile([P, J // 16], U16, name="offs_t")
         offs2_t = keep.tile([P, J // 16], U16, name="offs2_t")
@@ -39,33 +63,28 @@ def tile_list_sigm_scatb_kernel(
         wgo_t = keep.tile([P, J], F32, name="wgo_t")
         bias = keep.tile([P, N // P], F32, name="bias")
         warm = keep.tile([P, 2], F32, name="warm")
-        planes = {(a, i): keep.tile([P, T], F32, name="x%d%d" % (a, i), tag="x%d%d" % (a, i), align_bytes=64) for a in range(2) for i in range(PACK)}
         pages = [keep.tile([P, T], F32, name="page%d" % n) for n in range(4)]
         wu_sraw = keep.tile([P, R], U8, name="wu_sraw", align_bytes=64)
         wu_s = keep.tile([P, R], U8, name="wu_s", align_bytes=64)
         wd_s = keep.tile([P, N], U8, name="wd_s", align_bytes=64)
         wd_q = keep.tile([P, 2, N], I32, name="wd_q", align_bytes=64)
-        wu_q = [keep.tile([P, 2, PASS], I32, name="wu_q%d" % c, align_bytes=64) for c in range(2)]
-        wg_q = {(1, 1): keep.tile([P, PASS], I32, name="wg_q11", align_bytes=64)}
         wg_s = {(c, a): keep.tile([P, PASS], U8, name="wg_s%d%d" % (c, a), align_bytes=64) for c in range(2) for a in range(2)}
-        x_q = {1: keep.tile([P, J], I32, name="x_q1", align_bytes=64)}
-        x_s = [keep.tile([P, J], U8, name="x_s%d" % a, align_bytes=64) for a in range(2)]
-        h_q = [keep.tile([P, J], I32, name="h_q%d" % c, align_bytes=64) for c in range(2)]
-        h_s = [keep.tile([P, J], U8, name="h_s%d" % c, align_bytes=64) for c in range(2)]
+        ident = keep.tile([P, P], F32, name="ident")
+        rows = keep.tile([P, JT], F32, name="rows")
+        planes = {(a, i): placed("x%d%d" % (a, i), [P, T], F32, at_x(a, i)) for a in range(2) for i in range(PACK)}
+        gath = [placed("gath%d" % a, [P, PACK, J], F32, AT_GATH + a * 16 * KB) for a in range(2)]
 
         x_rows = xT.rearrange("(a p i) t -> a i p t", a=2, i=PACK)
         wg_rows = wg.rearrange("(a p i) r -> a p i r", a=2, i=PACK)
         wu_rows = wu_words.rearrange("a p r i -> p a (r i)")
 
-        ident = keep.tile([P, P], F32, name="ident")
-        rows = keep.tile([P, JT], F32, name="rows")
         make_identity(nc, ident[:])
-        nc.gpsimd.memset(wu_sraw[:].bitcast(I32), 0)
-        nc.gpsimd.memset(warm[:, 0:1], 0.0)
+        nc.vector.memset(warm[:, 0:1], 0.0)
         nc.scalar.activation(warm[:, 1:2], warm[:, 0:1], ACT.Sigmoid)
-        nc.gpsimd.memset(wd_s[:].bitcast(I32), 0)
+        nc.vector.memset(wu_sraw[:].bitcast(I32), 0)
+        nc.vector.memset(wd_s[:].bitcast(I32), 0)
         for n in range(4):
-            nc.gpsimd.memset(pages[n][:], 0.0)
+            nc.vector.memset(pages[n][:].bitcast(I32), 0)
 
         wg_raw = {}
         wu_raw = {}
@@ -74,80 +93,78 @@ def tile_list_sigm_scatb_kernel(
             nc.sync.dma_start(out=planes[a, i][:], in_=x_rows[a, i])
 
         def load_wg(c, a):
-            if c == 0:
-                wg_raw[c, a] = keep.tile([P, PACK, PASS], F32, name="wg_raw0%d" % a)
-            else:
-                wg_raw[c, a] = keep.tile([P, PACK, PASS], F32, name="wg_raw1%d" % a, tag="x0%d" % a, align_bytes=64)
+            at = AT_WG_RAW + a * 8 * KB if c == 0 else at_x(0, a)
+            wg_raw[c, a] = placed("wg_raw%d%d" % (c, a), [P, PACK, PASS], F32, at)
             nc.sync.dma_start(out=wg_raw[c, a][:], in_=wg_rows[a][:, :, c * PASS : (c + 1) * PASS])
 
         def load_wu(c):
-            wu_raw[c] = ring.tile([P, 2, PASS], I32, name="wu_raw", tag="wu_raw")
+            wu_raw[c] = placed("wu_raw%d" % c, [P, 2, PASS], I32, AT_WU_RAW + c * 4 * KB)
             nc.sync.dma_start(out=wu_raw[c][:], in_=wu_rows[:, :, c * PASS * PACK : (c + 1) * PASS * PACK].bitcast(I32))
 
-        nc.sync.dma_start(offs_t[:], offs)
-        nc.sync.dma_start(out=rows[0:64, :], in_=wgt[0:P:16, :].rearrange("g (u j) -> g u j", j=JT))
-        nc.sync.dma_start(out=rows[64:P, :], in_=wgo[0:P:16, :].rearrange("g (u j) -> g u j", j=JT))
-        load_x(0, 0)
-        load_x(0, 1)
-        load_wu(0)
-        load_x(0, 2)
-        load_wg(0, 1)
-        load_x(0, 3)
-        for q in range(4):
-            nc.sync.dma_start(out=wu_sraw[32 * q : 32 * q + 8, :].bitcast(I32), in_=wu_scales[:, 4 * q : 4 * q + 4, :].bitcast(I32))
-        load_x(1, 0)
-        load_x(1, 1)
-        load_wg(0, 0)
-        load_x(1, 2)
+        def load_scales(dst, src):
+            for q in range(4):
+                nc.sync.dma_start(out=dst[32 * q : 32 * q + 8, :].bitcast(I32), in_=src[:, 4 * q : 4 * q + 4, :].bitcast(I32))
 
-        gath = [keep.tile([P, PACK, J], F32, name="gath%d" % a, tag="gath%d" % a, align_bytes=64) for a in range(2)]
-        x_b = [keep.tile([P, J // (a + 1), PACK], BF16, name="x_b%d" % a, align_bytes=64) for a in range(2)]
-
-        def woven(a, j0, j1):
-            if a == 1 and j0 >= HALF:
-                return x_last[0][:, j0 - HALF : j1 - HALF, :]
-            return x_b[a][:, j0:j1, :]
-
+        x_b = {}
+        x_q = {}
+        x_s = {}
         wg_b = {}
-        x_last = []
+        wg_q = {}
+        wu_q = {}
         banks = {}
+        sigs = {}
         h_b = {}
-        y_sb = {}
+        h_q = {}
+        h_s = {}
 
         def gather(a, i, j0, j1):
             nc.vector.tensor_tensor(
                 gath[a][:, i, j0:j1], planes[a, i][:].indirect(offs_t[:, j0 // 16 : j1 // 16]), wgt_t[:, j0:j1], MULT
             )
 
-        def weave_x(a, j0, j1):
+        def x_piece(a, j0, j1, at):
+            x_b[a, j0] = placed("x_b%d_%d" % (a, j0), [P, j1 - j0, PACK], BF16, at)
+
+        def weave_x(a, j0, j1, at):
+            x_piece(a, j0, j1, at)
             nc.scalar.copy(
-                woven(a, j0, j1).rearrange("p (c j) i -> p c i j", j=4),
+                x_b[a, j0][:].rearrange("p (c j) i -> p c i j", j=4),
                 gath[a][:, :, j0:j1].rearrange("p i (c j) -> p c i j", j=4),
             )
 
-        def quant_x(a, j0, j1):
-            nc.vector.quantize_mx(
-                out=x_q[a][:, j0:j1].bitcast(FP8X4),
-                scales=x_s[a][:, j0:j1],
-                in_=woven(a, j0, j1).rearrange("p j i -> p (j i)"),
-            )
+        def weave_x_pool(a, j0, j1, at):
+            x_piece(a, j0, j1, at)
+            for j in range(j0, j1, JT):
+                nc.gpsimd.tensor_scalar(
+                    x_b[a, j0][:, j - j0 : j - j0 + JT, :], gath[a][:, :, j : j + JT].rearrange("p i j -> p j i"), 1.0, 0.0, MULT, ADD
+                )
+
+        def quant_x(a, j0, j1, at):
+            codes = placed("x_q%d_%d" % (a, j0), [P, j1 - j0], I32, at)
+            scales = keep.tile([P, j1 - j0], U8, name="x_s%d_%d" % (a, j0), align_bytes=64)
+            for jt in range(j0 // JT, j1 // JT):
+                x_q[a, jt] = codes[:, jt * JT - j0 : (jt + 1) * JT - j0]
+                x_s[a, jt] = scales[:, jt * JT - j0 : (jt + 1) * JT - j0]
+            nc.vector.quantize_mx(out=codes[:].bitcast(FP8X4), scales=scales[:], in_=x_b[a, j0][:].rearrange("p j i -> p (j i)"))
 
         def weave_wg(c, a, copy, m0, m1):
-            if m0 == 0:
-                wg_b[c, a] = keep.tile([P, PACK, P, PACK], BF16, name="wg_b%d%d" % (c, a), tag="wg_b%d" % (a + 2 * c * (1 - a)), align_bytes=64)
+            if (c, a) not in wg_b:
+                wg_b[c, a] = placed("wg_b%d%d" % (c, a), [P, PACK, P, PACK], BF16, AT_WG_B + (2 * c + a) * 4 * KB)
             copy(
                 wg_b[c, a][:, :, m0:m1, :].rearrange("p t m i -> p m t i"),
                 wg_raw[c, a][:, :, m0 * PACK : m1 * PACK].rearrange("p i (m t) -> p m t i", t=PACK),
             )
 
-        def quant_wg(c, a):
+        def quant_wg(c, a, at):
+            wg_q[c, a] = placed("wg_q%d%d" % (c, a), [P, PASS], I32, at)
             nc.vector.quantize_mx(
                 out=wg_q[c, a][:].bitcast(FP8X4),
                 scales=wg_s[c, a][:],
                 in_=wg_b[c, a][:].rearrange("p t m i -> p (t m i)"),
             )
 
-        def deal_wu(c):
+        def deal_wu(c, dst):
+            wu_q[c] = dst
             nc.vector.tensor_copy(
                 wu_q[c][:].rearrange("p a (t g m) -> p a g t m", t=PACK, m=4),
                 wu_raw[c][:].rearrange("p a (g m t) -> p a g t m", t=PACK, m=4),
@@ -159,11 +176,10 @@ def tile_list_sigm_scatb_kernel(
                 wu_sraw[:].rearrange("p (c m t) -> p c t m", c=2, t=PACK),
             )
 
-        def up_pass(c, jt, a):
-            if a == 0:
-                banks[c, jt] = [psum.tile([P, PACK, JT], F32, name="up", tag="bank") for s in range(2)]
-            cols = slice(jt * JT, (jt + 1) * JT)
-            for s in range(2):
+        def up_pass(c, jt, a, sides=(0, 1)):
+            if (c, jt) not in banks:
+                banks[c, jt] = [bank("up", [P, PACK, JT], jt + 4 * s if jt < 4 else None) for s in range(2)]
+            for s in sides:
                 for t in range(PACK):
                     m = slice(t * P, (t + 1) * P)
                     if s == 0:
@@ -174,78 +190,122 @@ def tile_list_sigm_scatb_kernel(
                         banks[c, jt][s][:, t, :],
                         lhsT=w.bitcast(FP8X4),
                         lhsT_scale=ws,
-                        rhs=x_q[a][:, cols].bitcast(FP8X4),
-                        rhs_scale=x_s[a][:, cols],
+                        rhs=x_q[a, jt].bitcast(FP8X4),
+                        rhs_scale=x_s[a, jt],
                         start=(a == 0 and t == 0),
                         stop=(a == 1 and t == PACK - 1),
                     )
 
+        def chunk_of(jt):
+            return (jt // 2 * QUART, QUART) if jt < 4 else (HALF, HALF)
+
+        def h_slot(c, jt):
+            j0, w = chunk_of(jt)
+            if j0 not in h_b:
+                h_b[j0] = placed("h_b%d" % j0, [P, 2 * w, PACK], BF16, AT_X_B + 8 * KB if j0 == 0 else AT_GATH)
+            lo = c * w + jt * JT - j0
+            return h_b[j0][:, lo : lo + JT, :]
+
+        def pairs(bank):
+            return bank[:].rearrange("p t (j e) -> p j t e", e=2)
+
+        def sigmoid(c, jt, sig):
+            sigs[c, jt] = sig
+            nc.scalar.activation(sig[:], pairs(banks[c, jt][0]), ACT.Sigmoid)
+
         def gate(c, jt):
-            if (c, jt) == (0, 0):
-                h_both = keep.tile([P, 2 * J, PACK], BF16, name="h_both", tag="gath0", align_bytes=64)
-                h_b[0] = h_both[:, :J, :]
-                h_b[1] = h_both[:, J:, :]
-            if (c, jt) in POOL_UNITS:
-                both = ring.tile([P, 2, JT, PACK], F32, name="both", tag="both", bufs=2)
-                nc.scalar.activation(both[:, 0], banks[c, jt][0][:].rearrange("p t j -> p j t"), ACT.Sigmoid)
-                nc.scalar.copy(both[:, 1], banks[c, jt][1][:].rearrange("p t j -> p j t"))
-                nc.gpsimd.tensor_tensor(h_b[c][:, jt * JT : (jt + 1) * JT, :], both[:, 0], both[:, 1], MULT)
-                return
-            sig = ring.tile([P, JT // 2, PACK, 2], F32, name="sig", tag="sig", bufs=3)
-            nc.scalar.activation(sig[:], banks[c, jt][0][:].rearrange("p t (j e) -> p j t e", e=2), ACT.Sigmoid)
             nc.vector.tensor_tensor(
-                h_b[c][:, jt * JT : (jt + 1) * JT, :].rearrange("p (j e) t -> p j t e", e=2),
-                banks[c, jt][1][:].rearrange("p t (j e) -> p j t e", e=2),
-                sig[:],
-                MULT,
+                h_slot(c, jt).rearrange("p (j e) t -> p j t e", e=2), pairs(banks[c, jt][1]), sigs[c, jt][:], MULT
             )
 
-        def quant_h(c, j0, j1):
-            nc.vector.quantize_mx(
-                out=h_q[c][:, j0:j1].bitcast(FP8X4),
-                scales=h_s[c][:, j0:j1],
-                in_=h_b[c][:, j0:j1, :].rearrange("p j t -> p (j t)"),
-            )
+        def ring_sig():
+            return ring.tile([P, JT // 2, PACK, 2], F32, name="sig", tag="sig", bufs=3)
 
         def unit(c, jt):
             up_pass(c, jt, 0)
             up_pass(c, jt, 1)
+            sigmoid(c, jt, ring_sig())
             gate(c, jt)
 
-        def down(n, j0, j1):
-            if j0 == 0:
-                y_sb[n] = keep.tile([P, J + HALF], F32, name="y_sb%d" % n, tag="x0%d" % n, align_bytes=64)
-            y = psum.tile([P, j1 - j0], F32, name="y", tag="bank")
-            for c in range(2):
-                nc.tensor.matmul_mx(
-                    y[:],
-                    lhsT=wd_q[:, c, n * P : (n + 1) * P].bitcast(FP8X4),
-                    lhsT_scale=wd_s[4 * c : P, n * P : (n + 1) * P],
-                    rhs=h_q[c][:, j0:j1].bitcast(FP8X4),
-                    rhs_scale=h_s[c][:, j0:j1],
-                    start=(c == 0),
-                    stop=(c == 1),
-                )
-            nc.scalar.activation(y_sb[n][:, j0:j1], y[:], ACT.Identity, bias=bias[:, n : n + 1])
-            if j0 < HALF:
-                nc.gpsimd.tensor_tensor(y_sb[n][:, J + j0 : J + j1], y_sb[n][:, j0:j1], wgo_t[:, j0:j1], MULT)
-                nc.vector.tensor_copy(pages[n][:].indirect(offs2_t[:, j0 // 16 : j1 // 16]), y_sb[n][:, J + j0 : J + j1])
-                return
-            nc.vector.tensor_tensor(
-                pages[n][:].indirect(offs2_t[:, j0 // 16 : j1 // 16]), y_sb[n][:, j0:j1], wgo_t[:, j0:j1], MULT
-            )
+        def at_both(k):
+            return AT_WG_RAW + k % 4 * 4 * KB
 
-        turned = psum.tile([P, 2, 8, 8], F32, name="turned", tag="bank")
-        nc.tensor.transpose(turned[:].rearrange("p w g u -> p (w g u)"), rows[:], ident[:])
+        def pool_unit(k, c, jt):
+            up_pass(c, jt, 0)
+            up_pass(c, jt, 1)
+            both = placed("both%d" % k, [P, 2, JT, PACK], F32, at_both(k))
+            nc.scalar.activation(both[:, 0].rearrange("p (j e) t -> p j t e", e=2), pairs(banks[c, jt][0]), ACT.Sigmoid)
+            nc.scalar.copy(both[:, 1].rearrange("p (j e) t -> p j t e", e=2), pairs(banks[c, jt][1]))
+            nc.gpsimd.tensor_tensor(h_slot(c, jt), both[:, 0], both[:, 1], MULT)
+
+        def quant_h(j0, w, at):
+            h_q[j0] = placed("h_q%d" % j0, [P, 2 * w], I32, at)
+            h_s[j0] = keep.tile([P, 2 * w], U8, name="h_s%d" % j0, align_bytes=64)
+            nc.vector.quantize_mx(out=h_q[j0][:].bitcast(FP8X4), scales=h_s[j0][:], in_=h_b[j0][:].rearrange("p j t -> p (j t)"))
+
+        def down(n, j0, j1):
+            y = bank("y", [P, j1 - j0])
+            w = QUART if j0 < HALF else HALF
+            for lo in range(j0, j1, w):
+                for c in range(2):
+                    nc.tensor.matmul_mx(
+                        y[:, lo - j0 : lo - j0 + w],
+                        lhsT=wd_q[:, c, n * P : (n + 1) * P].bitcast(FP8X4),
+                        lhsT_scale=wd_s[4 * c : P, n * P : (n + 1) * P],
+                        rhs=h_q[lo][:, c * w : (c + 1) * w].bitcast(FP8X4),
+                        rhs_scale=h_s[lo][:, c * w : (c + 1) * w],
+                        start=(c == 0),
+                        stop=(c == 1),
+                    )
+            return y
+
+        def window(n, j0, j1):
+            return pages[n][:].indirect(offs2_t[:, j0 // 16 : j1 // 16])
+
+        def biased(n, j0, j1, at):
+            y = down(n, j0, j1)
+            y_sb = placed("y%d_%d" % (n, j0), [P, j1 - j0], F32, at)
+            nc.scalar.activation(y_sb[:], y[:], ACT.Identity, bias=bias[:, n : n + 1])
+            return y_sb
+
+        def weighted(n, j0, j1, at, at_w):
+            y_sb = biased(n, j0, j1, at)
+            y_w = placed("yw%d_%d" % (n, j0), [P, j1 - j0], F32, at_w)
+            nc.gpsimd.tensor_tensor(y_w[:], y_sb[:], wgo_t[:, j0:j1], MULT)
+            return y_w
+
+        def put(n, j0, j1, y_w):
+            nc.vector.tensor_copy(window(n, j0, j1), y_w[:])
+
+        def fused(n, j0, j1, at):
+            y_sb = biased(n, j0, j1, at)
+            nc.vector.tensor_tensor(window(n, j0, j1), y_sb[:], wgo_t[:, j0:j1], MULT)
 
         def spread(w, dst, hf):
             wide = ring.tile([P, 4, 8, 16], F32, name="wide", tag="wide")
             src = turned[:, w, :, 4 * hf : 4 * hf + 4].rearrange("p g u -> p u g")
             nc.scalar.copy(wide[:], src.unsqueeze(3).to_broadcast([P, 4, 8, 16]))
-            back = psum.tile([P, 4, JT], F32, name="back", tag="bank")
+            back = bank("back", [P, 4, JT], 2 * w + hf)
             for u in range(4):
                 nc.tensor.transpose(back[:, u, :], wide[:, u, :, :].rearrange("p g r -> p (g r)"), ident[:])
             nc.scalar.copy(dst[:, hf * HALF : (hf + 1) * HALF], back[:].rearrange("p u j -> p (u j)"))
+
+        nc.sync.dma_start(out=rows[0:64, :], in_=wgt[0:P:16, :].rearrange("g (u j) -> g u j", j=JT))
+        nc.sync.dma_start(out=rows[64:P, :], in_=wgo[0:P:16, :].rearrange("g (u j) -> g u j", j=JT))
+        nc.sync.dma_start(offs_t[:], offs)
+        for i in range(PACK):
+            load_x(0, i)
+        load_scales(wu_sraw, wu_scales)
+        load_x(1, 0)
+        load_wg(0, 0)
+        load_x(1, 1)
+        load_wg(0, 1)
+        load_wu(0)
+        load_x(1, 2)
+        load_x(1, 3)
+
+        turned = bank("turned", [P, 2, 8, 8], 7)
+        nc.tensor.transpose(turned[:].rearrange("p w g u -> p (w g u)"), rows[:], ident[:])
 
         spread(0, wgt_t, 0)
         spread(0, wgt_t, 1)
@@ -255,86 +315,97 @@ def tile_list_sigm_scatb_kernel(
         spread(1, wgo_t, 1)
         gather(0, 1, 0, J)
         load_wg(1, 0)
-        load_x(1, 3)
         load_wg(1, 1)
-        deal_wu(0)
+        load_wu(1)
+        load_scales(wd_s, wd_scales)
+        nc.sync.dma_start(out=wd_q[:], in_=wd_words.rearrange("a p n i -> p a (n i)").bitcast(I32))
+        nc.sync.dma_start(offs2_t[:], offs2)
+        with nc.allow_non_contiguous_dma(reason="one bias value a partition"):
+            nc.sync.dma_start(out=bias[:], in_=b.rearrange("(c p) -> p c", p=P))
         gather(0, 2, 0, J)
         gather(0, 3, 0, HALF)
         gather(0, 3, HALF, J)
+        weave_x(0, 0, HALF, AT_X_B)
+        weave_x(0, HALF, J, AT_X_B + 4 * KB)
         deal_wu_scales()
-        weave_x(0, 0, HALF)
-        weave_x(0, HALF, J)
-        load_wu(1)
-        for q in range(4):
-            nc.sync.dma_start(out=wd_s[32 * q : 32 * q + 8, :].bitcast(I32), in_=wd_scales[:, 4 * q : 4 * q + 4, :].bitcast(I32))
-        nc.sync.dma_start(out=wd_q[:], in_=wd_words.rearrange("a p n i -> p a (n i)").bitcast(I32))
-        with nc.allow_non_contiguous_dma(reason="one bias value a partition"):
-            nc.sync.dma_start(out=bias[:], in_=b.rearrange("(c p) -> p c", p=P))
-        nc.sync.dma_start(offs2_t[:], offs2)
         gather(1, 0, 0, J)
-        weave_wg(0, 1, nc.scalar.copy, 0, P)
-        gather(1, 1, 0, J)
-        after11 = keep.tile([P, J + PASS], I32, name="after11", tag="x11", align_bytes=64)
-        x_q[0] = after11[:, :J]
-        wg_q[0, 1] = after11[:, J:]
+        quant_x(0, 0, HALF, at_x(1, 0))
         weave_wg(0, 0, nc.scalar.copy, 0, P)
-        quant_wg(0, 1)
-        quant_x(0, 0, J)
-        gather(1, 2, 0, J)
-        wg_q[0, 0] = keep.tile([P, PASS], I32, name="wg_q00", tag="x12", align_bytes=64)
-        quant_wg(0, 0)
-        weave_wg(1, 0, nc.scalar.copy, 0, P)
+        gather(1, 1, 0, J)
+        quant_x(0, HALF, J, at_x(1, 1) + 6 * KB)
+        quant_wg(0, 0, at_x(1, 1))
+        weave_wg(0, 1, nc.scalar.copy, 0, P)
+        deal_wu(0, keep.tile([P, 2, PASS], I32, name="wu_q0", align_bytes=64))
+        quant_wg(0, 1, at_x(0, 2))
         for jt in range(4):
             up_pass(0, jt, 0)
-        gather(1, 3, 0, HALF)
-        gather(1, 3, HALF, J)
-        wg_q[1, 0] = keep.tile([P, PASS], I32, name="wg_q10", tag="x13", align_bytes=64)
-        weave_x(1, 0, 256)
-        quant_x(1, 0, 256)
+        gather(1, 2, 0, J)
+        gather(1, 3, 0, QUART)
+        gather(1, 3, QUART, J)
+        weave_x(1, 0, QUART, AT_X_B + 8 * KB)
+        weave_x(1, QUART, HALF, AT_X_B + 10 * KB)
+        quant_x(1, 0, QUART, at_x(1, 3))
         up_pass(0, 0, 1)
         up_pass(0, 1, 1)
-        weave_x(1, 256, HALF)
-        quant_x(1, 256, HALF)
+        weave_wg(1, 0, nc.vector.tensor_copy, 0, P)
+        quant_x(1, QUART, HALF, at_x(0, 0))
         up_pass(0, 2, 1)
         up_pass(0, 3, 1)
-        weave_wg(1, 1, nc.vector.tensor_copy, 0, P // 2)
+        quant_wg(1, 0, at_x(0, 2) + 2 * KB)
+        first_sigs = [placed("sig%d" % jt, [P, JT // 2, PACK, 2], F32, AT_SIG + jt * 2 * KB) for jt in range(4)]
+        sigmoid(0, 0, first_sigs[0])
+        sigmoid(0, 1, first_sigs[1])
         gate(0, 0)
-        weave_wg(1, 1, nc.scalar.copy, P // 2, P)
         gate(0, 1)
-        quant_wg(1, 0)
-        deal_wu(1)
-        quant_wg(1, 1)
-        x_last.append(keep.tile([P, HALF, PACK], BF16, name="x_last", tag="wg_b1", align_bytes=64))
-        for j0 in range(HALF, J, JT):
-            nc.gpsimd.tensor_scalar(
-                woven(1, j0, j0 + JT), gath[1][:, :, j0 : j0 + JT].rearrange("p i j -> p j i"), 1.0, 0.0, MULT, ADD
-            )
+        weave_wg(1, 1, nc.scalar.copy, 0, P // 2)
+        weave_wg(1, 1, nc.vector.tensor_copy, P // 2, P)
+        quant_wg(1, 1, AT_SIG + 2 * KB)
+        deal_wu(1, placed("wu_q1", [P, 2, PASS], I32, AT_WG_B + 12 * KB))
+        sigmoid(0, 2, first_sigs[2])
+        sigmoid(0, 3, first_sigs[3])
         gate(0, 2)
         gate(0, 3)
-        unit(1, 0)
-        unit(1, 1)
-        quant_h(0, 0, HALF)
-        unit(1, 2)
-        quant_h(1, 0, 256)
-        quant_x(1, HALF, J)
-        unit(1, 3)
-        down(0, 0, 256)
-        unit(0, 4)
-        quant_h(1, 256, HALF)
-        down(1, 0, 256)
-        unit(0, 5)
-        down(2, 0, HALF)
-        unit(0, 6)
-        unit(0, 7)
-        down(3, 0, HALF)
-        unit(1, 4)
-        quant_h(0, HALF, J)
-        unit(1, 5)
-        unit(1, 7)
-        unit(1, 6)
-        down(0, 256, HALF)
-        quant_h(1, HALF, J)
-        down(1, 256, HALF)
+        for jt in range(4):
+            up_pass(1, jt, 0, (0,))
+        for jt in range(2):
+            up_pass(1, jt, 1, (0,))
+        for jt in range(2):
+            up_pass(1, jt, 0, (1,))
+            up_pass(1, jt, 1, (1,))
+            sigmoid(1, jt, ring_sig())
+        weave_x(1, HALF, HALF + QUART, AT_SIG)
+        gate(1, 0)
+        gate(1, 1)
+        quant_h(0, QUART, at_x(1, 1) + 2 * KB)
+        for jt in range(2, 4):
+            up_pass(1, jt, 1, (0,))
+            up_pass(1, jt, 0, (1,))
+            up_pass(1, jt, 1, (1,))
+            sigmoid(1, jt, ring_sig())
+            gate(1, jt)
+        weave_x(1, HALF + QUART, J, AT_SIG + 4 * KB)
+        quant_x(1, HALF, HALF + QUART, at_x(1, 3) + 2 * KB)
+        y = down(0, 0, QUART)
+        first = placed("yw0_0", [P, QUART], F32, at_x(0, 3))
+        nc.vector.scalar_tensor_tensor(first[:], y[:], bias[:, 0:1], wgo_t[:, 0:QUART], ADD, MULT)
+        quant_x(1, HALF + QUART, J, at_x(1, 3) + 3 * KB)
+        quant_h(QUART, QUART, at_x(1, 1) + 4 * KB)
+        put(0, 0, QUART, first)
+        put(1, 0, QUART, weighted(1, 0, QUART, at_x(0, 3) + KB, at_x(0, 3) + 2 * KB))
+        late = [(c, jt) for jt in range(4, 7) for c in range(2)]
+        pool_unit(0, *late[0])
+        put(2, 0, HALF, weighted(2, 0, HALF, at_x(0, 3) + 4 * KB, at_x(0, 3) + 6 * KB))
+        put(0, QUART, HALF, weighted(0, QUART, HALF, at_x(1, 2) + 4 * KB, at_x(1, 2) + 5 * KB))
+        put(1, QUART, HALF, weighted(1, QUART, HALF, at_x(1, 2) + 6 * KB, at_x(1, 2) + 7 * KB))
+        for k in range(1, 6):
+            pool_unit(k, *late[k])
+        for c in range(2):
+            up_pass(c, 7, 0)
+            up_pass(c, 7, 1)
+            sigmoid(c, 7, placed("sig_last%d" % c, [P, JT // 2, PACK, 2], F32, at_both(6) + (1 - c) * 2 * KB))
+            gate(c, 7)
+        quant_h(HALF, HALF, at_x(1, 0) + 4 * KB)
+        fused(3, 0, HALF, at_both(6) - KB)
         for n in range(4):
-            down(n, HALF, J)
+            fused(n, HALF, J, at_x(0, 1) + n * 2 * KB)
             nc.sync.dma_start(out=out[n * P : (n + 1) * P, :], in_=pages[n][:])

@@ -79,12 +79,12 @@ def tile_list_sigm_scatb_kernel(
         wu_rows = wu_words.rearrange("a p r i -> p a (r i)")
 
         make_identity(nc, ident[:])
+        nc.gpsimd.memset(wu_sraw[:].bitcast(I32), 0)
         nc.vector.memset(warm[:, 0:1], 0.0)
         nc.scalar.activation(warm[:, 1:2], warm[:, 0:1], ACT.Sigmoid)
-        nc.vector.memset(wu_sraw[:].bitcast(I32), 0)
-        nc.vector.memset(wd_s[:].bitcast(I32), 0)
+        nc.gpsimd.memset(wd_s[:].bitcast(I32), 0)
         for n in range(4):
-            nc.vector.memset(pages[n][:].bitcast(I32), 0)
+            nc.gpsimd.memset(pages[n][:], 0.0)
 
         wg_raw = {}
         wu_raw = {}
@@ -392,13 +392,14 @@ def tile_list_sigm_scatb_kernel(
         quant_h(QUART, QUART, at_x(1, 1) + 4 * KB)
         put(0, 0, QUART, first)
         put(1, 0, QUART, weighted(1, 0, QUART, at_x(0, 3) + KB, at_x(0, 3) + 2 * KB))
-        late = [(c, jt) for jt in range(4, 7) for c in range(2)]
-        pool_unit(0, *late[0])
+        pool_unit(0, 0, 4)
+        unit(1, 4)
         put(2, 0, HALF, weighted(2, 0, HALF, at_x(0, 3) + 4 * KB, at_x(0, 3) + 6 * KB))
         put(0, QUART, HALF, weighted(0, QUART, HALF, at_x(1, 2) + 4 * KB, at_x(1, 2) + 5 * KB))
         put(1, QUART, HALF, weighted(1, QUART, HALF, at_x(1, 2) + 6 * KB, at_x(1, 2) + 7 * KB))
-        for k in range(1, 6):
-            pool_unit(k, *late[k])
+        for jt in range(5, 7):
+            for c in range(2):
+                pool_unit(2 * jt + c - 8, c, jt)
         for c in range(2):
             up_pass(c, 7, 0)
             up_pass(c, 7, 1)

@@ -65,7 +65,6 @@ def tile_list_sigm_scatb_kernel(
         warm = keep.tile([P, 2], F32, name="warm")
         pages = [keep.tile([P, T], F32, name="page%d" % n) for n in range(4)]
         wu_sraw = keep.tile([P, R], U8, name="wu_sraw", align_bytes=64)
-        wu_s = keep.tile([P, R], U8, name="wu_s", align_bytes=64)
         wd_s = keep.tile([P, N], U8, name="wd_s", align_bytes=64)
         wd_q = keep.tile([P, 2, N], I32, name="wd_q", align_bytes=64)
         wg_s = {(c, a): keep.tile([P, PASS], U8, name="wg_s%d%d" % (c, a), align_bytes=64) for c in range(2) for a in range(2)}
@@ -82,9 +81,6 @@ def tile_list_sigm_scatb_kernel(
         nc.gpsimd.memset(wu_sraw[:].bitcast(I32), 0)
         nc.vector.memset(warm[:, 0:1], 0.0)
         nc.scalar.activation(warm[:, 1:2], warm[:, 0:1], ACT.Sigmoid)
-        nc.gpsimd.memset(wd_s[:].bitcast(I32), 0)
-        for n in range(4):
-            nc.gpsimd.memset(pages[n][:], 0.0)
 
         wg_raw = {}
         wu_raw = {}
@@ -101,9 +97,9 @@ def tile_list_sigm_scatb_kernel(
             wu_raw[c] = placed("wu_raw%d" % c, [P, 2, PASS], I32, AT_WU_RAW + c * 4 * KB)
             nc.sync.dma_start(out=wu_raw[c][:], in_=wu_rows[:, :, c * PASS * PACK : (c + 1) * PASS * PACK].bitcast(I32))
 
-        def load_scales(dst, src):
+        def load_scales(queue, dst, src):
             for q in range(4):
-                nc.sync.dma_start(out=dst[32 * q : 32 * q + 8, :].bitcast(I32), in_=src[:, 4 * q : 4 * q + 4, :].bitcast(I32))
+                queue.dma_start(out=dst[32 * q : 32 * q + 8, :].bitcast(I32), in_=src[:, 4 * q : 4 * q + 4, :].bitcast(I32))
 
         x_b = {}
         x_q = {}
@@ -170,7 +166,7 @@ def tile_list_sigm_scatb_kernel(
                 wu_raw[c][:].rearrange("p a (g m t) -> p a g t m", t=PACK, m=4),
             )
 
-        def deal_wu_scales():
+        def deal_wu_scales(wu_s):
             nc.vector.tensor_copy(
                 wu_s[:].rearrange("p (c t m) -> p c t m", c=2, t=PACK),
                 wu_sraw[:].rearrange("p (c m t) -> p c t m", c=2, t=PACK),
@@ -202,7 +198,7 @@ def tile_list_sigm_scatb_kernel(
         def h_slot(c, jt):
             j0, w = chunk_of(jt)
             if j0 not in h_b:
-                h_b[j0] = placed("h_b%d" % j0, [P, 2 * w, PACK], BF16, AT_X_B + 8 * KB if j0 == 0 else AT_GATH)
+                h_b[j0] = placed("h_b%d" % j0, [P, 2 * w, PACK], BF16, {0: AT_X_B + 8 * KB, QUART: AT_GATH, HALF: AT_GATH + 2 * KB}[j0])
             lo = c * w + jt * JT - j0
             return h_b[j0][:, lo : lo + JT, :]
 
@@ -290,12 +286,15 @@ def tile_list_sigm_scatb_kernel(
                 nc.tensor.transpose(back[:, u, :], wide[:, u, :, :].rearrange("p g r -> p (g r)"), ident[:])
             nc.scalar.copy(dst[:, hf * HALF : (hf + 1) * HALF], back[:].rearrange("p u j -> p (u j)"))
 
+        load_scales(nc.gpsimd, wu_sraw, wu_scales)
+        nc.gpsimd.memset(wd_s[:].bitcast(I32), 0)
+        for n in range(4):
+            nc.gpsimd.memset(pages[n][:], 0.0)
         nc.sync.dma_start(out=rows[0:64, :], in_=wgt[0:P:16, :].rearrange("g (u j) -> g u j", j=JT))
         nc.sync.dma_start(out=rows[64:P, :], in_=wgo[0:P:16, :].rearrange("g (u j) -> g u j", j=JT))
         nc.sync.dma_start(offs_t[:], offs)
         for i in range(PACK):
             load_x(0, i)
-        load_scales(wu_sraw, wu_scales)
         load_x(1, 0)
         load_wg(0, 0)
         load_x(1, 1)
@@ -317,7 +316,7 @@ def tile_list_sigm_scatb_kernel(
         load_wg(1, 0)
         load_wg(1, 1)
         load_wu(1)
-        load_scales(wd_s, wd_scales)
+        load_scales(nc.sync, wd_s, wd_scales)
         nc.sync.dma_start(out=wd_q[:], in_=wd_words.rearrange("a p n i -> p a (n i)").bitcast(I32))
         nc.sync.dma_start(offs2_t[:], offs2)
         with nc.allow_non_contiguous_dma(reason="one bias value a partition"):
@@ -327,13 +326,14 @@ def tile_list_sigm_scatb_kernel(
         gather(0, 3, HALF, J)
         weave_x(0, 0, HALF, AT_X_B)
         weave_x(0, HALF, J, AT_X_B + 4 * KB)
-        deal_wu_scales()
         gather(1, 0, 0, J)
         quant_x(0, 0, HALF, at_x(1, 0))
         weave_wg(0, 0, nc.scalar.copy, 0, P)
         gather(1, 1, 0, J)
         quant_x(0, HALF, J, at_x(1, 1) + 6 * KB)
         quant_wg(0, 0, at_x(1, 1))
+        wu_s = placed("wu_s", [P, R], U8, at_x(1, 1) + 4 * KB)
+        deal_wu_scales(wu_s)
         weave_wg(0, 1, nc.scalar.copy, 0, P)
         deal_wu(0, keep.tile([P, 2, PASS], I32, name="wu_q0", align_bytes=64))
         quant_wg(0, 1, at_x(0, 2))
@@ -344,27 +344,28 @@ def tile_list_sigm_scatb_kernel(
         gather(1, 3, QUART, J)
         weave_x(1, 0, QUART, AT_X_B + 8 * KB)
         weave_x(1, QUART, HALF, AT_X_B + 10 * KB)
-        quant_x(1, 0, QUART, at_x(1, 3))
-        up_pass(0, 0, 1)
-        up_pass(0, 1, 1)
+        quant_x(1, 0, QUART, at_x(0, 2) + 5 * KB)
+        for side in range(2):
+            for jt in range(2):
+                up_pass(0, jt, 1, (side,))
         weave_wg(1, 0, nc.vector.tensor_copy, 0, P)
         quant_x(1, QUART, HALF, at_x(0, 0))
-        up_pass(0, 2, 1)
-        up_pass(0, 3, 1)
+        for side in range(2):
+            for jt in range(2, 4):
+                up_pass(0, jt, 1, (side,))
         quant_wg(1, 0, at_x(0, 2) + 2 * KB)
         first_sigs = [placed("sig%d" % jt, [P, JT // 2, PACK, 2], F32, AT_SIG + jt * 2 * KB) for jt in range(4)]
         sigmoid(0, 0, first_sigs[0])
         sigmoid(0, 1, first_sigs[1])
         gate(0, 0)
-        gate(0, 1)
         weave_wg(1, 1, nc.scalar.copy, 0, P // 2)
         weave_wg(1, 1, nc.vector.tensor_copy, P // 2, P)
-        quant_wg(1, 1, AT_SIG + 2 * KB)
-        deal_wu(1, placed("wu_q1", [P, 2, PASS], I32, AT_WG_B + 12 * KB))
-        sigmoid(0, 2, first_sigs[2])
-        sigmoid(0, 3, first_sigs[3])
-        gate(0, 2)
-        gate(0, 3)
+        gate(0, 1)
+        quant_wg(1, 1, at_x(0, 2) + 6 * KB)
+        deal_wu(1, placed("wu_q1", [P, 2, PASS], I32, at_x(1, 3) + 4 * KB))
+        for jt in range(2, 4):
+            sigmoid(0, jt, first_sigs[jt])
+            gate(0, jt)
         for jt in range(4):
             up_pass(1, jt, 0, (0,))
         for jt in range(2):
@@ -373,7 +374,7 @@ def tile_list_sigm_scatb_kernel(
             up_pass(1, jt, 0, (1,))
             up_pass(1, jt, 1, (1,))
             sigmoid(1, jt, ring_sig())
-        weave_x(1, HALF, HALF + QUART, AT_SIG)
+        weave_x(1, HALF, HALF + QUART, AT_SIG + 2 * KB)
         gate(1, 0)
         gate(1, 1)
         quant_h(0, QUART, at_x(1, 1) + 2 * KB)
@@ -389,9 +390,9 @@ def tile_list_sigm_scatb_kernel(
         first = placed("yw0_0", [P, QUART], F32, at_x(0, 3))
         nc.vector.scalar_tensor_tensor(first[:], y[:], bias[:, 0:1], wgo_t[:, 0:QUART], ADD, MULT)
         quant_x(1, HALF + QUART, J, at_x(1, 3) + 3 * KB)
-        quant_h(QUART, QUART, at_x(1, 1) + 4 * KB)
+        quant_h(QUART, QUART, at_x(1, 2))
         put(0, 0, QUART, first)
-        put(1, 0, QUART, weighted(1, 0, QUART, at_x(0, 3) + KB, at_x(0, 3) + 2 * KB))
+        put(1, 0, QUART, weighted(1, 0, QUART, at_x(0, 3) + KB, AT_GATH))
         pool_unit(0, 0, 4)
         unit(1, 4)
         put(2, 0, HALF, weighted(2, 0, HALF, at_x(0, 3) + 4 * KB, at_x(0, 3) + 6 * KB))

@@ -202,20 +202,20 @@ def tile_list_sigm_scatb_kernel(
             lo = c * w + jt * JT - j0
             return h_b[j0][:, lo : lo + JT, :]
 
-        def pairs(bank):
-            return bank[:].rearrange("p t (j e) -> p j t e", e=2)
+        def woven(bank):
+            return bank[:].rearrange("p t j -> p j t")
 
         def sigmoid(c, jt, sig):
             sigs[c, jt] = sig
-            nc.scalar.activation(sig[:], pairs(banks[c, jt][0]), ACT.Sigmoid)
+            nc.scalar.activation(sig[:], woven(banks[c, jt][0]), ACT.Sigmoid)
 
         def gate(c, jt):
             nc.vector.tensor_tensor(
-                h_slot(c, jt).rearrange("p (j e) t -> p j t e", e=2), pairs(banks[c, jt][1]), sigs[c, jt][:], MULT
+                h_slot(c, jt), woven(banks[c, jt][1]), sigs[c, jt][:], MULT
             )
 
         def ring_sig():
-            return ring.tile([P, JT // 2, PACK, 2], F32, name="sig", tag="sig", bufs=3)
+            return ring.tile([P, JT, PACK], F32, name="sig", tag="sig", bufs=3)
 
         def unit(c, jt):
             up_pass(c, jt, 0)
@@ -230,8 +230,8 @@ def tile_list_sigm_scatb_kernel(
             up_pass(c, jt, 0)
             up_pass(c, jt, 1)
             both = placed("both%d" % k, [P, 2, JT, PACK], F32, at_both(k))
-            nc.scalar.activation(both[:, 0].rearrange("p (j e) t -> p j t e", e=2), pairs(banks[c, jt][0]), ACT.Sigmoid)
-            nc.scalar.copy(both[:, 1].rearrange("p (j e) t -> p j t e", e=2), pairs(banks[c, jt][1]))
+            nc.scalar.activation(both[:, 0], woven(banks[c, jt][0]), ACT.Sigmoid)
+            nc.scalar.copy(both[:, 1], woven(banks[c, jt][1]))
             nc.gpsimd.tensor_tensor(h_slot(c, jt), both[:, 0], both[:, 1], MULT)
 
         def quant_h(j0, w, at):
@@ -354,7 +354,7 @@ def tile_list_sigm_scatb_kernel(
             for jt in range(2, 4):
                 up_pass(0, jt, 1, (side,))
         quant_wg(1, 0, at_x(0, 2) + 2 * KB)
-        first_sigs = [placed("sig%d" % jt, [P, JT // 2, PACK, 2], F32, AT_SIG + jt * 2 * KB) for jt in range(4)]
+        first_sigs = [placed("sig%d" % jt, [P, JT, PACK], F32, AT_SIG + jt * 2 * KB) for jt in range(4)]
         sigmoid(0, 0, first_sigs[0])
         sigmoid(0, 1, first_sigs[1])
         gate(0, 0)
@@ -404,7 +404,7 @@ def tile_list_sigm_scatb_kernel(
         for c in range(2):
             up_pass(c, 7, 0)
             up_pass(c, 7, 1)
-            sigmoid(c, 7, placed("sig_last%d" % c, [P, JT // 2, PACK, 2], F32, at_both(6) + (1 - c) * 2 * KB))
+            sigmoid(c, 7, placed("sig_last%d" % c, [P, JT, PACK], F32, at_both(6) + (1 - c) * 2 * KB))
             gate(c, 7)
         quant_h(HALF, HALF, at_x(1, 0) + 4 * KB)
         fused(3, 0, HALF, at_both(6) - KB)

@@ -277,14 +277,14 @@ def tile_list_sigm_scatb_kernel(
             y_sb = biased(n, j0, j1, at)
             nc.vector.tensor_tensor(window(n, j0, j1), y_sb[:], wgo_t[:, j0:j1], MULT)
 
-        def spread(w, dst, hf):
-            wide = ring.tile([P, 4, 8, 16], F32, name="wide", tag="wide")
-            src = turned[:, w, :, 4 * hf : 4 * hf + 4].rearrange("p g u -> p u g")
-            nc.scalar.copy(wide[:], src.unsqueeze(3).to_broadcast([P, 4, 8, 16]))
-            back = bank("back", [P, 4, JT], 2 * w + hf)
-            for u in range(4):
+        def spread(w, dst, u0, u1, k):
+            wide = ring.tile([P, u1 - u0, 8, 16], F32, name="wide", tag="wide")
+            src = turned[:, w, :, u0:u1].rearrange("p g u -> p u g")
+            nc.scalar.copy(wide[:], src.unsqueeze(3).to_broadcast([P, u1 - u0, 8, 16]))
+            back = bank("back", [P, u1 - u0, JT], k)
+            for u in range(u1 - u0):
                 nc.tensor.transpose(back[:, u, :], wide[:, u, :, :].rearrange("p g r -> p (g r)"), ident[:])
-            nc.scalar.copy(dst[:, hf * HALF : (hf + 1) * HALF], back[:].rearrange("p u j -> p (u j)"))
+            nc.scalar.copy(dst[:, u0 * JT : u1 * JT], back[:].rearrange("p u j -> p (u j)"))
 
         load_scales(nc.gpsimd, wu_sraw, wu_scales)
         nc.gpsimd.memset(wd_s[:].bitcast(I32), 0)
@@ -306,12 +306,14 @@ def tile_list_sigm_scatb_kernel(
         turned = bank("turned", [P, 2, 8, 8], 7)
         nc.tensor.transpose(turned[:].rearrange("p w g u -> p (w g u)"), rows[:], ident[:])
 
-        spread(0, wgt_t, 0)
-        spread(0, wgt_t, 1)
-        gather(0, 0, 0, HALF)
-        gather(0, 0, HALF, J)
-        spread(1, wgo_t, 0)
-        spread(1, wgo_t, 1)
+        spread(0, wgt_t, 0, 2, 0)
+        spread(0, wgt_t, 2, 5, 1)
+        spread(0, wgt_t, 5, 8, 2)
+        gather(0, 0, 0, 2 * JT)
+        gather(0, 0, 2 * JT, 5 * JT)
+        gather(0, 0, 5 * JT, J)
+        spread(1, wgo_t, 0, 4, 3)
+        spread(1, wgo_t, 4, 8, 4)
         gather(0, 1, 0, J)
         load_wg(1, 0)
         load_wg(1, 1)
@@ -366,17 +368,21 @@ def tile_list_sigm_scatb_kernel(
         for jt in range(2, 4):
             sigmoid(0, jt, first_sigs[jt])
             gate(0, jt)
+        weave_x_pool(1, HALF + QUART, J, AT_WU_RAW + 4 * KB)
         for jt in range(4):
             up_pass(1, jt, 0, (0,))
         for jt in range(2):
             up_pass(1, jt, 1, (0,))
+        weave_x(1, HALF, HALF + QUART, AT_SIG + 2 * KB)
         for jt in range(2):
             up_pass(1, jt, 0, (1,))
             up_pass(1, jt, 1, (1,))
-            sigmoid(1, jt, ring_sig())
-        weave_x(1, HALF, HALF + QUART, AT_SIG + 2 * KB)
+        sigmoid(1, 0, placed("sig10", [P, JT, PACK], F32, at_x(1, 3)))
+        sigmoid(1, 1, ring_sig())
         gate(1, 0)
         gate(1, 1)
+        quant_x(1, HALF, HALF + QUART, at_x(1, 3))
+        quant_x(1, HALF + QUART, J, at_x(1, 3) + KB)
         quant_h(0, QUART, at_x(1, 1) + 2 * KB)
         for jt in range(2, 4):
             up_pass(1, jt, 1, (0,))
@@ -384,12 +390,9 @@ def tile_list_sigm_scatb_kernel(
             up_pass(1, jt, 1, (1,))
             sigmoid(1, jt, ring_sig())
             gate(1, jt)
-        weave_x(1, HALF + QUART, J, AT_SIG + 4 * KB)
-        quant_x(1, HALF, HALF + QUART, at_x(1, 3) + 2 * KB)
         y = down(0, 0, QUART)
         first = placed("yw0_0", [P, QUART], F32, at_x(0, 3))
         nc.vector.scalar_tensor_tensor(first[:], y[:], bias[:, 0:1], wgo_t[:, 0:QUART], ADD, MULT)
-        quant_x(1, HALF + QUART, J, at_x(1, 3) + 3 * KB)
         quant_h(QUART, QUART, at_x(1, 2))
         put(0, 0, QUART, first)
         put(1, 0, QUART, weighted(1, 0, QUART, at_x(0, 3) + KB, AT_GATH))

@@ -93,6 +93,11 @@ def tile_list_sigm_scatb_kernel(
             wg_raw[c, a] = placed("wg_raw%d%d" % (c, a), [P, PACK, PASS], F32, at)
             nc.sync.dma_start(out=wg_raw[c, a][:], in_=wg_rows[a][:, :, c * PASS : (c + 1) * PASS])
 
+        def load_wg_half(c, a, hf):
+            lo = c * PASS + hf * QUART
+            wg_raw[c, a, hf] = placed("wg_raw%d%d%d" % (c, a, hf), [P, PACK, QUART], F32, at_x(0, a) + hf * 4 * KB)
+            nc.sync.dma_start(out=wg_raw[c, a, hf][:], in_=wg_rows[a][:, :, lo : lo + QUART])
+
         def load_wu(c):
             wu_raw[c] = placed("wu_raw%d" % c, [P, 2, PASS], I32, AT_WU_RAW + c * 4 * KB)
             nc.sync.dma_start(out=wu_raw[c][:], in_=wu_rows[:, :, c * PASS * PACK : (c + 1) * PASS * PACK].bitcast(I32))
@@ -146,10 +151,8 @@ def tile_list_sigm_scatb_kernel(
         def weave_wg(c, a, copy, m0, m1):
             if (c, a) not in wg_b:
                 wg_b[c, a] = placed("wg_b%d%d" % (c, a), [P, PACK, P, PACK], BF16, AT_WG_B + (2 * c + a) * 4 * KB)
-            copy(
-                wg_b[c, a][:, :, m0:m1, :].rearrange("p t m i -> p m t i"),
-                wg_raw[c, a][:, :, m0 * PACK : m1 * PACK].rearrange("p i (m t) -> p m t i", t=PACK),
-            )
+            raw = wg_raw[c, a] if m1 - m0 == P else wg_raw[c, a, m0 // (P // 2)]
+            copy(wg_b[c, a][:, :, m0:m1, :].rearrange("p t m i -> p m t i"), raw[:].rearrange("p i (m t) -> p m t i", t=PACK))
 
         def quant_wg(c, a, at):
             wg_q[c, a] = placed("wg_q%d%d" % (c, a), [P, PASS], I32, at)
@@ -316,7 +319,8 @@ def tile_list_sigm_scatb_kernel(
         spread(1, wgo_t, 4, 8, 4)
         gather(0, 1, 0, J)
         load_wg(1, 0)
-        load_wg(1, 1)
+        load_wg_half(1, 1, 1)
+        load_wg_half(1, 1, 0)
         load_wu(1)
         load_scales(nc.sync, wd_s, wd_scales)
         nc.sync.dma_start(out=wd_q[:], in_=wd_words.rearrange("a p n i -> p a (n i)").bitcast(I32))
@@ -351,6 +355,7 @@ def tile_list_sigm_scatb_kernel(
             for jt in range(2):
                 up_pass(0, jt, 1, (side,))
         weave_wg(1, 0, nc.vector.tensor_copy, 0, P)
+        weave_wg(1, 1, nc.vector.tensor_copy, P // 2, P)
         quant_x(1, QUART, HALF, at_x(0, 0))
         for side in range(2):
             for jt in range(2, 4):
@@ -361,7 +366,6 @@ def tile_list_sigm_scatb_kernel(
         sigmoid(0, 1, first_sigs[1])
         gate(0, 0)
         weave_wg(1, 1, nc.scalar.copy, 0, P // 2)
-        weave_wg(1, 1, nc.vector.tensor_copy, P // 2, P)
         gate(0, 1)
         quant_wg(1, 1, at_x(0, 2) + 6 * KB)
         deal_wu(1, placed("wu_q1", [P, 2, PASS], I32, at_x(1, 3) + 4 * KB))

@@ -152,7 +152,7 @@ def tile_list_sigm_scatb_kernel(
             if (c, a) not in wg_b:
                 wg_b[c, a] = placed("wg_b%d%d" % (c, a), [P, PACK, P, PACK], BF16, AT_WG_B + (2 * c + a) * 4 * KB)
             raw = wg_raw[c, a] if m1 - m0 == P else wg_raw[c, a, m0 // (P // 2)]
-            copy(wg_b[c, a][:, :, m0:m1, :].rearrange("p t m i -> p m t i"), raw[:].rearrange("p i (m t) -> p m t i", t=PACK))
+            copy(wg_b[c, a][:, :, m0:m1, :].rearrange("p t m i -> p m i t"), raw[:].rearrange("p i (m t) -> p m i t", t=PACK))
 
         def quant_wg(c, a, at):
             wg_q[c, a] = placed("wg_q%d%d" % (c, a), [P, PASS], I32, at)
@@ -165,8 +165,8 @@ def tile_list_sigm_scatb_kernel(
         def deal_wu(c, dst):
             wu_q[c] = dst
             nc.vector.tensor_copy(
-                wu_q[c][:].rearrange("p a (t g m) -> p a g t m", t=PACK, m=4),
-                wu_raw[c][:].rearrange("p a (g m t) -> p a g t m", t=PACK, m=4),
+                wu_q[c][:].rearrange("p a (t m) -> p a m t", t=PACK),
+                wu_raw[c][:].rearrange("p a (m t) -> p a m t", t=PACK),
             )
 
         def deal_wu_scales(wu_s):

@@ -18,10 +18,12 @@ ACT = mybir.ActivationFunctionType
 
 P = 128
 PACK = 4
-PASS = 512
-HALF = 512
-QUART = 256
+PASS = P * PACK
+HALF = J // 2
+QUART = J // 4
 JT = 128
+GROUP = 16
+BANKS = 8
 KB = 1024
 
 AT_X = 0
@@ -46,24 +48,25 @@ def tile_list_sigm_scatb_kernel(
         def placed(name, shape, dtype, at):
             return share.tile(shape, dtype, name=name, offset=at, align_bytes=64)
 
-        handed = []
-
-        def bank(name, shape, k=None):
-            if k is None:
-                k = len(handed) % 8
-                handed.append(name)
-            return psum.tile(shape, F32, name=name, tag="bank%d" % k)
-
         def at_x(a, i):
             return AT_X + (PACK * a + i) * 8 * KB
 
-        offs_t = keep.tile([P, J // 16], U16, name="offs_t")
-        offs2_t = keep.tile([P, J // 16], U16, name="offs2_t")
+        handed = []
+
+        def bank(name, shape, k):
+            return psum.tile(shape, F32, name=name, tag="bank%d" % k)
+
+        def next_bank(name, shape):
+            handed.append(name)
+            return bank(name, shape, (len(handed) - 1) % BANKS)
+
+        offs_t = keep.tile([P, J // GROUP], U16, name="offs_t")
+        offs2_t = keep.tile([P, J // GROUP], U16, name="offs2_t")
         wgt_t = keep.tile([P, J], F32, name="wgt_t")
         wgo_t = keep.tile([P, J], F32, name="wgo_t")
         bias = keep.tile([P, N // P], F32, name="bias")
         warm = keep.tile([P, 2], F32, name="warm")
-        pages = [keep.tile([P, T], F32, name="page%d" % n) for n in range(4)]
+        pages = [keep.tile([P, T], F32, name="page%d" % n) for n in range(N // P)]
         wu_sraw = keep.tile([P, R], U8, name="wu_sraw", align_bytes=64)
         wd_s = keep.tile([P, N], U8, name="wd_s", align_bytes=64)
         wd_q = keep.tile([P, 2, N], I32, name="wd_q", align_bytes=64)
@@ -77,35 +80,7 @@ def tile_list_sigm_scatb_kernel(
         wg_rows = wg.rearrange("(a p i) r -> a p i r", a=2, i=PACK)
         wu_rows = wu_words.rearrange("a p r i -> p a (r i)")
 
-        make_identity(nc, ident[:])
-        nc.gpsimd.memset(wu_sraw[:].bitcast(I32), 0)
-        nc.vector.memset(warm[:, 0:1], 0.0)
-        nc.scalar.activation(warm[:, 1:2], warm[:, 0:1], ACT.Sigmoid)
-
-        wg_raw = {}
         wu_raw = {}
-
-        def load_x(a, i):
-            nc.sync.dma_start(out=planes[a, i][:], in_=x_rows[a, i])
-
-        def load_wg(c, a):
-            at = AT_WG_RAW + a * 8 * KB if c == 0 else at_x(0, a)
-            wg_raw[c, a] = placed("wg_raw%d%d" % (c, a), [P, PACK, PASS], F32, at)
-            nc.sync.dma_start(out=wg_raw[c, a][:], in_=wg_rows[a][:, :, c * PASS : (c + 1) * PASS])
-
-        def load_wg_half(c, a, hf):
-            lo = c * PASS + hf * QUART
-            wg_raw[c, a, hf] = placed("wg_raw%d%d%d" % (c, a, hf), [P, PACK, QUART], F32, at_x(0, a) + hf * 4 * KB)
-            nc.sync.dma_start(out=wg_raw[c, a, hf][:], in_=wg_rows[a][:, :, lo : lo + QUART])
-
-        def load_wu(c):
-            wu_raw[c] = placed("wu_raw%d" % c, [P, 2, PASS], I32, AT_WU_RAW + c * 4 * KB)
-            nc.sync.dma_start(out=wu_raw[c][:], in_=wu_rows[:, :, c * PASS * PACK : (c + 1) * PASS * PACK].bitcast(I32))
-
-        def load_scales(queue, dst, src):
-            for q in range(4):
-                queue.dma_start(out=dst[32 * q : 32 * q + 8, :].bitcast(I32), in_=src[:, 4 * q : 4 * q + 4, :].bitcast(I32))
-
         x_b = {}
         x_q = {}
         x_s = {}
@@ -118,23 +93,45 @@ def tile_list_sigm_scatb_kernel(
         h_q = {}
         h_s = {}
 
+        def load_x(a, i):
+            nc.sync.dma_start(out=planes[a, i][:], in_=x_rows[a, i])
+
+        def load_wg(a, r0, r1, at):
+            raw = placed("wg_raw%d_%d" % (a, r0), [P, PACK, r1 - r0], F32, at)
+            nc.sync.dma_start(out=raw[:], in_=wg_rows[a][:, :, r0:r1])
+            return raw
+
+        def load_wu(c):
+            wu_raw[c] = placed("wu_raw%d" % c, [P, 2, PASS], I32, AT_WU_RAW + c * 4 * KB)
+            nc.sync.dma_start(out=wu_raw[c][:], in_=wu_rows[:, :, c * PASS * PACK : (c + 1) * PASS * PACK].bitcast(I32))
+
+        def load_scales(queue, dst, src):
+            for q in range(4):
+                queue.dma_start(out=dst[32 * q : 32 * q + 8, :].bitcast(I32), in_=src[:, 4 * q : 4 * q + 4, :].bitcast(I32))
+
+        def spread(w, dst, u0, u1, k):
+            wide = ring.tile([P, u1 - u0, P // GROUP, GROUP], F32, name="wide", tag="wide")
+            src = turned[:, w, :, u0:u1].rearrange("p g u -> p u g")
+            nc.scalar.copy(wide[:], src.unsqueeze(3).to_broadcast([P, u1 - u0, P // GROUP, GROUP]))
+            back = bank("back", [P, u1 - u0, JT], k)
+            for u in range(u1 - u0):
+                nc.tensor.transpose(back[:, u, :], wide[:, u, :, :].rearrange("p g r -> p (g r)"), ident[:])
+            nc.scalar.copy(dst[:, u0 * JT : u1 * JT], back[:].rearrange("p u j -> p (u j)"))
+
         def gather(a, i, j0, j1):
             nc.vector.tensor_tensor(
-                gath[a][:, i, j0:j1], planes[a, i][:].indirect(offs_t[:, j0 // 16 : j1 // 16]), wgt_t[:, j0:j1], MULT
+                gath[a][:, i, j0:j1], planes[a, i][:].indirect(offs_t[:, j0 // GROUP : j1 // GROUP]), wgt_t[:, j0:j1], MULT
             )
 
-        def x_piece(a, j0, j1, at):
-            x_b[a, j0] = placed("x_b%d_%d" % (a, j0), [P, j1 - j0, PACK], BF16, at)
-
         def weave_x(a, j0, j1, at):
-            x_piece(a, j0, j1, at)
+            x_b[a, j0] = placed("x_b%d_%d" % (a, j0), [P, j1 - j0, PACK], BF16, at)
             nc.scalar.copy(
                 x_b[a, j0][:].rearrange("p (c j) i -> p c i j", j=4),
                 gath[a][:, :, j0:j1].rearrange("p i (c j) -> p c i j", j=4),
             )
 
         def weave_x_pool(a, j0, j1, at):
-            x_piece(a, j0, j1, at)
+            x_b[a, j0] = placed("x_b%d_%d" % (a, j0), [P, j1 - j0, PACK], BF16, at)
             for j in range(j0, j1, JT):
                 nc.gpsimd.tensor_scalar(
                     x_b[a, j0][:, j - j0 : j - j0 + JT, :], gath[a][:, :, j : j + JT].rearrange("p i j -> p j i"), 1.0, 0.0, MULT, ADD
@@ -148,36 +145,27 @@ def tile_list_sigm_scatb_kernel(
                 x_s[a, jt] = scales[:, jt * JT - j0 : (jt + 1) * JT - j0]
             nc.vector.quantize_mx(out=codes[:].bitcast(FP8X4), scales=scales[:], in_=x_b[a, j0][:].rearrange("p j i -> p (j i)"))
 
-        def weave_wg(c, a, copy, m0, m1):
+        def weave_wg(c, a, copy, raw, m0, m1):
             if (c, a) not in wg_b:
                 wg_b[c, a] = placed("wg_b%d%d" % (c, a), [P, PACK, P, PACK], BF16, AT_WG_B + (2 * c + a) * 4 * KB)
-            raw = wg_raw[c, a] if m1 - m0 == P else wg_raw[c, a, m0 // (P // 2)]
             copy(wg_b[c, a][:, :, m0:m1, :].rearrange("p t m i -> p m i t"), raw[:].rearrange("p i (m t) -> p m i t", t=PACK))
 
         def quant_wg(c, a, at):
             wg_q[c, a] = placed("wg_q%d%d" % (c, a), [P, PASS], I32, at)
             nc.vector.quantize_mx(
-                out=wg_q[c, a][:].bitcast(FP8X4),
-                scales=wg_s[c, a][:],
-                in_=wg_b[c, a][:].rearrange("p t m i -> p (t m i)"),
+                out=wg_q[c, a][:].bitcast(FP8X4), scales=wg_s[c, a][:], in_=wg_b[c, a][:].rearrange("p t m i -> p (t m i)")
             )
 
         def deal_wu(c, dst):
             wu_q[c] = dst
             nc.vector.tensor_copy(
-                wu_q[c][:].rearrange("p a (t m) -> p a m t", t=PACK),
-                wu_raw[c][:].rearrange("p a (m t) -> p a m t", t=PACK),
-            )
-
-        def deal_wu_scales(wu_s):
-            nc.vector.tensor_copy(
-                wu_s[:].rearrange("p (c t m) -> p c t m", c=2, t=PACK),
-                wu_sraw[:].rearrange("p (c m t) -> p c t m", c=2, t=PACK),
+                wu_q[c][:].rearrange("p a (t m) -> p a m t", t=PACK), wu_raw[c][:].rearrange("p a (m t) -> p a m t", t=PACK)
             )
 
         def up_pass(c, jt, a, sides=(0, 1)):
             if (c, jt) not in banks:
-                banks[c, jt] = [bank("up", [P, PACK, JT], jt + 4 * s if jt < 4 else None) for s in range(2)]
+                shape = [P, PACK, JT]
+                banks[c, jt] = [bank("up", shape, jt + 4 * s) if jt < 4 else next_bank("up", shape) for s in range(2)]
             for s in sides:
                 for t in range(PACK):
                     m = slice(t * P, (t + 1) * P)
@@ -195,44 +183,44 @@ def tile_list_sigm_scatb_kernel(
                         stop=(a == 1 and t == PACK - 1),
                     )
 
-        def chunk_of(jt):
-            return (jt // 2 * QUART, QUART) if jt < 4 else (HALF, HALF)
+        at_h = {0: AT_X_B + 8 * KB, QUART: AT_GATH, HALF: AT_GATH + 2 * KB}
 
         def h_slot(c, jt):
-            j0, w = chunk_of(jt)
+            j0, w = (jt // 2 * QUART, QUART) if jt < 4 else (HALF, HALF)
             if j0 not in h_b:
-                h_b[j0] = placed("h_b%d" % j0, [P, 2 * w, PACK], BF16, {0: AT_X_B + 8 * KB, QUART: AT_GATH, HALF: AT_GATH + 2 * KB}[j0])
+                h_b[j0] = placed("h_b%d" % j0, [P, 2 * w, PACK], BF16, at_h[j0])
             lo = c * w + jt * JT - j0
             return h_b[j0][:, lo : lo + JT, :]
 
-        def woven(bank):
-            return bank[:].rearrange("p t j -> p j t")
+        def woven(sums):
+            return sums[:].rearrange("p t j -> p j t")
 
         def sigmoid(c, jt, sig):
             sigs[c, jt] = sig
             nc.scalar.activation(sig[:], woven(banks[c, jt][0]), ACT.Sigmoid)
 
         def gate(c, jt):
-            nc.vector.tensor_tensor(
-                h_slot(c, jt), woven(banks[c, jt][1]), sigs[c, jt][:], MULT
-            )
+            nc.vector.tensor_tensor(h_slot(c, jt), woven(banks[c, jt][1]), sigs[c, jt][:], MULT)
 
         def ring_sig():
             return ring.tile([P, JT, PACK], F32, name="sig", tag="sig", bufs=3)
 
-        def unit(c, jt):
+        def placed_sig(c, jt, at):
+            return placed("sig%d%d" % (c, jt), [P, JT, PACK], F32, at)
+
+        def vector_unit(c, jt, sig):
             up_pass(c, jt, 0)
             up_pass(c, jt, 1)
-            sigmoid(c, jt, ring_sig())
+            sigmoid(c, jt, sig)
             gate(c, jt)
 
-        def at_both(k):
-            return AT_WG_RAW + k % 4 * 4 * KB
+        def at_both(slot):
+            return AT_WG_RAW + slot * 4 * KB
 
-        def pool_unit(k, c, jt):
+        def pool_unit(c, jt, slot):
             up_pass(c, jt, 0)
             up_pass(c, jt, 1)
-            both = placed("both%d" % k, [P, 2, JT, PACK], F32, at_both(k))
+            both = placed("both%d%d" % (c, jt), [P, 2, JT, PACK], F32, at_both(slot))
             nc.scalar.activation(both[:, 0], woven(banks[c, jt][0]), ACT.Sigmoid)
             nc.scalar.copy(both[:, 1], woven(banks[c, jt][1]))
             nc.gpsimd.tensor_tensor(h_slot(c, jt), both[:, 0], both[:, 1], MULT)
@@ -243,7 +231,7 @@ def tile_list_sigm_scatb_kernel(
             nc.vector.quantize_mx(out=h_q[j0][:].bitcast(FP8X4), scales=h_s[j0][:], in_=h_b[j0][:].rearrange("p j t -> p (j t)"))
 
         def down(n, j0, j1):
-            y = bank("y", [P, j1 - j0])
+            y = next_bank("y", [P, j1 - j0])
             w = QUART if j0 < HALF else HALF
             for lo in range(j0, j1, w):
                 for c in range(2):
@@ -259,7 +247,7 @@ def tile_list_sigm_scatb_kernel(
             return y
 
         def window(n, j0, j1):
-            return pages[n][:].indirect(offs2_t[:, j0 // 16 : j1 // 16])
+            return pages[n][:].indirect(offs2_t[:, j0 // GROUP : j1 // GROUP])
 
         def biased(n, j0, j1, at):
             y = down(n, j0, j1)
@@ -267,66 +255,57 @@ def tile_list_sigm_scatb_kernel(
             nc.scalar.activation(y_sb[:], y[:], ACT.Identity, bias=bias[:, n : n + 1])
             return y_sb
 
-        def weighted(n, j0, j1, at, at_w):
+        def put_copied(n, j0, j1, at, at_w):
             y_sb = biased(n, j0, j1, at)
             y_w = placed("yw%d_%d" % (n, j0), [P, j1 - j0], F32, at_w)
             nc.gpsimd.tensor_tensor(y_w[:], y_sb[:], wgo_t[:, j0:j1], MULT)
-            return y_w
-
-        def put(n, j0, j1, y_w):
             nc.vector.tensor_copy(window(n, j0, j1), y_w[:])
 
-        def fused(n, j0, j1, at):
+        def put_fused(n, j0, j1, at):
             y_sb = biased(n, j0, j1, at)
             nc.vector.tensor_tensor(window(n, j0, j1), y_sb[:], wgo_t[:, j0:j1], MULT)
 
-        def spread(w, dst, u0, u1, k):
-            wide = ring.tile([P, u1 - u0, 8, 16], F32, name="wide", tag="wide")
-            src = turned[:, w, :, u0:u1].rearrange("p g u -> p u g")
-            nc.scalar.copy(wide[:], src.unsqueeze(3).to_broadcast([P, u1 - u0, 8, 16]))
-            back = bank("back", [P, u1 - u0, JT], k)
-            for u in range(u1 - u0):
-                nc.tensor.transpose(back[:, u, :], wide[:, u, :, :].rearrange("p g r -> p (g r)"), ident[:])
-            nc.scalar.copy(dst[:, u0 * JT : u1 * JT], back[:].rearrange("p u j -> p (u j)"))
-
+        make_identity(nc, ident[:])
+        nc.gpsimd.memset(wu_sraw[:].bitcast(I32), 0)
+        nc.vector.memset(warm[:, 0:1], 0.0)
+        nc.scalar.activation(warm[:, 1:2], warm[:, 0:1], ACT.Sigmoid)
         load_scales(nc.gpsimd, wu_sraw, wu_scales)
         nc.gpsimd.memset(wd_s[:].bitcast(I32), 0)
-        for n in range(4):
-            nc.gpsimd.memset(pages[n][:], 0.0)
-        nc.sync.dma_start(out=rows[0:64, :], in_=wgt[0:P:16, :].rearrange("g (u j) -> g u j", j=JT))
-        nc.sync.dma_start(out=rows[64:P, :], in_=wgo[0:P:16, :].rearrange("g (u j) -> g u j", j=JT))
+        for page in pages:
+            nc.gpsimd.memset(page[:], 0.0)
+        nc.sync.dma_start(out=rows[0 : P // 2, :], in_=wgt[0:P:GROUP, :].rearrange("g (u j) -> g u j", j=JT))
+        nc.sync.dma_start(out=rows[P // 2 : P, :], in_=wgo[0:P:GROUP, :].rearrange("g (u j) -> g u j", j=JT))
         nc.sync.dma_start(offs_t[:], offs)
         for i in range(PACK):
             load_x(0, i)
         load_x(1, 0)
-        load_wg(0, 0)
+        raw00 = load_wg(0, 0, PASS, AT_WG_RAW)
         load_x(1, 1)
-        load_wg(0, 1)
+        raw01 = load_wg(1, 0, PASS, AT_WG_RAW + 8 * KB)
         load_wu(0)
         load_x(1, 2)
         load_x(1, 3)
 
-        turned = bank("turned", [P, 2, 8, 8], 7)
+        turned = bank("turned", [P, 2, P // GROUP, J // JT], BANKS - 1)
         nc.tensor.transpose(turned[:].rearrange("p w g u -> p (w g u)"), rows[:], ident[:])
-
-        spread(0, wgt_t, 0, 2, 0)
-        spread(0, wgt_t, 2, 5, 1)
-        spread(0, wgt_t, 5, 8, 2)
-        gather(0, 0, 0, 2 * JT)
-        gather(0, 0, 2 * JT, 5 * JT)
-        gather(0, 0, 5 * JT, J)
+        cuts = (0, 2, 5, 8)
+        for k in range(3):
+            spread(0, wgt_t, cuts[k], cuts[k + 1], k)
+        for k in range(3):
+            gather(0, 0, cuts[k] * JT, cuts[k + 1] * JT)
         spread(1, wgo_t, 0, 4, 3)
         spread(1, wgo_t, 4, 8, 4)
         gather(0, 1, 0, J)
-        load_wg(1, 0)
-        load_wg_half(1, 1, 1)
-        load_wg_half(1, 1, 0)
+        raw10 = load_wg(0, PASS, R, at_x(0, 0))
+        raw11_vector = load_wg(1, R - QUART, R, at_x(0, 1) + 4 * KB)
+        raw11_scalar = load_wg(1, PASS, R - QUART, at_x(0, 1))
         load_wu(1)
         load_scales(nc.sync, wd_s, wd_scales)
         nc.sync.dma_start(out=wd_q[:], in_=wd_words.rearrange("a p n i -> p a (n i)").bitcast(I32))
         nc.sync.dma_start(offs2_t[:], offs2)
         with nc.allow_non_contiguous_dma(reason="one bias value a partition"):
             nc.sync.dma_start(out=bias[:], in_=b.rearrange("(c p) -> p c", p=P))
+
         gather(0, 2, 0, J)
         gather(0, 3, 0, HALF)
         gather(0, 3, HALF, J)
@@ -334,13 +313,15 @@ def tile_list_sigm_scatb_kernel(
         weave_x(0, HALF, J, AT_X_B + 4 * KB)
         gather(1, 0, 0, J)
         quant_x(0, 0, HALF, at_x(1, 0))
-        weave_wg(0, 0, nc.scalar.copy, 0, P)
+        weave_wg(0, 0, nc.scalar.copy, raw00, 0, P)
         gather(1, 1, 0, J)
         quant_x(0, HALF, J, at_x(1, 1) + 6 * KB)
         quant_wg(0, 0, at_x(1, 1))
         wu_s = placed("wu_s", [P, R], U8, at_x(1, 1) + 4 * KB)
-        deal_wu_scales(wu_s)
-        weave_wg(0, 1, nc.scalar.copy, 0, P)
+        nc.vector.tensor_copy(
+            wu_s[:].rearrange("p (c t m) -> p c t m", c=2, t=PACK), wu_sraw[:].rearrange("p (c m t) -> p c t m", c=2, t=PACK)
+        )
+        weave_wg(0, 1, nc.scalar.copy, raw01, 0, P)
         deal_wu(0, keep.tile([P, 2, PASS], I32, name="wu_q0", align_bytes=64))
         quant_wg(0, 1, at_x(0, 2))
         for jt in range(4):
@@ -348,31 +329,33 @@ def tile_list_sigm_scatb_kernel(
         gather(1, 2, 0, J)
         gather(1, 3, 0, QUART)
         gather(1, 3, QUART, J)
+
         weave_x(1, 0, QUART, AT_X_B + 8 * KB)
         weave_x(1, QUART, HALF, AT_X_B + 10 * KB)
         quant_x(1, 0, QUART, at_x(0, 2) + 5 * KB)
         for side in range(2):
             for jt in range(2):
                 up_pass(0, jt, 1, (side,))
-        weave_wg(1, 0, nc.vector.tensor_copy, 0, P)
-        weave_wg(1, 1, nc.vector.tensor_copy, P // 2, P)
+        weave_wg(1, 0, nc.vector.tensor_copy, raw10, 0, P)
+        weave_wg(1, 1, nc.vector.tensor_copy, raw11_vector, P // 2, P)
         quant_x(1, QUART, HALF, at_x(0, 0))
         for side in range(2):
             for jt in range(2, 4):
                 up_pass(0, jt, 1, (side,))
         quant_wg(1, 0, at_x(0, 2) + 2 * KB)
-        first_sigs = [placed("sig%d" % jt, [P, JT, PACK], F32, AT_SIG + jt * 2 * KB) for jt in range(4)]
+        first_sigs = [placed_sig(0, jt, AT_SIG + jt * 2 * KB) for jt in range(4)]
         sigmoid(0, 0, first_sigs[0])
         sigmoid(0, 1, first_sigs[1])
         gate(0, 0)
-        weave_wg(1, 1, nc.scalar.copy, 0, P // 2)
+        weave_wg(1, 1, nc.scalar.copy, raw11_scalar, 0, P // 2)
         gate(0, 1)
         quant_wg(1, 1, at_x(0, 2) + 6 * KB)
         deal_wu(1, placed("wu_q1", [P, 2, PASS], I32, at_x(1, 3) + 4 * KB))
         for jt in range(2, 4):
             sigmoid(0, jt, first_sigs[jt])
             gate(0, jt)
-        weave_x_pool(1, HALF + QUART, J, AT_WU_RAW + 4 * KB)
+
+        weave_x_pool(1, HALF + QUART, J - JT, AT_WU_RAW + 4 * KB)
         for jt in range(4):
             up_pass(1, jt, 0, (0,))
         for jt in range(2):
@@ -381,12 +364,14 @@ def tile_list_sigm_scatb_kernel(
         for jt in range(2):
             up_pass(1, jt, 0, (1,))
             up_pass(1, jt, 1, (1,))
-        sigmoid(1, 0, placed("sig10", [P, JT, PACK], F32, at_x(1, 3)))
+        sigmoid(1, 0, placed_sig(1, 0, at_x(1, 3)))
         sigmoid(1, 1, ring_sig())
+        weave_x(1, J - JT, J, AT_SIG + 6 * KB)
         gate(1, 0)
         gate(1, 1)
         quant_x(1, HALF, HALF + QUART, at_x(1, 3))
-        quant_x(1, HALF + QUART, J, at_x(1, 3) + KB)
+        quant_x(1, HALF + QUART, J - JT, at_x(1, 3) + KB)
+        quant_x(1, J - JT, J, at_x(1, 3) + 3 * KB // 2)
         quant_h(0, QUART, at_x(1, 1) + 2 * KB)
         for jt in range(2, 4):
             up_pass(1, jt, 1, (0,))
@@ -394,27 +379,26 @@ def tile_list_sigm_scatb_kernel(
             up_pass(1, jt, 1, (1,))
             sigmoid(1, jt, ring_sig())
             gate(1, jt)
+
         y = down(0, 0, QUART)
         first = placed("yw0_0", [P, QUART], F32, at_x(0, 3))
         nc.vector.scalar_tensor_tensor(first[:], y[:], bias[:, 0:1], wgo_t[:, 0:QUART], ADD, MULT)
         quant_h(QUART, QUART, at_x(1, 2))
-        put(0, 0, QUART, first)
-        put(1, 0, QUART, weighted(1, 0, QUART, at_x(0, 3) + KB, AT_GATH))
-        pool_unit(0, 0, 4)
-        unit(1, 4)
-        put(2, 0, HALF, weighted(2, 0, HALF, at_x(0, 3) + 4 * KB, at_x(0, 3) + 6 * KB))
-        put(0, QUART, HALF, weighted(0, QUART, HALF, at_x(1, 2) + 4 * KB, at_x(1, 2) + 5 * KB))
-        put(1, QUART, HALF, weighted(1, QUART, HALF, at_x(1, 2) + 6 * KB, at_x(1, 2) + 7 * KB))
+        nc.vector.tensor_copy(window(0, 0, QUART), first[:])
+        put_copied(1, 0, QUART, at_x(0, 3) + KB, AT_GATH)
+        pool_unit(0, 4, 0)
+        vector_unit(1, 4, ring_sig())
+        put_copied(2, 0, HALF, at_x(0, 3) + 4 * KB, at_x(0, 3) + 6 * KB)
+        put_copied(0, QUART, HALF, at_x(1, 2) + 4 * KB, at_x(1, 2) + 5 * KB)
+        put_copied(1, QUART, HALF, at_x(1, 2) + 6 * KB, at_x(1, 2) + 7 * KB)
         for jt in range(5, 7):
             for c in range(2):
-                pool_unit(2 * jt + c - 8, c, jt)
+                pool_unit(c, jt, (2 * jt + c) % 4)
         for c in range(2):
-            up_pass(c, 7, 0)
-            up_pass(c, 7, 1)
-            sigmoid(c, 7, placed("sig_last%d" % c, [P, JT, PACK], F32, at_both(6) + (1 - c) * 2 * KB))
-            gate(c, 7)
+            vector_unit(c, 7, placed_sig(c, 7, at_both(2) + (1 - c) * 2 * KB))
         quant_h(HALF, HALF, at_x(1, 0) + 4 * KB)
-        fused(3, 0, HALF, at_both(6) - KB)
-        for n in range(4):
-            fused(n, HALF, J, at_x(0, 1) + n * 2 * KB)
+
+        put_fused(3, 0, HALF, at_both(2) - KB)
+        for n in range(N // P):
+            put_fused(n, HALF, J, at_x(0, 1) + n * 2 * KB)
             nc.sync.dma_start(out=out[n * P : (n + 1) * P, :], in_=pages[n][:])

@@ -109,8 +109,7 @@ def tile_list_sigm_scatb_kernel(
             for q in range(4):
                 queue.dma_start(out=dst[32 * q : 32 * q + 8, :].bitcast(I32), in_=src[:, 4 * q : 4 * q + 4, :].bitcast(I32))
 
-        def spread(w, dst, u0, u1, k):
-            wide = ring.tile([P, u1 - u0, P // GROUP, GROUP], F32, name="wide", tag="wide")
+        def spread(w, dst, u0, u1, k, wide):
             src = turned[:, w, :, u0:u1].rearrange("p g u -> p u g")
             nc.scalar.copy(wide[:], src.unsqueeze(3).to_broadcast([P, u1 - u0, P // GROUP, GROUP]))
             back = bank("back", [P, u1 - u0, JT], k)
@@ -163,10 +162,13 @@ def tile_list_sigm_scatb_kernel(
             )
 
         def up_pass(c, jt, a, sides=(0, 1)):
-            if (c, jt) not in banks:
-                shape = [P, PACK, JT]
-                banks[c, jt] = [bank("up", shape, jt + 4 * s) if jt < 4 else next_bank("up", shape) for s in range(2)]
+            shape = [P, PACK, JT]
+            if jt >= 4 and (c, jt, 0) not in banks:
+                for s in range(2):
+                    banks[c, jt, s] = next_bank("up", shape)
             for s in sides:
+                if (c, jt, s) not in banks:
+                    banks[c, jt, s] = bank("up", shape, jt + 4 * s)
                 for t in range(PACK):
                     m = slice(t * P, (t + 1) * P)
                     if s == 0:
@@ -174,7 +176,7 @@ def tile_list_sigm_scatb_kernel(
                     else:
                         w, ws = wu_q[c][:, a, m], wu_s[4 * a : P, c * PASS + t * P : c * PASS + (t + 1) * P]
                     nc.tensor.matmul_mx(
-                        banks[c, jt][s][:, t, :],
+                        banks[c, jt, s][:, t, :],
                         lhsT=w.bitcast(FP8X4),
                         lhsT_scale=ws,
                         rhs=x_q[a, jt].bitcast(FP8X4),
@@ -197,10 +199,10 @@ def tile_list_sigm_scatb_kernel(
 
         def sigmoid(c, jt, sig):
             sigs[c, jt] = sig
-            nc.scalar.activation(sig[:], woven(banks[c, jt][0]), ACT.Sigmoid)
+            nc.scalar.activation(sig[:], woven(banks[c, jt, 0]), ACT.Sigmoid)
 
         def gate(c, jt):
-            nc.vector.tensor_tensor(h_slot(c, jt), woven(banks[c, jt][1]), sigs[c, jt][:], MULT)
+            nc.vector.tensor_tensor(h_slot(c, jt), woven(banks[c, jt, 1]), sigs[c, jt][:], MULT)
 
         def ring_sig():
             return ring.tile([P, JT, PACK], F32, name="sig", tag="sig", bufs=3)
@@ -221,8 +223,8 @@ def tile_list_sigm_scatb_kernel(
             up_pass(c, jt, 0)
             up_pass(c, jt, 1)
             both = placed("both%d%d" % (c, jt), [P, 2, JT, PACK], F32, at_both(slot))
-            nc.scalar.activation(both[:, 0], woven(banks[c, jt][0]), ACT.Sigmoid)
-            nc.scalar.copy(both[:, 1], woven(banks[c, jt][1]))
+            nc.scalar.activation(both[:, 0], woven(banks[c, jt, 0]), ACT.Sigmoid)
+            nc.scalar.copy(both[:, 1], woven(banks[c, jt, 1]))
             nc.gpsimd.tensor_tensor(h_slot(c, jt), both[:, 0], both[:, 1], MULT)
 
         def quant_h(j0, w, at):
@@ -290,11 +292,10 @@ def tile_list_sigm_scatb_kernel(
         nc.tensor.transpose(turned[:].rearrange("p w g u -> p (w g u)"), rows[:], ident[:])
         cuts = (0, 2, 5, 8)
         for k in range(3):
-            spread(0, wgt_t, cuts[k], cuts[k + 1], k)
+            wide = ring.tile([P, cuts[k + 1] - cuts[k], P // GROUP, GROUP], F32, name="wide", tag="wide")
+            spread(0, wgt_t, cuts[k], cuts[k + 1], k, wide)
         for k in range(3):
             gather(0, 0, cuts[k] * JT, cuts[k + 1] * JT)
-        spread(1, wgo_t, 0, 4, 3)
-        spread(1, wgo_t, 4, 8, 4)
         gather(0, 1, 0, J)
         raw10 = load_wg(0, PASS, R, at_x(0, 0))
         raw11_vector = load_wg(1, R - QUART, R, at_x(0, 1) + 4 * KB)
@@ -324,8 +325,17 @@ def tile_list_sigm_scatb_kernel(
         weave_wg(0, 1, nc.scalar.copy, raw01, 0, P)
         deal_wu(0, keep.tile([P, 2, PASS], I32, name="wu_q0", align_bytes=64))
         quant_wg(0, 1, at_x(0, 2))
-        for jt in range(4):
-            up_pass(0, jt, 0)
+        wide = placed("wide_o", [P, BANKS, P // GROUP, GROUP], F32, AT_WG_B)
+        for u in range(0, BANKS, 4):
+            src = turned[:, 1, :, u : u + 4].rearrange("p g u -> p u g")
+            nc.scalar.copy(wide[:, u : u + 4], src.unsqueeze(3).to_broadcast([P, 4, P // GROUP, GROUP]))
+        backs = [bank("back_o", [P, JT], u // 2 + 4 * (u % 2)) for u in range(BANKS)]
+        for u in range(BANKS):
+            nc.tensor.transpose(backs[u][:], wide[:, u].rearrange("p g r -> p (g r)"), ident[:])
+        for u in range(BANKS):
+            nc.scalar.copy(wgo_t[:, u * JT : (u + 1) * JT], backs[u][:])
+        for u in range(BANKS):
+            up_pass(0, u // 2, 0, (u % 2,))
         gather(1, 2, 0, J)
         gather(1, 3, 0, QUART)
         gather(1, 3, QUART, J)

@@ -9,6 +9,7 @@ FLOPS = 2 * J * (2 * K * R + R * N)
 F32 = mybir.dt.float32
 BF16 = mybir.dt.bfloat16
 I32 = mybir.dt.int32
+U32 = mybir.dt.uint32
 U16 = mybir.dt.uint16
 U8 = mybir.dt.uint8
 FP8X4 = mybir.dt.float8_e4m3fn_x4
@@ -80,7 +81,6 @@ def tile_list_sigm_scatb_kernel(
         wg_rows = wg.rearrange("(a p i) r -> a p i r", a=2, i=PACK)
         wu_rows = wu_words.rearrange("a p r i -> p a (r i)")
 
-        wu_raw = {}
         x_b = {}
         x_q = {}
         x_s = {}
@@ -101,9 +101,10 @@ def tile_list_sigm_scatb_kernel(
             nc.sync.dma_start(out=raw[:], in_=wg_rows[a][:, :, r0:r1])
             return raw
 
-        def load_wu(c):
-            wu_raw[c] = placed("wu_raw%d" % c, [P, 2, PASS], I32, AT_WU_RAW + c * 4 * KB)
-            nc.sync.dma_start(out=wu_raw[c][:], in_=wu_rows[:, :, c * PASS * PACK : (c + 1) * PASS * PACK].bitcast(I32))
+        def load_wu(c, a0, a1):
+            raw = placed("wu_raw%d%d" % (c, a0), [P, a1 - a0, PASS], I32, AT_WU_RAW + (2 * c + a0) * 2 * KB)
+            nc.sync.dma_start(out=raw[:], in_=wu_rows[:, a0:a1, c * PASS * PACK : (c + 1) * PASS * PACK].bitcast(I32))
+            return raw
 
         def load_scales(queue, dst, src):
             for q in range(4):
@@ -155,10 +156,10 @@ def tile_list_sigm_scatb_kernel(
                 out=wg_q[c, a][:].bitcast(FP8X4), scales=wg_s[c, a][:], in_=wg_b[c, a][:].rearrange("p t m i -> p (t m i)")
             )
 
-        def deal_wu(c, dst):
-            wu_q[c] = dst
-            nc.vector.tensor_copy(
-                wu_q[c][:].rearrange("p a (t m) -> p a m t", t=PACK), wu_raw[c][:].rearrange("p a (m t) -> p a m t", t=PACK)
+        def deal_wu(copy, dst, raw):
+            copy(
+                dst.bitcast(U32).rearrange("p a (t m) -> p a m t", t=PACK),
+                raw[:].bitcast(U32).rearrange("p a (m t) -> p a m t", t=PACK),
             )
 
         def up_pass(c, jt, a, sides=(0, 1)):
@@ -284,9 +285,10 @@ def tile_list_sigm_scatb_kernel(
         raw00 = load_wg(0, 0, PASS, AT_WG_RAW)
         load_x(1, 1)
         raw01 = load_wg(1, 0, PASS, AT_WG_RAW + 8 * KB)
-        load_wu(0)
+        wu_raw00 = load_wu(0, 0, 1)
         load_x(1, 2)
         load_x(1, 3)
+        wu_raw01 = load_wu(0, 1, 2)
 
         turned = bank("turned", [P, 2, P // GROUP, J // JT], BANKS - 1)
         nc.tensor.transpose(turned[:].rearrange("p w g u -> p (w g u)"), rows[:], ident[:])
@@ -300,7 +302,7 @@ def tile_list_sigm_scatb_kernel(
         raw10 = load_wg(0, PASS, R, at_x(0, 0))
         raw11_vector = load_wg(1, R - QUART, R, at_x(0, 1) + 4 * KB)
         raw11_scalar = load_wg(1, PASS, R - QUART, at_x(0, 1))
-        load_wu(1)
+        wu_raw1 = load_wu(1, 0, 2)
         load_scales(nc.sync, wd_s, wd_scales)
         nc.sync.dma_start(out=wd_q[:], in_=wd_words.rearrange("a p n i -> p a (n i)").bitcast(I32))
         nc.sync.dma_start(offs2_t[:], offs2)
@@ -323,7 +325,8 @@ def tile_list_sigm_scatb_kernel(
             wu_s[:].rearrange("p (c t m) -> p c t m", c=2, t=PACK), wu_sraw[:].rearrange("p (c m t) -> p c t m", c=2, t=PACK)
         )
         weave_wg(0, 1, nc.scalar.copy, raw01, 0, P)
-        deal_wu(0, keep.tile([P, 2, PASS], I32, name="wu_q0", align_bytes=64))
+        wu_q[0] = keep.tile([P, 2, PASS], I32, name="wu_q0", align_bytes=64)
+        deal_wu(nc.scalar.copy, wu_q[0][:, 0:1, :], wu_raw00)
         quant_wg(0, 1, at_x(0, 2))
         wide = placed("wide_o", [P, BANKS, P // GROUP, GROUP], F32, AT_WG_B)
         for u in range(0, BANKS, 4):
@@ -340,6 +343,7 @@ def tile_list_sigm_scatb_kernel(
         gather(1, 3, 0, QUART)
         gather(1, 3, QUART, J)
 
+        deal_wu(nc.scalar.copy, wu_q[0][:, 1:2, :], wu_raw01)
         weave_x(1, 0, QUART, AT_X_B + 8 * KB)
         weave_x(1, QUART, HALF, AT_X_B + 10 * KB)
         quant_x(1, 0, QUART, at_x(0, 2) + 5 * KB)
@@ -360,7 +364,8 @@ def tile_list_sigm_scatb_kernel(
         weave_wg(1, 1, nc.scalar.copy, raw11_scalar, 0, P // 2)
         gate(0, 1)
         quant_wg(1, 1, at_x(0, 2) + 6 * KB)
-        deal_wu(1, placed("wu_q1", [P, 2, PASS], I32, at_x(1, 3) + 4 * KB))
+        wu_q[1] = placed("wu_q1", [P, 2, PASS], I32, at_x(1, 3) + 4 * KB)
+        deal_wu(nc.vector.tensor_copy, wu_q[1][:], wu_raw1)
         for jt in range(2, 4):
             sigmoid(0, jt, first_sigs[jt])
             gate(0, jt)

@@ -186,14 +186,14 @@ def tile_list_sigm_scatb_kernel(
                         stop=(a == 1 and t == PACK - 1),
                     )
 
-        at_h = {0: AT_X_B + 8 * KB, QUART: AT_GATH, HALF: AT_GATH + 2 * KB}
+        at_h = {0: AT_X_B + 8 * KB, QUART: AT_GATH, HALF: AT_GATH + 2 * KB, HALF + QUART: AT_GATH + 6 * KB}
 
-        def h_slot(c, jt):
-            j0, w = (jt // 2 * QUART, QUART) if jt < 4 else (HALF, HALF)
+        def h_slot(c, jt, count=1):
+            j0 = jt // 2 * QUART
             if j0 not in h_b:
-                h_b[j0] = placed("h_b%d" % j0, [P, 2 * w, PACK], BF16, at_h[j0])
-            lo = c * w + jt * JT - j0
-            return h_b[j0][:, lo : lo + JT, :]
+                h_b[j0] = placed("h_b%d" % j0, [P, 2 * QUART, PACK], BF16, at_h[j0])
+            lo = c * QUART + jt * JT - j0
+            return h_b[j0][:, lo : lo + count * JT, :]
 
         def woven(sums):
             return sums[:].rearrange("p t j -> p j t")
@@ -212,61 +212,87 @@ def tile_list_sigm_scatb_kernel(
             return placed("sig%d%d" % (c, jt), [P, JT, PACK], F32, at)
 
         def vector_unit(c, jt, sig):
-            up_pass(c, jt, 0)
-            up_pass(c, jt, 1)
+            for s in range(2):
+                for a in range(2):
+                    up_pass(c, jt, a, (s,))
             sigmoid(c, jt, sig)
             gate(c, jt)
 
-        def at_both(slot):
-            return AT_WG_RAW + slot * 4 * KB
+        def handed_over(c, jt0, count, at):
+            both = placed("both%d%d" % (c, jt0), [P, 2, count * JT, PACK], F32, at)
+            for u in range(count):
+                for s in range(2):
+                    for a in range(2):
+                        up_pass(c, jt0 + u, a, (s,))
+                nc.scalar.activation(both[:, 0, u * JT : (u + 1) * JT], woven(banks[c, jt0 + u, 0]), ACT.Sigmoid)
+                nc.scalar.copy(both[:, 1, u * JT : (u + 1) * JT], woven(banks[c, jt0 + u, 1]))
+            return both
 
-        def pool_unit(c, jt, slot):
-            up_pass(c, jt, 0)
-            up_pass(c, jt, 1)
-            both = placed("both%d%d" % (c, jt), [P, 2, JT, PACK], F32, at_both(slot))
-            nc.scalar.activation(both[:, 0], woven(banks[c, jt, 0]), ACT.Sigmoid)
-            nc.scalar.copy(both[:, 1], woven(banks[c, jt, 1]))
-            nc.gpsimd.tensor_tensor(h_slot(c, jt), both[:, 0], both[:, 1], MULT)
+        def pool_gate(c, jt0, count, both):
+            nc.gpsimd.tensor_tensor(h_slot(c, jt0, count), both[:, 0], both[:, 1], MULT)
 
-        def quant_h(j0, w, at):
-            h_q[j0] = placed("h_q%d" % j0, [P, 2 * w], I32, at)
-            h_s[j0] = keep.tile([P, 2 * w], U8, name="h_s%d" % j0, align_bytes=64)
+        def quant_h(j0, at):
+            h_q[j0] = placed("h_q%d" % j0, [P, 2 * QUART], I32, at)
+            h_s[j0] = keep.tile([P, 2 * QUART], U8, name="h_s%d" % j0, align_bytes=64)
             nc.vector.quantize_mx(out=h_q[j0][:].bitcast(FP8X4), scales=h_s[j0][:], in_=h_b[j0][:].rearrange("p j t -> p (j t)"))
 
-        def down(n, j0, j1):
-            y = next_bank("y", [P, j1 - j0])
-            w = QUART if j0 < HALF else HALF
-            for lo in range(j0, j1, w):
+        def down(pieces, k=None):
+            shape = [P, sum(j1 - j0 for n, j0, j1 in pieces)]
+            y = next_bank("y", shape) if k is None else bank("y", shape, k)
+            parts = []
+            for n, j0, j1 in pieces:
+                at = sum(part.shape[1] for part in parts)
+                parts.append(y[:, at : at + j1 - j0])
+                q0 = j0 // QUART * QUART
                 for c in range(2):
+                    cols = slice(c * QUART + j0 - q0, c * QUART + j1 - q0)
                     nc.tensor.matmul_mx(
-                        y[:, lo - j0 : lo - j0 + w],
+                        parts[-1],
                         lhsT=wd_q[:, c, n * P : (n + 1) * P].bitcast(FP8X4),
                         lhsT_scale=wd_s[4 * c : P, n * P : (n + 1) * P],
-                        rhs=h_q[lo][:, c * w : (c + 1) * w].bitcast(FP8X4),
-                        rhs_scale=h_s[lo][:, c * w : (c + 1) * w],
+                        rhs=h_q[q0][:, cols].bitcast(FP8X4),
+                        rhs_scale=h_s[q0][:, cols],
                         start=(c == 0),
                         stop=(c == 1),
                     )
-            return y
+            return y, parts
+
+        def quarters(pieces):
+            return down([(n, j0, j0 + QUART) for n, j0 in pieces])[1]
 
         def window(n, j0, j1):
             return pages[n][:].indirect(offs2_t[:, j0 // GROUP : j1 // GROUP])
 
-        def biased(n, j0, j1, at):
-            y = down(n, j0, j1)
-            y_sb = placed("y%d_%d" % (n, j0), [P, j1 - j0], F32, at)
-            nc.scalar.activation(y_sb[:], y[:], ACT.Identity, bias=bias[:, n : n + 1])
+        def add_bias(dst, y, n):
+            nc.scalar.activation(dst, y, ACT.Identity, bias=bias[:, n : n + 1])
+
+        def biased(ns, j0, ys, at):
+            y_sb = placed("y%d_%d" % (ns[0], j0), [P, len(ns), QUART], F32, at)
+            for u, n in enumerate(ns):
+                add_bias(y_sb[:, u, :], ys[u], n)
             return y_sb
 
-        def put_copied(n, j0, j1, at, at_w):
-            y_sb = biased(n, j0, j1, at)
-            y_w = placed("yw%d_%d" % (n, j0), [P, j1 - j0], F32, at_w)
-            nc.gpsimd.tensor_tensor(y_w[:], y_sb[:], wgo_t[:, j0:j1], MULT)
-            nc.vector.tensor_copy(window(n, j0, j1), y_w[:])
+        def biased_run(n, j0, j1, at, k=None):
+            cut = (j0 // QUART + 1) * QUART
+            y_sb = placed("y%d_%d" % (n, j0), [P, j1 - j0], F32, at)
+            add_bias(y_sb[:], down([(n, j0, cut), (n, cut, j1)], k)[0][:], n)
+            return y_sb[:]
 
-        def put_fused(n, j0, j1, at):
-            y_sb = biased(n, j0, j1, at)
-            nc.vector.tensor_tensor(window(n, j0, j1), y_sb[:], wgo_t[:, j0:j1], MULT)
+        def pool_weighted(n, j0, j1, y_sb, at):
+            y_w = placed("yw%d_%d" % (n, j0), [P, j1 - j0], F32, at)
+            nc.gpsimd.tensor_tensor(y_w[:], y_sb, wgo_t[:, j0:j1], MULT)
+            return y_w[:]
+
+        def weighted(n, j0, y, at):
+            y_w = placed("yw%d_%d" % (n, j0), [P, QUART], F32, at)
+            nc.vector.scalar_tensor_tensor(y_w[:], y, bias[:, n : n + 1], wgo_t[:, j0 : j0 + QUART], ADD, MULT)
+            return y_w[:]
+
+        def put_copied(n, j0, j1, y_w):
+            nc.vector.tensor_copy(window(n, j0, j1), y_w)
+
+        def put_fused(n, j0, j1, y_sb):
+            nc.vector.tensor_tensor(window(n, j0, j1), y_sb, wgo_t[:, j0:j1], MULT)
 
         make_identity(nc, ident[:])
         nc.gpsimd.memset(wu_sraw[:].bitcast(I32), 0)
@@ -387,7 +413,7 @@ def tile_list_sigm_scatb_kernel(
         quant_x(1, HALF, HALF + QUART, at_x(1, 3))
         quant_x(1, HALF + QUART, J - JT, at_x(1, 3) + KB)
         quant_x(1, J - JT, J, at_x(1, 3) + 3 * KB // 2)
-        quant_h(0, QUART, at_x(1, 1) + 2 * KB)
+        quant_h(0, at_x(1, 1) + 2 * KB)
         for jt in range(2, 4):
             up_pass(1, jt, 1, (0,))
             up_pass(1, jt, 0, (1,))
@@ -395,25 +421,30 @@ def tile_list_sigm_scatb_kernel(
             sigmoid(1, jt, ring_sig())
             gate(1, jt)
 
-        y = down(0, 0, QUART)
-        first = placed("yw0_0", [P, QUART], F32, at_x(0, 3))
-        nc.vector.scalar_tensor_tensor(first[:], y[:], bias[:, 0:1], wgo_t[:, 0:QUART], ADD, MULT)
-        quant_h(QUART, QUART, at_x(1, 2))
-        nc.vector.tensor_copy(window(0, 0, QUART), first[:])
-        put_copied(1, 0, QUART, at_x(0, 3) + KB, AT_GATH)
-        pool_unit(0, 4, 0)
-        vector_unit(1, 4, ring_sig())
-        put_copied(2, 0, HALF, at_x(0, 3) + 4 * KB, at_x(0, 3) + 6 * KB)
-        put_copied(0, QUART, HALF, at_x(1, 2) + 4 * KB, at_x(1, 2) + 5 * KB)
-        put_copied(1, QUART, HALF, at_x(1, 2) + 6 * KB, at_x(1, 2) + 7 * KB)
-        for jt in range(5, 7):
-            for c in range(2):
-                pool_unit(c, jt, (2 * jt + c) % 4)
-        for c in range(2):
-            vector_unit(c, 7, placed_sig(c, 7, at_both(2) + (1 - c) * 2 * KB))
-        quant_h(HALF, HALF, at_x(1, 0) + 4 * KB)
+        ja, jb, jc, jd = range(0, J, QUART)
+        at_y = at_x(0, 3)
+        first = weighted(0, ja, quarters([(0, ja)])[0], at_y)
+        y_a = biased([1], ja, quarters([(1, ja)]), at_y + KB)
+        quant_h(jb, at_x(1, 2))
+        put_copied(0, ja, jb, first)
+        y_b = biased([1], jb, quarters([(1, jb)]), at_y + 2 * KB)
+        yw = placed("yw1", [P, HALF], F32, AT_GATH)
+        for j0, y_sb in ((ja, y_a), (jb, y_b)):
+            nc.gpsimd.tensor_tensor(yw[:, j0 : j0 + QUART], y_sb[:, 0, :], wgo_t[:, j0 : j0 + QUART], MULT)
+        vector_unit(0, 4, ring_sig())
+        put_copied(1, ja, jc, yw[:])
+        pool_gate(0, 5, 1, handed_over(0, 5, 1, AT_WG_RAW))
+        put_copied(2, ja, jc, pool_weighted(2, ja, jc, biased_run(2, ja, jc, at_y + 3 * KB), at_x(1, 2) + 2 * KB))
+        pool_gate(1, 4, 2, handed_over(1, 4, 2, AT_WG_RAW + 4 * KB))
+        put_copied(3, ja, jc, pool_weighted(3, ja, jc, biased_run(3, ja, jc, at_y + 5 * KB), at_x(1, 2) + 4 * KB))
+        pool_gate(0, 6, 2, handed_over(0, 6, 2, at_x(0, 0)))
+        pool_gate(1, 6, 1, handed_over(1, 6, 1, AT_WG_RAW + 12 * KB))
+        vector_unit(1, 7, ring_sig())
+        y_held = biased([0], jb, quarters([(0, jb)]), AT_WG_RAW + 12 * KB)
+        quant_h(jc, AT_WG_RAW + 13 * KB)
+        quant_h(jd, at_x(1, 0) + 6 * KB)
 
-        put_fused(3, 0, HALF, at_both(2) - KB)
-        for n in range(N // P):
-            put_fused(n, HALF, J, at_x(0, 1) + n * 2 * KB)
+        put_fused(0, jb, jc, y_held[:, 0, :])
+        for n in (1, 0, 2, 3):
+            put_fused(n, jc, J, biased_run(n, jc, J, at_x(0, 1) + n * 2 * KB, 0))
             nc.sync.dma_start(out=out[n * P : (n + 1) * P, :], in_=pages[n][:])

@@ -186,13 +186,16 @@ def tile_list_sigm_scatb_kernel(
                         stop=(a == 1 and t == PACK - 1),
                     )
 
-        at_h = {0: AT_X_B + 8 * KB, QUART: AT_GATH, HALF: AT_GATH + 2 * KB, HALF + QUART: AT_GATH + 6 * KB}
+        at_h = {0: AT_X_B + 8 * KB, QUART: AT_GATH, HALF: AT_GATH + 2 * KB}
+
+        def chunk(j):
+            return (j // QUART * QUART, QUART) if j < HALF else (HALF, HALF)
 
         def h_slot(c, jt, count=1):
-            j0 = jt // 2 * QUART
+            j0, w = chunk(jt * JT)
             if j0 not in h_b:
-                h_b[j0] = placed("h_b%d" % j0, [P, 2 * QUART, PACK], BF16, at_h[j0])
-            lo = c * QUART + jt * JT - j0
+                h_b[j0] = placed("h_b%d" % j0, [P, 2 * w, PACK], BF16, at_h[j0])
+            lo = c * w + jt * JT - j0
             return h_b[j0][:, lo : lo + count * JT, :]
 
         def woven(sums):
@@ -211,41 +214,38 @@ def tile_list_sigm_scatb_kernel(
         def placed_sig(c, jt, at):
             return placed("sig%d%d" % (c, jt), [P, JT, PACK], F32, at)
 
-        def vector_unit(c, jt, sig):
+        def unit(c, jt):
             for s in range(2):
                 for a in range(2):
                     up_pass(c, jt, a, (s,))
-            sigmoid(c, jt, sig)
-            gate(c, jt)
 
-        def handed_over(c, jt0, count, at):
-            both = placed("both%d%d" % (c, jt0), [P, 2, count * JT, PACK], F32, at)
-            for u in range(count):
-                for s in range(2):
-                    for a in range(2):
-                        up_pass(c, jt0 + u, a, (s,))
-                nc.scalar.activation(both[:, 0, u * JT : (u + 1) * JT], woven(banks[c, jt0 + u, 0]), ACT.Sigmoid)
-                nc.scalar.copy(both[:, 1, u * JT : (u + 1) * JT], woven(banks[c, jt0 + u, 1]))
-            return both
+        def pair_tile(c, jt0, at):
+            return placed("both%d%d" % (c, jt0), [P, 2, 2, JT, PACK], F32, at)
 
-        def pool_gate(c, jt0, count, both):
-            nc.gpsimd.tensor_tensor(h_slot(c, jt0, count), both[:, 0], both[:, 1], MULT)
+        def hand_over(c, jt, both):
+            unit(c, jt)
+            nc.scalar.activation(both[:, 0, jt % 2], woven(banks[c, jt, 0]), ACT.Sigmoid)
+            nc.scalar.copy(both[:, 1, jt % 2], woven(banks[c, jt, 1]))
+
+        def pool_gate(c, jt0, both):
+            pair = "p u j t -> p (u j) t"
+            nc.gpsimd.tensor_tensor(h_slot(c, jt0, 2), both[:, 0].rearrange(pair), both[:, 1].rearrange(pair), MULT)
 
         def quant_h(j0, at):
-            h_q[j0] = placed("h_q%d" % j0, [P, 2 * QUART], I32, at)
-            h_s[j0] = keep.tile([P, 2 * QUART], U8, name="h_s%d" % j0, align_bytes=64)
+            w = chunk(j0)[1]
+            h_q[j0] = placed("h_q%d" % j0, [P, 2 * w], I32, at)
+            h_s[j0] = keep.tile([P, 2 * w], U8, name="h_s%d" % j0, align_bytes=64)
             nc.vector.quantize_mx(out=h_q[j0][:].bitcast(FP8X4), scales=h_s[j0][:], in_=h_b[j0][:].rearrange("p j t -> p (j t)"))
 
-        def down(pieces, k=None):
-            shape = [P, sum(j1 - j0 for n, j0, j1 in pieces)]
-            y = next_bank("y", shape) if k is None else bank("y", shape, k)
+        def down(pieces):
+            y = next_bank("y", [P, sum(j1 - j0 for n, j0, j1 in pieces)])
             parts = []
             for n, j0, j1 in pieces:
                 at = sum(part.shape[1] for part in parts)
                 parts.append(y[:, at : at + j1 - j0])
-                q0 = j0 // QUART * QUART
+                q0, w = chunk(j0)
                 for c in range(2):
-                    cols = slice(c * QUART + j0 - q0, c * QUART + j1 - q0)
+                    cols = slice(c * w + j0 - q0, c * w + j1 - q0)
                     nc.tensor.matmul_mx(
                         parts[-1],
                         lhsT=wd_q[:, c, n * P : (n + 1) * P].bitcast(FP8X4),
@@ -272,24 +272,19 @@ def tile_list_sigm_scatb_kernel(
                 add_bias(y_sb[:, u, :], ys[u], n)
             return y_sb
 
-        def biased_run(n, j0, j1, at, k=None):
-            cut = (j0 // QUART + 1) * QUART
-            y_sb = placed("y%d_%d" % (n, j0), [P, j1 - j0], F32, at)
-            add_bias(y_sb[:], down([(n, j0, cut), (n, cut, j1)], k)[0][:], n)
-            return y_sb[:]
-
-        def pool_weighted(n, j0, j1, y_sb, at):
-            y_w = placed("yw%d_%d" % (n, j0), [P, j1 - j0], F32, at)
-            nc.gpsimd.tensor_tensor(y_w[:], y_sb, wgo_t[:, j0:j1], MULT)
-            return y_w[:]
+        def pool_weighted(ns, j0, y_sb, at):
+            shape = [P, len(ns), QUART]
+            y_w = placed("yw%d_%d" % (ns[0], j0), shape, F32, at)
+            nc.gpsimd.tensor_tensor(y_w[:], y_sb[:], wgo_t[:, j0 : j0 + QUART].unsqueeze(1).to_broadcast(shape), MULT)
+            return [y_w[:, u, :] for u in range(len(ns))]
 
         def weighted(n, j0, y, at):
             y_w = placed("yw%d_%d" % (n, j0), [P, QUART], F32, at)
             nc.vector.scalar_tensor_tensor(y_w[:], y, bias[:, n : n + 1], wgo_t[:, j0 : j0 + QUART], ADD, MULT)
             return y_w[:]
 
-        def put_copied(n, j0, j1, y_w):
-            nc.vector.tensor_copy(window(n, j0, j1), y_w)
+        def put_copied(n, j0, y_w):
+            nc.vector.tensor_copy(window(n, j0, j0 + QUART), y_w)
 
         def put_fused(n, j0, j1, y_sb):
             nc.vector.tensor_tensor(window(n, j0, j1), y_sb, wgo_t[:, j0:j1], MULT)
@@ -424,27 +419,36 @@ def tile_list_sigm_scatb_kernel(
         ja, jb, jc, jd = range(0, J, QUART)
         at_y = at_x(0, 3)
         first = weighted(0, ja, quarters([(0, ja)])[0], at_y)
-        y_a = biased([1], ja, quarters([(1, ja)]), at_y + KB)
+        y = quarters([(1, ja), (2, ja)]) + quarters([(3, ja)])
+        y_a = [biased([1, 2], ja, y[0:2], at_y + KB), biased([3], ja, y[2:3], at_y + 3 * KB)]
         quant_h(jb, at_x(1, 2))
-        put_copied(0, ja, jb, first)
-        y_b = biased([1], jb, quarters([(1, jb)]), at_y + 2 * KB)
-        yw = placed("yw1", [P, HALF], F32, AT_GATH)
-        for j0, y_sb in ((ja, y_a), (jb, y_b)):
-            nc.gpsimd.tensor_tensor(yw[:, j0 : j0 + QUART], y_sb[:, 0, :], wgo_t[:, j0 : j0 + QUART], MULT)
-        vector_unit(0, 4, ring_sig())
-        put_copied(1, ja, jc, yw[:])
-        pool_gate(0, 5, 1, handed_over(0, 5, 1, AT_WG_RAW))
-        put_copied(2, ja, jc, pool_weighted(2, ja, jc, biased_run(2, ja, jc, at_y + 3 * KB), at_x(1, 2) + 2 * KB))
-        pool_gate(1, 4, 2, handed_over(1, 4, 2, AT_WG_RAW + 4 * KB))
-        put_copied(3, ja, jc, pool_weighted(3, ja, jc, biased_run(3, ja, jc, at_y + 5 * KB), at_x(1, 2) + 4 * KB))
-        pool_gate(0, 6, 2, handed_over(0, 6, 2, at_x(0, 0)))
-        pool_gate(1, 6, 1, handed_over(1, 6, 1, AT_WG_RAW + 12 * KB))
-        vector_unit(1, 7, ring_sig())
-        y_held = biased([0], jb, quarters([(0, jb)]), AT_WG_RAW + 12 * KB)
-        quant_h(jc, AT_WG_RAW + 13 * KB)
-        quant_h(jd, at_x(1, 0) + 6 * KB)
+        put_copied(0, ja, first)
+        yw_a = pool_weighted([1, 2], ja, y_a[0], AT_GATH)
+        yw_a += pool_weighted([3], ja, y_a[1], AT_GATH + 10 * KB)
+        both = [pair_tile(0, 4, AT_WG_RAW), pair_tile(1, 4, AT_WG_RAW + 8 * KB), pair_tile(0, 6, at_x(0, 0))]
+        hand_over(0, 4, both[0])
+        y_b = biased([1, 2, 3], jb, quarters([(1, jb), (2, jb)]) + quarters([(3, jb)]), at_y + 4 * KB)
+        yw_b = pool_weighted([1, 2, 3], jb, y_b, at_x(1, 2) + 2 * KB)
+        hand_over(0, 5, both[0])
+        pool_gate(0, 4, both[0])
+        for c, jt0, pair in ((1, 4, both[1]), (0, 6, both[2])):
+            hand_over(c, jt0, pair)
+            hand_over(c, jt0 + 1, pair)
+            pool_gate(c, jt0, pair)
+        for j0, yw in ((ja, yw_a), (jb, yw_b)):
+            for u in range(3):
+                put_copied(1 + u, j0, yw[u])
+        for jt in range(6, 8):
+            unit(1, jt)
+            sigmoid(1, jt, placed_sig(1, jt, at_x(0, 1) + (7 - jt) * 2 * KB))
+            gate(1, jt)
+        y_held = biased([0], jb, quarters([(0, jb)]), at_x(0, 1) - KB // 2)
+        quant_h(jc, at_x(1, 0) + 4 * KB)
 
         put_fused(0, jb, jc, y_held[:, 0, :])
-        for n in (1, 0, 2, 3):
-            put_fused(n, jc, J, biased_run(n, jc, J, at_x(0, 1) + n * 2 * KB, 0))
-            nc.sync.dma_start(out=out[n * P : (n + 1) * P, :], in_=pages[n][:])
+        for n, j0, j1 in ((1, jc, jd), (0, jc, J), (1, jd, J), (2, jc, J), (3, jc, J)):
+            y_sb = placed("y%d_%d" % (n, j0), [P, j1 - j0], F32, at_x(1, 3) + n * 2 * KB + (j0 - jc) * 4)
+            add_bias(y_sb[:], down([(n, j0, j1)])[0][:], n)
+            put_fused(n, j0, j1, y_sb[:])
+            if j1 == J:
+                nc.sync.dma_start(out=out[n * P : (n + 1) * P, :], in_=pages[n][:])

@@ -25,6 +25,7 @@ QUART = J // 4
 JT = 128
 GROUP = 16
 BANKS = 8
+CUT0, CUT1 = 96, 112
 KB = 1024
 
 AT_X = 0
@@ -132,10 +133,7 @@ def tile_list_sigm_scatb_kernel(
 
         def weave_x_pool(a, j0, j1, at):
             x_b[a, j0] = placed("x_b%d_%d" % (a, j0), [P, j1 - j0, PACK], BF16, at)
-            for j in range(j0, j1, JT):
-                nc.gpsimd.tensor_scalar(
-                    x_b[a, j0][:, j - j0 : j - j0 + JT, :], gath[a][:, :, j : j + JT].rearrange("p i j -> p j i"), 1.0, 0.0, MULT, ADD
-                )
+            nc.gpsimd.tensor_scalar(x_b[a, j0][:], gath[a][:, :, j0:j1].rearrange("p i j -> p j i"), 1.0, 0.0, MULT, ADD)
 
         def quant_x(a, j0, j1, at):
             codes = placed("x_q%d_%d" % (a, j0), [P, j1 - j0], I32, at)
@@ -148,7 +146,7 @@ def tile_list_sigm_scatb_kernel(
         def weave_wg(c, a, copy, raw, m0, m1):
             if (c, a) not in wg_b:
                 wg_b[c, a] = placed("wg_b%d%d" % (c, a), [P, PACK, P, PACK], BF16, AT_WG_B + (2 * c + a) * 4 * KB)
-            copy(wg_b[c, a][:, :, m0:m1, :].rearrange("p t m i -> p m i t"), raw[:].rearrange("p i (m t) -> p m i t", t=PACK))
+            copy(wg_b[c, a][:, :, m0:m1, :].rearrange("p t m i -> p m i t"), raw.rearrange("p i (m t) -> p m i t", t=PACK))
 
         def quant_wg(c, a, at):
             wg_q[c, a] = placed("wg_q%d%d" % (c, a), [P, PASS], I32, at)
@@ -337,15 +335,17 @@ def tile_list_sigm_scatb_kernel(
         weave_x(0, HALF, J, AT_X_B + 4 * KB)
         gather(1, 0, 0, J)
         quant_x(0, 0, HALF, at_x(1, 0))
-        weave_wg(0, 0, nc.scalar.copy, raw00, 0, P)
+        weave_wg(0, 0, nc.vector.tensor_copy, raw00[:, :, PACK * CUT0 : PASS], CUT0, P)
+        weave_wg(0, 0, nc.scalar.copy, raw00[:, :, 0 : PACK * CUT0], 0, CUT0)
         gather(1, 1, 0, J)
         quant_x(0, HALF, J, at_x(1, 1) + 6 * KB)
         quant_wg(0, 0, at_x(1, 1))
+        weave_wg(0, 1, nc.vector.tensor_copy, raw01[:, :, PACK * CUT1 : PASS], CUT1, P)
         wu_s = placed("wu_s", [P, R], U8, at_x(1, 1) + 4 * KB)
         nc.vector.tensor_copy(
             wu_s[:].rearrange("p (c t m) -> p c t m", c=2, t=PACK), wu_sraw[:].rearrange("p (c m t) -> p c t m", c=2, t=PACK)
         )
-        weave_wg(0, 1, nc.scalar.copy, raw01, 0, P)
+        weave_wg(0, 1, nc.scalar.copy, raw01[:, :, 0 : PACK * CUT1], 0, CUT1)
         wu_q[0] = keep.tile([P, 2, PASS], I32, name="wu_q0", align_bytes=64)
         deal_wu(nc.scalar.copy, wu_q[0][:, 0:1, :], wu_raw00)
         quant_wg(0, 1, at_x(0, 2))
@@ -362,7 +362,8 @@ def tile_list_sigm_scatb_kernel(
             up_pass(0, u // 2, 0, (u % 2,))
         gather(1, 2, 0, J)
         gather(1, 3, 0, QUART)
-        gather(1, 3, QUART, J)
+        gather(1, 3, QUART, HALF)
+        gather(1, 3, HALF, J)
 
         deal_wu(nc.scalar.copy, wu_q[0][:, 1:2, :], wu_raw01)
         weave_x(1, 0, QUART, AT_X_B + 8 * KB)
@@ -371,8 +372,8 @@ def tile_list_sigm_scatb_kernel(
         for side in range(2):
             for jt in range(2):
                 up_pass(0, jt, 1, (side,))
-        weave_wg(1, 0, nc.vector.tensor_copy, raw10, 0, P)
-        weave_wg(1, 1, nc.vector.tensor_copy, raw11_vector, P // 2, P)
+        weave_wg(1, 0, nc.vector.tensor_copy, raw10[:], 0, P)
+        weave_wg(1, 1, nc.vector.tensor_copy, raw11_vector[:], P // 2, P)
         quant_x(1, QUART, HALF, at_x(0, 0))
         for side in range(2):
             for jt in range(2, 4):
@@ -382,7 +383,7 @@ def tile_list_sigm_scatb_kernel(
         sigmoid(0, 0, first_sigs[0])
         sigmoid(0, 1, first_sigs[1])
         gate(0, 0)
-        weave_wg(1, 1, nc.scalar.copy, raw11_scalar, 0, P // 2)
+        weave_wg(1, 1, nc.scalar.copy, raw11_scalar[:], 0, P // 2)
         gate(0, 1)
         quant_wg(1, 1, at_x(0, 2) + 6 * KB)
         wu_q[1] = placed("wu_q1", [P, 2, PASS], I32, at_x(1, 3) + 4 * KB)
@@ -391,7 +392,7 @@ def tile_list_sigm_scatb_kernel(
             sigmoid(0, jt, first_sigs[jt])
             gate(0, jt)
 
-        weave_x_pool(1, HALF + QUART, J - JT, AT_WU_RAW + 4 * KB)
+        weave_x_pool(1, HALF + QUART, J, AT_WU_RAW + 4 * KB)
         for jt in range(4):
             up_pass(1, jt, 0, (0,))
         for jt in range(2):
@@ -402,12 +403,10 @@ def tile_list_sigm_scatb_kernel(
             up_pass(1, jt, 1, (1,))
         sigmoid(1, 0, placed_sig(1, 0, at_x(1, 3)))
         sigmoid(1, 1, ring_sig())
-        weave_x(1, J - JT, J, AT_SIG + 6 * KB)
         gate(1, 0)
         gate(1, 1)
         quant_x(1, HALF, HALF + QUART, at_x(1, 3))
-        quant_x(1, HALF + QUART, J - JT, at_x(1, 3) + KB)
-        quant_x(1, J - JT, J, at_x(1, 3) + 3 * KB // 2)
+        quant_x(1, HALF + QUART, J, at_x(1, 3) + KB)
         quant_h(0, at_x(1, 1) + 2 * KB)
         for jt in range(2, 4):
             up_pass(1, jt, 1, (0,))

@@ -419,11 +419,11 @@ def tile_list_sigm_scatb_kernel(
         at_y = at_x(0, 3)
         first = weighted(0, ja, quarters([(0, ja)])[0], at_y)
         y = quarters([(1, ja), (2, ja)]) + quarters([(3, ja)])
-        y_a = [biased([1, 2], ja, y[0:2], at_y + KB), biased([3], ja, y[2:3], at_y + 3 * KB)]
+        y_a = [biased([1], ja, y[0:1], at_y + KB), biased([2, 3], ja, y[1:3], at_y + 2 * KB)]
         quant_h(jb, at_x(1, 2))
         put_copied(0, ja, first)
-        yw_a = pool_weighted([1, 2], ja, y_a[0], AT_GATH)
-        yw_a += pool_weighted([3], ja, y_a[1], AT_GATH + 10 * KB)
+        yw_a = pool_weighted([1], ja, y_a[0], AT_GATH)
+        yw_a += pool_weighted([2, 3], ja, y_a[1], AT_GATH + 10 * KB)
         both = [pair_tile(0, 4, AT_WG_RAW), pair_tile(1, 4, AT_WG_RAW + 8 * KB), pair_tile(0, 6, at_x(0, 0))]
         hand_over(0, 4, both[0])
         y_b = biased([1, 2, 3], jb, quarters([(1, jb), (2, jb)]) + quarters([(3, jb)]), at_y + 4 * KB)

@@ -32,8 +32,8 @@ AT_X = 0
 AT_GATH = 64 * KB
 AT_WG_RAW = 96 * KB
 AT_WG_B = 112 * KB
-AT_SIG = 128 * KB
-AT_WU_RAW = 136 * KB
+AT_WU_RAW = 128 * KB
+AT_SIG = 136 * KB
 AT_X_B = 144 * KB
 
 
@@ -103,7 +103,7 @@ def tile_list_sigm_scatb_kernel(
             return raw
 
         def load_wu(c, a0, a1):
-            raw = placed("wu_raw%d%d" % (c, a0), [P, a1 - a0, PASS], I32, AT_WU_RAW + (2 * c + a0) * 2 * KB)
+            raw = placed("wu_raw%d%d" % (c, a0), [P, a1 - a0, PASS], I32, AT_WU_RAW + (2 * (1 - c) + a0) * 2 * KB)
             nc.sync.dma_start(out=raw[:], in_=wu_rows[:, a0:a1, c * PASS * PACK : (c + 1) * PASS * PACK].bitcast(I32))
             return raw
 
@@ -379,7 +379,7 @@ def tile_list_sigm_scatb_kernel(
             for jt in range(2, 4):
                 up_pass(0, jt, 1, (side,))
         quant_wg(1, 0, at_x(0, 2) + 2 * KB)
-        first_sigs = [placed_sig(0, jt, AT_SIG + jt * 2 * KB) for jt in range(4)]
+        first_sigs = [placed_sig(0, jt, (AT_SIG if jt < 2 else at_x(0, 1)) + jt % 2 * 2 * KB) for jt in range(4)]
         sigmoid(0, 0, first_sigs[0])
         sigmoid(0, 1, first_sigs[1])
         gate(0, 0)
@@ -392,8 +392,8 @@ def tile_list_sigm_scatb_kernel(
             sigmoid(0, jt, first_sigs[jt])
             gate(0, jt)
 
-        weave_x_pool(1, HALF + QUART, J, AT_WU_RAW + 4 * KB)
-        for jt in range(4):
+        weave_x_pool(1, HALF + QUART, J, AT_WU_RAW - KB)
+        for jt in range(3):
             up_pass(1, jt, 0, (0,))
         for jt in range(2):
             up_pass(1, jt, 1, (0,))
@@ -409,7 +409,8 @@ def tile_list_sigm_scatb_kernel(
         quant_x(1, HALF + QUART, J, at_x(1, 3) + KB)
         quant_h(0, at_x(1, 1) + 2 * KB)
         for jt in range(2, 4):
-            up_pass(1, jt, 1, (0,))
+            for a in range(3 - jt, 2):
+                up_pass(1, jt, a, (0,))
             up_pass(1, jt, 0, (1,))
             up_pass(1, jt, 1, (1,))
             sigmoid(1, jt, ring_sig())

@@ -25,7 +25,7 @@ QUART = J // 4
 JT = 128
 GROUP = 16
 BANKS = 8
-CUT0, CUT1 = 96, 112
+CUT0 = 96
 KB = 1024
 
 AT_X = 0
@@ -303,9 +303,9 @@ def tile_list_sigm_scatb_kernel(
         load_x(1, 0)
         raw00 = load_wg(0, 0, PASS, AT_WG_RAW)
         load_x(1, 1)
-        raw01 = load_wg(1, 0, PASS, AT_WG_RAW + 8 * KB)
-        wu_raw00 = load_wu(0, 0, 1)
+        raw01 = [load_wg(1, h * QUART, (h + 1) * QUART, AT_WG_RAW + (8 + 4 * h) * KB) for h in range(2)]
         load_x(1, 2)
+        wu_raw00 = load_wu(0, 0, 1)
         load_x(1, 3)
         wu_raw01 = load_wu(0, 1, 2)
 
@@ -340,12 +340,12 @@ def tile_list_sigm_scatb_kernel(
         gather(1, 1, 0, J)
         quant_x(0, HALF, J, at_x(1, 1) + 6 * KB)
         quant_wg(0, 0, at_x(1, 1))
-        weave_wg(0, 1, nc.vector.tensor_copy, raw01[:, :, PACK * CUT1 : PASS], CUT1, P)
         wu_s = placed("wu_s", [P, R], U8, at_x(1, 1) + 4 * KB)
         nc.vector.tensor_copy(
             wu_s[:].rearrange("p (c t m) -> p c t m", c=2, t=PACK), wu_sraw[:].rearrange("p (c m t) -> p c t m", c=2, t=PACK)
         )
-        weave_wg(0, 1, nc.scalar.copy, raw01[:, :, 0 : PACK * CUT1], 0, CUT1)
+        for h in range(2):
+            weave_wg(0, 1, nc.scalar.copy, raw01[h][:], h * P // 2, (h + 1) * P // 2)
         wu_q[0] = keep.tile([P, 2, PASS], I32, name="wu_q0", align_bytes=64)
         deal_wu(nc.scalar.copy, wu_q[0][:, 0:1, :], wu_raw00)
         quant_wg(0, 1, at_x(0, 2))
@@ -397,16 +397,16 @@ def tile_list_sigm_scatb_kernel(
             up_pass(1, jt, 0, (0,))
         for jt in range(2):
             up_pass(1, jt, 1, (0,))
-        weave_x(1, HALF, HALF + QUART, AT_SIG + 2 * KB)
         for jt in range(2):
             up_pass(1, jt, 0, (1,))
             up_pass(1, jt, 1, (1,))
         sigmoid(1, 0, placed_sig(1, 0, at_x(1, 3)))
         sigmoid(1, 1, ring_sig())
+        weave_x(1, HALF, HALF + QUART, at_x(0, 1))
         gate(1, 0)
         gate(1, 1)
-        quant_x(1, HALF, HALF + QUART, at_x(1, 3))
-        quant_x(1, HALF + QUART, J, at_x(1, 3) + KB)
+        quant_x(1, HALF + QUART, J, at_x(1, 3))
+        quant_x(1, HALF, HALF + QUART, at_x(1, 3) + KB)
         quant_h(0, at_x(1, 1) + 2 * KB)
         for jt in range(2, 4):
             for a in range(3 - jt, 2):

from contextlib import ExitStack

import concourse.mybir as mybir
from concourse.masks import make_identity

K, R, N, T, J = 1024, 1024, 512, 2048, 1024
FLOPS = 2 * J * (2 * K * R + R * N)

F32 = mybir.dt.float32
BF16 = mybir.dt.bfloat16
I32 = mybir.dt.int32
U32 = mybir.dt.uint32
U16 = mybir.dt.uint16
U8 = mybir.dt.uint8
FP8X4 = mybir.dt.float8_e4m3fn_x4
MULT = mybir.AluOpType.mult
ADD = mybir.AluOpType.add
ACT = mybir.ActivationFunctionType

P = 128
PACK = 4
PASS = P * PACK
HALF = J // 2
QUART = J // 4
JT = 128
GROUP = 16
BANKS = 8
CUT0 = 96
KB = 1024

AT_X = 0
AT_GATH = 64 * KB
AT_WG_RAW = 96 * KB
AT_WG_B = 112 * KB
AT_WU_RAW = 128 * KB
AT_SIG = 136 * KB
AT_X_B = 144 * KB


def tile_list_sigm_scatb_kernel(
    tc, xT, wgt, wg, wu_words, wu_scales, wd_words, wd_scales, b, wgo, offs, offs2, out
):
    nc = tc.nc
    with ExitStack() as ctx:
        keep = ctx.enter_context(tc.tile_pool(name="keep", bufs=1))
        share = ctx.enter_context(tc.tile_pool(name="share", bufs=1))
        ring = ctx.enter_context(tc.tile_pool(name="ring", bufs=2))
        psum = ctx.enter_context(tc.psum_pool(name="psum", bufs=1))

        def placed(name, shape, dtype, at):
            return share.tile(shape, dtype, name=name, offset=at, align_bytes=64)

        def at_x(a, i):
            return AT_X + (PACK * a + i) * 8 * KB

        handed = []

        def bank(name, shape, k):
            return psum.tile(shape, F32, name=name, tag="bank%d" % k)

        def next_bank(name, shape):
            handed.append(name)
            return bank(name, shape, (len(handed) - 1) % BANKS)

        offs_t = keep.tile([P, J // GROUP], U16, name="offs_t")
        offs2_t = keep.tile([P, J // GROUP], U16, name="offs2_t")
        wgt_t = keep.tile([P, J], F32, name="wgt_t")
        wgo_t = keep.tile([P, J], F32, name="wgo_t")
        bias = keep.tile([P, N // P], F32, name="bias")
        warm = keep.tile([P, 2], F32, name="warm")
        pages = [keep.tile([P, T], F32, name="page%d" % n) for n in range(N // P)]
        wu_sraw = keep.tile([P, R], U8, name="wu_sraw", align_bytes=64)
        wd_s = keep.tile([P, N], U8, name="wd_s", align_bytes=64)
        wd_q = keep.tile([P, 2, N], I32, name="wd_q", align_bytes=64)
        wg_s = {(c, a): keep.tile([P, PASS], U8, name="wg_s%d%d" % (c, a), align_bytes=64) for c in range(2) for a in range(2)}
        ident = keep.tile([P, P], F32, name="ident")
        rows = keep.tile([P, JT], F32, name="rows")
        planes = {(a, i): placed("x%d%d" % (a, i), [P, T], F32, at_x(a, i)) for a in range(2) for i in range(PACK)}
        gath = [placed("gath%d" % a, [P, PACK, J], F32, AT_GATH + a * 16 * KB) for a in range(2)]

        x_rows = xT.rearrange("(a p i) t -> a i p t", a=2, i=PACK)
        wg_rows = wg.rearrange("(a p i) r -> a p i r", a=2, i=PACK)
        wu_rows = wu_words.rearrange("a p r i -> p a (r i)")

        x_b = {}
        x_q = {}
        x_s = {}
        wg_b = {}
        wg_q = {}
        wu_q = {}
        banks = {}
        sigs = {}
        h_b = {}
        h_q = {}
        h_s = {}

        def load_x(a, i):
            nc.sync.dma_start(out=planes[a, i][:], in_=x_rows[a, i])

        def load_wg(a, r0, r1, at):
            raw = placed("wg_raw%d_%d" % (a, r0), [P, PACK, r1 - r0], F32, at)
            nc.sync.dma_start(out=raw[:], in_=wg_rows[a][:, :, r0:r1])
            return raw

        def load_wu(c, a0, a1):
            raw = placed("wu_raw%d%d" % (c, a0), [P, a1 - a0, PASS], I32, AT_WU_RAW + (2 * (1 - c) + a0) * 2 * KB)
            nc.sync.dma_start(out=raw[:], in_=wu_rows[:, a0:a1, c * PASS * PACK : (c + 1) * PASS * PACK].bitcast(I32))
            return raw

        def load_scales(queue, dst, src):
            for q in range(4):
                queue.dma_start(out=dst[32 * q : 32 * q + 8, :].bitcast(I32), in_=src[:, 4 * q : 4 * q + 4, :].bitcast(I32))

        def spread(w, dst, u0, u1, k, wide):
            src = turned[:, w, :, u0:u1].rearrange("p g u -> p u g")
            nc.scalar.copy(wide[:], src.unsqueeze(3).to_broadcast([P, u1 - u0, P // GROUP, GROUP]))
            back = bank("back", [P, u1 - u0, JT], k)
            for u in range(u1 - u0):
                nc.tensor.transpose(back[:, u, :], wide[:, u, :, :].rearrange("p g r -> p (g r)"), ident[:])
            nc.scalar.copy(dst[:, u0 * JT : u1 * JT], back[:].rearrange("p u j -> p (u j)"))

        def gather(a, i, j0, j1):
            nc.vector.tensor_tensor(
                gath[a][:, i, j0:j1], planes[a, i][:].indirect(offs_t[:, j0 // GROUP : j1 // GROUP]), wgt_t[:, j0:j1], MULT
            )

        def weave_x(a, j0, j1, at):
            x_b[a, j0] = placed("x_b%d_%d" % (a, j0), [P, j1 - j0, PACK], BF16, at)
            nc.scalar.copy(
                x_b[a, j0][:].rearrange("p (c j) i -> p c i j", j=4),
                gath[a][:, :, j0:j1].rearrange("p i (c j) -> p c i j", j=4),
            )

        def weave_x_pool(a, j0, j1, at):
            x_b[a, j0] = placed("x_b%d_%d" % (a, j0), [P, j1 - j0, PACK], BF16, at)
            nc.gpsimd.tensor_scalar(x_b[a, j0][:], gath[a][:, :, j0:j1].rearrange("p i j -> p j i"), 1.0, 0.0, MULT, ADD)

        def quant_x(a, j0, j1, at):
            codes = placed("x_q%d_%d" % (a, j0), [P, j1 - j0], I32, at)
            scales = keep.tile([P, j1 - j0], U8, name="x_s%d_%d" % (a, j0), align_bytes=64)
            for jt in range(j0 // JT, j1 // JT):
                x_q[a, jt] = codes[:, jt * JT - j0 : (jt + 1) * JT - j0]
                x_s[a, jt] = scales[:, jt * JT - j0 : (jt + 1) * JT - j0]
            nc.vector.quantize_mx(out=codes[:].bitcast(FP8X4), scales=scales[:], in_=x_b[a, j0][:].rearrange("p j i -> p (j i)"))

        def weave_wg(c, a, copy, raw, m0, m1):
            if (c, a) not in wg_b:
                wg_b[c, a] = placed("wg_b%d%d" % (c, a), [P, PACK, P, PACK], BF16, AT_WG_B + (2 * c + a) * 4 * KB)
            copy(wg_b[c, a][:, :, m0:m1, :].rearrange("p t m i -> p m i t"), raw.rearrange("p i (m t) -> p m i t", t=PACK))

        def quant_wg(c, a, at):
            wg_q[c, a] = placed("wg_q%d%d" % (c, a), [P, PASS], I32, at)
            nc.vector.quantize_mx(
                out=wg_q[c, a][:].bitcast(FP8X4), scales=wg_s[c, a][:], in_=wg_b[c, a][:].rearrange("p t m i -> p (t m i)")
            )

        def deal_wu(copy, dst, raw):
            copy(
                dst.bitcast(U32).rearrange("p a (t m) -> p a m t", t=PACK),
                raw[:].bitcast(U32).rearrange("p a (m t) -> p a m t", t=PACK),
            )

        def up_pass(c, jt, a, sides=(0, 1)):
            shape = [P, PACK, JT]
            if jt >= 4 and (c, jt, 0) not in banks:
                for s in range(2):
                    banks[c, jt, s] = next_bank("up", shape)
            for s in sides:
                if (c, jt, s) not in banks:
                    banks[c, jt, s] = bank("up", shape, jt + 4 * s)
                for t in range(PACK):
                    m = slice(t * P, (t + 1) * P)
                    if s == 0:
                        w, ws = wg_q[c, a][:, m], wg_s[c, a][:, m]
                    else:
                        w, ws = wu_q[c][:, a, m], wu_s[4 * a : P, c * PASS + t * P : c * PASS + (t + 1) * P]
                    nc.tensor.matmul_mx(
                        banks[c, jt, s][:, t, :],
                        lhsT=w.bitcast(FP8X4),
                        lhsT_scale=ws,
                        rhs=x_q[a, jt].bitcast(FP8X4),
                        rhs_scale=x_s[a, jt],
                        start=(a == 0 and t == 0),
                        stop=(a == 1 and t == PACK - 1),
                    )

        at_h = {0: AT_X_B + 8 * KB, QUART: AT_GATH, HALF: AT_GATH + 2 * KB}

        def chunk(j):
            return (j // QUART * QUART, QUART) if j < HALF else (HALF, HALF)

        def h_slot(c, jt, count=1):
            j0, w = chunk(jt * JT)
            if j0 not in h_b:
                h_b[j0] = placed("h_b%d" % j0, [P, 2 * w, PACK], BF16, at_h[j0])
            lo = c * w + jt * JT - j0
            return h_b[j0][:, lo : lo + count * JT, :]

        def woven(sums):
            return sums[:].rearrange("p t j -> p j t")

        def sigmoid(c, jt, sig):
            sigs[c, jt] = sig
            nc.scalar.activation(sig[:], woven(banks[c, jt, 0]), ACT.Sigmoid)

        def gate(c, jt):
            nc.vector.tensor_tensor(h_slot(c, jt), woven(banks[c, jt, 1]), sigs[c, jt][:], MULT)

        def ring_sig():
            return ring.tile([P, JT, PACK], F32, name="sig", tag="sig", bufs=3)

        def placed_sig(c, jt, at):
            return placed("sig%d%d" % (c, jt), [P, JT, PACK], F32, at)

        def unit(c, jt):
            for s in range(2):
                for a in range(2):
                    up_pass(c, jt, a, (s,))

        def pair_tile(c, jt0, at):
            return placed("both%d%d" % (c, jt0), [P, 2, 2, JT, PACK], F32, at)

        def hand_over(c, jt, both):
            unit(c, jt)
            nc.scalar.activation(both[:, 0, jt % 2], woven(banks[c, jt, 0]), ACT.Sigmoid)
            nc.scalar.copy(both[:, 1, jt % 2], woven(banks[c, jt, 1]))

        def pool_gate(c, jt0, both):
            pair = "p u j t -> p (u j) t"
            nc.gpsimd.tensor_tensor(h_slot(c, jt0, 2), both[:, 0].rearrange(pair), both[:, 1].rearrange(pair), MULT)

        def quant_h(j0, at):
            w = chunk(j0)[1]
            h_q[j0] = placed("h_q%d" % j0, [P, 2 * w], I32, at)
            h_s[j0] = keep.tile([P, 2 * w], U8, name="h_s%d" % j0, align_bytes=64)
            nc.vector.quantize_mx(out=h_q[j0][:].bitcast(FP8X4), scales=h_s[j0][:], in_=h_b[j0][:].rearrange("p j t -> p (j t)"))

        def down(pieces):
            y = next_bank("y", [P, sum(j1 - j0 for n, j0, j1 in pieces)])
            parts = []
            for n, j0, j1 in pieces:
                at = sum(part.shape[1] for part in parts)
                parts.append(y[:, at : at + j1 - j0])
                q0, w = chunk(j0)
                for c in range(2):
                    cols = slice(c * w + j0 - q0, c * w + j1 - q0)
                    nc.tensor.matmul_mx(
                        parts[-1],
                        lhsT=wd_q[:, c, n * P : (n + 1) * P].bitcast(FP8X4),
                        lhsT_scale=wd_s[4 * c : P, n * P : (n + 1) * P],
                        rhs=h_q[q0][:, cols].bitcast(FP8X4),
                        rhs_scale=h_s[q0][:, cols],
                        start=(c == 0),
                        stop=(c == 1),
                    )
            return y, parts

        def quarters(pieces):
            return down([(n, j0, j0 + QUART) for n, j0 in pieces])[1]

        def window(n, j0, j1):
            return pages[n][:].indirect(offs2_t[:, j0 // GROUP : j1 // GROUP])

        def add_bias(dst, y, n):
            nc.scalar.activation(dst, y, ACT.Identity, bias=bias[:, n : n + 1])

        def biased(ns, j0, ys, at):
            y_sb = placed("y%d_%d" % (ns[0], j0), [P, len(ns), QUART], F32, at)
            for u, n in enumerate(ns):
                add_bias(y_sb[:, u, :], ys[u], n)
            return y_sb

        def pool_weighted(ns, j0, y_sb, at):
            shape = [P, len(ns), QUART]
            y_w = placed("yw%d_%d" % (ns[0], j0), shape, F32, at)
            nc.gpsimd.tensor_tensor(y_w[:], y_sb[:], wgo_t[:, j0 : j0 + QUART].unsqueeze(1).to_broadcast(shape), MULT)
            return [y_w[:, u, :] for u in range(len(ns))]

        def weighted(n, j0, y, at):
            y_w = placed("yw%d_%d" % (n, j0), [P, QUART], F32, at)
            nc.vector.scalar_tensor_tensor(y_w[:], y, bias[:, n : n + 1], wgo_t[:, j0 : j0 + QUART], ADD, MULT)
            return y_w[:]

        def put_copied(n, j0, y_w):
            nc.vector.tensor_copy(window(n, j0, j0 + QUART), y_w)

        def put_fused(n, j0, j1, y_sb):
            nc.vector.tensor_tensor(window(n, j0, j1), y_sb, wgo_t[:, j0:j1], MULT)

        make_identity(nc, ident[:])
        nc.gpsimd.memset(wu_sraw[:].bitcast(I32), 0)
        nc.vector.memset(warm[:, 0:1], 0.0)
        nc.scalar.activation(warm[:, 1:2], warm[:, 0:1], ACT.Sigmoid)
        load_scales(nc.gpsimd, wu_sraw, wu_scales)
        nc.gpsimd.memset(wd_s[:].bitcast(I32), 0)
        for page in pages:
            nc.gpsimd.memset(page[:], 0.0)
        nc.sync.dma_start(out=rows[0 : P // 2, :], in_=wgt[0:P:GROUP, :].rearrange("g (u j) -> g u j", j=JT))
        nc.sync.dma_start(out=rows[P // 2 : P, :], in_=wgo[0:P:GROUP, :].rearrange("g (u j) -> g u j", j=JT))
        nc.sync.dma_start(offs_t[:], offs)
        for i in range(PACK):
            load_x(0, i)
        load_x(1, 0)
        raw00 = load_wg(0, 0, PASS, AT_WG_RAW)
        load_x(1, 1)
        raw01 = [load_wg(1, h * QUART, (h + 1) * QUART, AT_WG_RAW + (8 + 4 * h) * KB) for h in range(2)]
        load_x(1, 2)
        wu_raw00 = load_wu(0, 0, 1)
        load_x(1, 3)
        wu_raw01 = load_wu(0, 1, 2)

        turned = bank("turned", [P, 2, P // GROUP, J // JT], BANKS - 1)
        nc.tensor.transpose(turned[:].rearrange("p w g u -> p (w g u)"), rows[:], ident[:])
        cuts = (0, 2, 5, 8)
        for k in range(3):
            wide = ring.tile([P, cuts[k + 1] - cuts[k], P // GROUP, GROUP], F32, name="wide", tag="wide")
            spread(0, wgt_t, cuts[k], cuts[k + 1], k, wide)
        for k in range(3):
            gather(0, 0, cuts[k] * JT, cuts[k + 1] * JT)
        gather(0, 1, 0, J)
        raw10 = load_wg(0, PASS, R, at_x(0, 0))
        raw11_vector = load_wg(1, R - QUART, R, at_x(0, 1) + 4 * KB)
        raw11_scalar = load_wg(1, PASS, R - QUART, at_x(0, 1))
        wu_raw1 = load_wu(1, 0, 2)
        load_scales(nc.sync, wd_s, wd_scales)
        nc.sync.dma_start(out=wd_q[:], in_=wd_words.rearrange("a p n i -> p a (n i)").bitcast(I32))
        nc.sync.dma_start(offs2_t[:], offs2)
        with nc.allow_non_contiguous_dma(reason="one bias value a partition"):
            nc.sync.dma_start(out=bias[:], in_=b.rearrange("(c p) -> p c", p=P))

        gather(0, 2, 0, J)
        gather(0, 3, 0, HALF)
        gather(0, 3, HALF, J)
        weave_x(0, 0, HALF, AT_X_B)
        weave_x(0, HALF, J, AT_X_B + 4 * KB)
        gather(1, 0, 0, J)
        quant_x(0, 0, HALF, at_x(1, 0))
        weave_wg(0, 0, nc.vector.tensor_copy, raw00[:, :, PACK * CUT0 : PASS], CUT0, P)
        weave_wg(0, 0, nc.scalar.copy, raw00[:, :, 0 : PACK * CUT0], 0, CUT0)
        gather(1, 1, 0, J)
        quant_x(0, HALF, J, at_x(1, 1) + 6 * KB)
        quant_wg(0, 0, at_x(1, 1))
        wu_s = placed("wu_s", [P, R], U8, at_x(1, 1) + 4 * KB)
        nc.vector.tensor_copy(
            wu_s[:].rearrange("p (c t m) -> p c t m", c=2, t=PACK), wu_sraw[:].rearrange("p (c m t) -> p c t m", c=2, t=PACK)
        )
        for h in range(2):
            weave_wg(0, 1, nc.scalar.copy, raw01[h][:], h * P // 2, (h + 1) * P // 2)
        wu_q[0] = keep.tile([P, 2, PASS], I32, name="wu_q0", align_bytes=64)
        deal_wu(nc.scalar.copy, wu_q[0][:, 0:1, :], wu_raw00)
        quant_wg(0, 1, at_x(0, 2))
        wide = placed("wide_o", [P, BANKS, P // GROUP, GROUP], F32, AT_WG_B)
        for u in range(0, BANKS, 4):
            src = turned[:, 1, :, u : u + 4].rearrange("p g u -> p u g")
            nc.scalar.copy(wide[:, u : u + 4], src.unsqueeze(3).to_broadcast([P, 4, P // GROUP, GROUP]))
        backs = [bank("back_o", [P, JT], u // 2 + 4 * (u % 2)) for u in range(BANKS)]
        for u in range(BANKS):
            nc.tensor.transpose(backs[u][:], wide[:, u].rearrange("p g r -> p (g r)"), ident[:])
        for u in range(BANKS):
            nc.scalar.copy(wgo_t[:, u * JT : (u + 1) * JT], backs[u][:])
        for u in range(BANKS):
            up_pass(0, u // 2, 0, (u % 2,))
        gather(1, 2, 0, J)
        gather(1, 3, 0, QUART)
        gather(1, 3, QUART, HALF)
        gather(1, 3, HALF, J)

        deal_wu(nc.scalar.copy, wu_q[0][:, 1:2, :], wu_raw01)
        weave_x(1, 0, QUART, AT_X_B + 8 * KB)
        weave_x(1, QUART, HALF, AT_X_B + 10 * KB)
        quant_x(1, 0, QUART, at_x(0, 2) + 5 * KB)
        for side in range(2):
            for jt in range(2):
                up_pass(0, jt, 1, (side,))
        weave_wg(1, 0, nc.vector.tensor_copy, raw10[:], 0, P)
        weave_wg(1, 1, nc.vector.tensor_copy, raw11_vector[:], P // 2, P)
        quant_x(1, QUART, HALF, at_x(0, 0))
        for side in range(2):
            for jt in range(2, 4):
                up_pass(0, jt, 1, (side,))
        quant_wg(1, 0, at_x(0, 2) + 2 * KB)
        first_sigs = [placed_sig(0, jt, (AT_SIG if jt < 2 else at_x(0, 1)) + jt % 2 * 2 * KB) for jt in range(4)]
        sigmoid(0, 0, first_sigs[0])
        sigmoid(0, 1, first_sigs[1])
        gate(0, 0)
        weave_wg(1, 1, nc.scalar.copy, raw11_scalar[:], 0, P // 2)
        gate(0, 1)
        quant_wg(1, 1, at_x(0, 2) + 6 * KB)
        wu_q[1] = placed("wu_q1", [P, 2, PASS], I32, at_x(1, 3) + 4 * KB)
        deal_wu(nc.vector.tensor_copy, wu_q[1][:], wu_raw1)
        for jt in range(2, 4):
            sigmoid(0, jt, first_sigs[jt])
            gate(0, jt)

        weave_x_pool(1, HALF + QUART, J, AT_WU_RAW - KB)
        for jt in range(3):
            up_pass(1, jt, 0, (0,))
        for jt in range(2):
            up_pass(1, jt, 1, (0,))
        for jt in range(2):
            up_pass(1, jt, 0, (1,))
            up_pass(1, jt, 1, (1,))
        sigmoid(1, 0, placed_sig(1, 0, at_x(1, 3)))
        sigmoid(1, 1, ring_sig())
        weave_x(1, HALF, HALF + QUART, at_x(0, 1))
        gate(1, 0)
        gate(1, 1)
        quant_x(1, HALF + QUART, J, at_x(1, 3))
        quant_x(1, HALF, HALF + QUART, at_x(1, 3) + KB)
        quant_h(0, at_x(1, 1) + 2 * KB)
        for jt in range(2, 4):
            for a in range(3 - jt, 2):
                up_pass(1, jt, a, (0,))
            up_pass(1, jt, 0, (1,))
            up_pass(1, jt, 1, (1,))
            sigmoid(1, jt, ring_sig())
            gate(1, jt)

        ja, jb, jc, jd = range(0, J, QUART)
        at_y = at_x(0, 3)
        first = weighted(0, ja, quarters([(0, ja)])[0], at_y)
        y = quarters([(1, ja), (2, ja)]) + quarters([(3, ja)])
        y_a = [biased([1], ja, y[0:1], at_y + KB), biased([2, 3], ja, y[1:3], at_y + 2 * KB)]
        quant_h(jb, at_x(1, 2))
        put_copied(0, ja, first)
        yw_a = pool_weighted([1], ja, y_a[0], AT_GATH)
        yw_a += pool_weighted([2, 3], ja, y_a[1], AT_GATH + 10 * KB)
        both = [pair_tile(0, 4, AT_WG_RAW), pair_tile(1, 4, AT_WG_RAW + 8 * KB), pair_tile(0, 6, at_x(0, 0))]
        hand_over(0, 4, both[0])
        y_b = biased([1, 2, 3], jb, quarters([(1, jb), (2, jb)]) + quarters([(3, jb)]), at_y + 4 * KB)
        yw_b = pool_weighted([1, 2, 3], jb, y_b, at_x(1, 2) + 2 * KB)
        hand_over(0, 5, both[0])
        pool_gate(0, 4, both[0])
        for c, jt0, pair in ((1, 4, both[1]), (0, 6, both[2])):
            hand_over(c, jt0, pair)
            hand_over(c, jt0 + 1, pair)
            pool_gate(c, jt0, pair)
        for j0, yw in ((ja, yw_a), (jb, yw_b)):
            for u in range(3):
                put_copied(1 + u, j0, yw[u])
        for jt in range(6, 8):
            unit(1, jt)
            sigmoid(1, jt, placed_sig(1, jt, at_x(0, 1) + (7 - jt) * 2 * KB))
            gate(1, jt)
        y_held = biased([0], jb, quarters([(0, jb)]), at_x(0, 1) - KB // 2)
        quant_h(jc, at_x(1, 0) + 4 * KB)

        put_fused(0, jb, jc, y_held[:, 0, :])
        for n, j0, j1 in ((1, jc, jd), (0, jc, J), (1, jd, J), (2, jc, J), (3, jc, J)):
            y_sb = placed("y%d_%d" % (n, j0), [P, j1 - j0], F32, at_x(1, 3) + n * 2 * KB + (j0 - jc) * 4)
            add_bias(y_sb[:], down([(n, j0, j1)])[0][:], n)
            put_fused(n, j0, j1, y_sb[:])
            if j1 == J:
                nc.sync.dma_start(out=out[n * P : (n + 1) * P, :], in_=pages[n][:])
